import numpy as np, ml_dtypes
CORES = [35,38,43,46]
N = 4
BF = ml_dtypes.bfloat16
W, S, PA, TH, E, R = 4096, 256, 2, 136, 12, 5
def near(rng, pro, kin, amp):
    v = pro[np.arange(8)[None, :, None], kin]; v = v + rng.integers(-amp, amp + 1, v.shape)
    return np.ascontiguousarray(np.minimum(np.maximum(v, 0), 255).transpose(0, 1, 3, 2))
def parts(rng, ends=False):
    pro = rng.integers(0, 256, (8, 3, 16))
    x = near(rng, pro, rng.integers(0, 3, (N, 8, S)), E); d = near(rng, pro, rng.integers(0, 3, (N, 8, W)), E)
    d = np.where(rng.random((N, 8, 1, W)) < 0.25, rng.integers(0, 256, d.shape), d)
    key = rng.random((N, 8, R, W))
    if ends: key[..., 0] = -1.0; key[..., W - 1] = -1.0
    a = np.argsort(key, axis=-1)[..., :S]
    a = rng.permuted(a, axis=-1)
    b = rng.integers(0, W, (N, 8, R, S)); o = rng.integers(0, W, (N, 8, 16, S)); k = rng.integers(0, 2 * R, o.shape)
    for r in range(N):
        for t in range(R): o[r] = np.where(k[r] == t, a[(r + t) % N, :, t][:, None, :], o[r])
    h = np.where(rng.random((N, 8, W)) < 0.5, grantors(rng, a, W), rng.integers(0, W, (N, 8, W)))
    return x, d, o, h, a, b
def grantors(rng, a, n):
    return np.take_along_axis(a.reshape(N, 8, R * S), rng.integers(0, R * S, (N, 8, n)), 2)
def pack(x, d, o, h, a, b):
    return {"own": np.ascontiguousarray(o).reshape(N, 128, S).astype(np.int32), "lm": np.ascontiguousarray(x).reshape(N, 128, S).astype(np.float32).astype(BF),
            "bk": np.ascontiguousarray(d).reshape(N, 128, W).astype(np.float32).astype(BF), "heir": np.ascontiguousarray(h).astype(np.int32),
            "da": np.ascontiguousarray(a).reshape(N, 8, R * S).astype(np.int32), "db": np.ascontiguousarray(b).reshape(N, 8, R * S).astype(np.int32)}
def setup_inputs(rng):
    return pack(*parts(rng))
def setup_inputs_ties(rng):
    x, d, o, h, a, b = parts(rng); mid = rng.integers(60, 196, (8, 16)); x = x * 0 + mid[None, :, :, None]
    s = TH + rng.integers(-1, 2, (N, 8, 1, W)); v = s // 16 + (np.arange(16)[None, None, :, None] < s % 16)
    u = rng.integers(0, (TH - 1) // 16 + 1, (N, 8, 8, W)); v[:, :, :8] += u; v[:, :, 8:] -= u
    d = mid[None, :, :, None] + v * (1 - 2 * rng.integers(0, 2, v.shape))
    return pack(x, d, o, h, a, b)
def setup_inputs_wake(rng):
    x, d, o, h, a, b = parts(rng); pro = rng.integers(40, 216, (8, 1, 16))
    x = near(rng, pro, np.zeros((N, 8, S), np.int64), E // 2); d = rng.integers(0, 256, d.shape)
    o1 = grantors(rng, a, 16 * S).reshape(o.shape); o2 = np.roll(grantors(rng, a, 16 * S), -1, axis=0).reshape(o.shape)
    o = np.where(rng.random(o.shape) < 0.6, o1, o2); h = grantors(rng, a, W); b = np.roll(grantors(rng, a, R * S), -1, axis=0).reshape(b.shape)
    return pack(x, d, o, h, a, b)
def setup_inputs_sleep(rng):
    x, d, o, h, a, b = parts(rng); m = rng.permutation(8); g = m[0]
    a[:, g] = 2 * np.argsort(rng.random((N, W // 2)), axis=-1)[:, :R * S].reshape(N, R, S); x[:, g, :, ::8] = 0
    o[:, g] = 2 * rng.integers(0, W // 2, (N, 16, S)) + 1; h[:, g] = 2 * rng.integers(0, W // 2, (N, W)) + 1; b[:, g] = 2 * rng.integers(0, W // 2, (N, R, S)) + 1
    g = m[1]; a[:, g] = np.argsort(rng.random((N, R, S)), axis=-1)
    o[:, g] = rng.integers(S, W, (N, 16, S)); h[:, g] = rng.integers(S, W, (N, W)); b[:, g] = rng.integers(S, W, (N, R, S))
    nxt = np.roll(a, -1, axis=0)
    for g in m[2:4]:
        x[:, g] = rng.integers(155, 256, (N, 16, S)); d[:, g] = rng.integers(0, 101, (N, 16, W)); b[:, g, :R - 1] = nxt[:, g, 1:]
    o[:, m[2]] = a[:, m[2], 0][:, None, :]; o[:, m[3], 15] = a[:, m[3], 0]
    pro = rng.integers(0, 256, (8, 1, 16)); xn = near(rng, pro, np.zeros((N, 8, S), np.int64), E // 4); dn = near(rng, pro, np.zeros((N, 8, W), np.int64), E // 4)
    for g in m[4:6]:
        x[:, g] = xn[:, g]; d[:, g] = dn[:, g]; h[:, g] = (np.arange(W) + 1) % W
    for r in range(N):
        o[r, m[4]] = rng.permutation((W - 1 - np.arange(16 * S)) % W).reshape(16, S)
        o[r, m[5]] = W - 1 - (r % 2) * rng.integers(0, W // 4, (16, S))
    return pack(x, d, o, h, a, b)
def setup_inputs_alike(rng):
    x, d, o, h, a, b = parts(rng, True); c = 255 * rng.integers(0, 2, (8, 16))[None, :, :, None]; q = rng.permutation(N)
    x = x * 0 + c; x[..., 1::2] = 255 - x[..., 1::2]; x[q[0]] = c[0]
    v = np.where(rng.random((N, 8, 1, W)) < 0.5, c, 255 - c); v[q[0]] = c[0]
    two = rng.random((N, 8, 1, W)) < 0.25; two[q[0]] = False
    s = np.where(two, rng.choice(np.array([128, 160]), two.shape), rng.choice(np.array([0, TH, TH, TH + 1, TH + 1, 255]), two.shape))
    s[q[0]] = rng.choice(np.array([0, TH, TH]), (8, 1, W))
    i = rng.integers(0, 16, two.shape); j = (i + rng.choice(np.array([1, 2, 4, 8, 8]), two.shape)) % 16; p = np.arange(16)[None, None, :, None]
    one = (p == i) | (two & (p == j)); d = v + np.where(v == 0, s, -s) * one
    few = np.array([0, W - 1, W // 2, 3]); o[:, ::2] = rng.choice(few, (N, 4, 16, S))
    h = np.where(rng.random(h.shape) < 0.4, rng.choice(few, h.shape), h); b = np.where(rng.random(b.shape) < 0.3, rng.choice(few, b.shape), b)
    b[..., ::16] = a[..., ::16]; o[q[1], :, 5] = a[q[1], :, 0]
    return pack(x, d, o, h, a, b)
def setup_inputs_spread(rng):
    x, d, o, h, a, b = parts(rng); pro = (np.exp2(8 * rng.random((8, 3, 16))) - 1).astype(np.int64)
    x = near(rng, pro, (3 * rng.random((N, 8, S)) ** 2).astype(np.int64), rng.integers(0, 2 * E + 1, (N, 8, S, 1)))
    d = near(rng, pro, (3 * rng.random((N, 8, W)) ** 2).astype(np.int64), rng.integers(0, 2 * E + 1, (N, 8, W, 1)))
    o = np.where(rng.random(o.shape) < 0.5, (W * rng.random(o.shape) ** 3).astype(np.int64), o)
    h = (W * rng.random(h.shape) ** 3).astype(np.int64); b = (W * rng.random(b.shape) ** 3).astype(np.int64)
    return pack(x, d, np.minimum(o, W - 1), np.minimum(h, W - 1), a, np.minimum(b, W - 1))
def check_inputs(d):
    bad = []
    for k in ("own", "heir", "da", "db"):
        if np.min(d[k]) < 0 or np.max(d[k]) > W - 1: bad.append("range of " + k)
    for k in ("lm", "bk"):
        v = np.asarray(d[k]).astype(np.float32)
        if not np.all((v >= 0) & (v <= 255) & (v == np.floor(v))): bad.append("whole numbers from 0 to 255 in " + k)
    s = np.sort(np.asarray(d["da"]).reshape(N, 8, R, S), axis=-1)
    if np.any(s[..., 1:] == s[..., :-1]): bad.append("different grantors in a round of a rank and group")
    return bad
def reference(own, lm, bk, heir, da, db):
    o = own.astype(np.int64).reshape(N, 8, 16, S); x = lm.astype(np.float32).astype(np.int32).reshape(N, 8, 16, S)
    d = bk.astype(np.float32).astype(np.int32).reshape(N, 8, 16, W); h = heir.astype(np.int64)
    for t in range(R):
        for r in range(N):
            c = (r + t) % N
            a = da[c][:, t * S:(t + 1) * S].astype(np.int64); b = db[c][:, t * S:(t + 1) * S].astype(np.int64)
            hit = o[r] == a[:, None, :]
            o[r] = np.where(hit, b[:, None, :], o[r])
            g, i = np.nonzero(~np.any(hit, axis=1))
            d[c][g, :, a[g, i]] = x[r][g, :, i]
            h[c][g, a[g, i]] = b[g, i]
            for s in range(PA):
                e = o[r].reshape(8, 16 * S)
                w = np.take_along_axis(d[c], e[:, None, :], 2).reshape(8, 16, 16, S)
                dist = np.add.reduce(np.abs(w - x[r][:, :, None, :]), axis=1)
                o[r] = np.where(dist <= TH, np.take_along_axis(h[c], e, 1).reshape(8, 16, S), o[r])
    return {"yo": o.reshape(N, 128, S).astype(np.float32), "yd": d.reshape(N, 128, W).astype(np.float32).astype(BF), "yh": h.astype(np.float32)}

@@ -1,0 +1,525 @@
+from concourse.mybir import AluOpType as A, ActivationFunctionType as F
+
+BIAS = 2048
+TH = 136.5 + 2048
+R = 5
+VS, SS = 104, 88
+VR0, VR = 2, 3
+VCOPY = (1, 4, 6)
+
+SCRATCH = {}
+SEMAPHORES = ["v", "s", "t", "p", "loc", "dout"]
+
+
+def _buf(name, cols, dtype, where="sbuf", rows=128):
+    SCRATCH[name] = (where, [rows, cols], dtype)
+
+
+for _n, _c in (("pi", 1), ("ci", 128), ("p15i", 1), ("p4i", 1), ("p2i", 1), ("pki", 1), ("pgi", 1), ("phi", 1),
+               ("c15i", 128), ("c4i", 128), ("ownI", 256), ("heirI", 512), ("hcut", 512)):
+    _buf(_n, _c, "int32")
+_buf("daI", 1280, "int32", rows=8)
+_buf("dbI", 1280, "int32", rows=8)
+for _n in ("pf", "p15", "p4", "p2", "pk", "pg", "ph", "tn", "th", "hb2", "l01", "l29", "m1", "cb", "ncb"):
+    _buf(_n, 1, "float32")
+for _n, _c in (("BO", 128), ("nBO", 128), ("maskP", 128), ("C01", 128), ("WN", 128), ("Z2", 128),
+               ("RM", 8), ("RH", 24), ("K4", 8), ("yha", 256), ("yhb", 256),
+               ("W", 8192), ("HN", 8192), ("M0", 2048), ("M1", 2048), ("H0", 2048), ("H1", 2048),
+               ("Yn", 256), ("NH0", 256), ("NH1", 256), ("HT0", 128), ("HT1", 128), ("X0", 128), ("X1", 128),
+               ("SG0", 128), ("SG1", 128), ("lm0", 256), ("lm1", 256), ("lm2", 256), ("lm3", 256),
+               ("lr0", 4096), ("lr1", 4096), ("lr2", 4096), ("lr3", 4096)):
+    _buf(_n, _c, "bfloat16")
+for _n, _c in (("IdH", 128), ("HI2", 256), ("WH", 1024), ("K1", 8), ("Hs", 512), ("ownH", 256), ("ownN0", 128), ("ownN1", 128),
+               ("OT0", 128), ("OT1", 128), ("MA0", 256), ("MA1", 256)):
+    _buf(_n, _c, "float16")
+for _n, _c in (("E8", 128), ("nE8", 128), ("E01", 128), ("ab", 1280), ("bb", 1280)):
+    _buf(_n, _c, "float16", rows=8)
+for _n, _c in (("AN", 1280), ("BA", 1280), ("hb0", 128), ("hb1", 128), ("tt0", 128), ("tt1", 128),
+               ("yof", 256), ("yh2", 256), ("yhf", 256)):
+    _buf(_n, _c, "float32")
+_buf("off", 256, "uint16")
+_buf("LS0", 8, "uint16")
+_buf("LS1", 8, "uint16")
+for _t in range(4):
+    for _c in range(2):
+        _buf("SD%d%d" % (_t, _c), 128, "float16")
+        _buf("R%d%d" % (_t + 1, _c), 128, "float16")
+        SEMAPHORES.append("r%d%d" % (_t + 1, _c))
+for _t in (1, 2, 3):
+    SEMAPHORES.append("l%d" % _t)
+for _n in ("own", "lm", "heir", "heir2", "da", "db", "yha", "yhb", "bk0", "bk1", "bk2", "bk3"):
+    SEMAPHORES.append("d_" + _n)
+for _k in range(8):
+    _buf("b%d" % _k, 512, "float32", "psum")
+BANKS = ["b%d" % _k for _k in range(8)]
+
+
+def rank_program(g, core, T, topo):
+    rank = T.rank_of(core)
+    if rank is None:
+        return
+    n = len(T.cores)
+    eng = {"v": g.vector, "s": g.scalar, "t": g.tensor, "p": g, "y": g.sync}
+    know = {q: {} for q in eng}
+    cnt = {}
+    snap = {}
+    wr, rd, acc = {}, {}, {}
+
+    def wait(q, deps):
+        todo = {s: c for s, c in deps.items() if know[q].get(s, 0) < c}
+        for s, c in sorted(todo.items()):
+            if any(o != s and snap.get((o, oc), {}).get(s, 0) >= c for o, oc in todo.items()):
+                continue
+            eng[q].wait_ge(T.sem[s], c)
+        for s, c in todo.items():
+            for s2, c2 in snap.get((s, c), {}).items():
+                know[q][s2] = max(know[q].get(s2, 0), c2)
+            know[q][s] = max(know[q].get(s, 0), c)
+
+    def deps_of(q, reads, writes):
+        d = {}
+
+        def put(src, skip=None):
+            for s, c in src.items():
+                if s != skip:
+                    d[s] = max(d.get(s, 0), c)
+        for k in list(reads) + list(writes):
+            if k in BANKS:
+                put(acc.get(k, {}), q)
+            else:
+                put(wr.get(k, {}))
+        for k in writes:
+            if k not in BANKS:
+                put(rd.get(k, {}))
+        return d
+
+    def note(q, sem, inc, reads, writes):
+        cnt[sem] = cnt.get(sem, 0) + inc
+        c = cnt[sem]
+        snap[(sem, c)] = dict(know[q])
+        for k in list(reads) + list(writes):
+            if k in BANKS:
+                acc.setdefault(k, {})[sem] = c
+        for k in reads:
+            if k not in BANKS:
+                rd.setdefault(k, {})[sem] = c
+        for k in writes:
+            if k not in BANKS:
+                wr[k] = {sem: c}
+                rd[k] = {}
+
+    def op(q, fn, reads, writes, sem=None, inc=1):
+        wait(q, deps_of(q, reads, writes))
+        sem = sem or q
+        fn().then_inc(T.sem[sem], inc)
+        note(q, sem, inc, reads, writes)
+
+    def ts(out, in0, s1, op0, reads, writes, s2=None, op1=None):
+        if op1 is None:
+            op("v", lambda: g.vector.tensor_scalar(out=out, in0=in0, scalar1=s1, scalar2=None, op0=op0), reads, writes)
+        else:
+            op("v", lambda: g.vector.tensor_scalar(out=out, in0=in0, scalar1=s1, scalar2=s2, op0=op0, op1=op1), reads, writes)
+
+    def tt(out, in0, in1, o, reads, writes):
+        op("v", lambda: g.vector.tensor_tensor(out=out, in0=in0, in1=in1, op=o), reads, writes)
+
+    def vcopy(out, in_, reads, writes):
+        op("v", lambda: g.vector.tensor_copy(out=out, in_=in_), reads, writes)
+
+    def act(out, in_, reads, writes, func=F.Copy, **kw):
+        op("s", lambda: g.scalar.activation(out=out, in_=in_, func=func, **kw), reads, writes)
+
+    def mm(out, lhsT, rhs, start, stop, reads, writes):
+        op("t", lambda: g.tensor.matmul(out=out, lhsT=lhsT, rhs=rhs, start=start, stop=stop), reads, writes)
+
+    def load(q, out, in_, sem, key):
+        op(q, lambda: eng[q].dma_start(out=out, in_=in_), [], [key], sem, 16)
+
+    b = [T[k] for k in BANKS]
+
+    load("y", T.lm0[:], T.lm[:], "d_lm", "lm0")
+    load("s", T.heirI[0:64, :], T.heir[:], "d_heir", "heirA")
+    load("s", T.heirI[64:128, :], T.heir[:], "d_heir2", "heirB")
+    load("y", T.daI[:], T.da[:], "d_da", "daI")
+    load("s", T.dbI[:], T.db[:], "d_db", "dbI")
+    load("y", T.ownI[:], T.own[:], "d_own", "ownI")
+    PIECE = (0, 1536, 2560, 3584, 4096)
+    for k in range(4):
+        lo, hi = PIECE[k], PIECE[k + 1]
+        load("s" if k % 2 == 0 else "y", T.W[:, lo:hi], T.bk[:, lo:hi], "d_bk%d" % k, "Wk%d" % k)
+    WK = ["Wk%d" % k for k in range(4)]
+    HK = ["HN%d" % k for k in range(8)]
+
+    op("p", lambda: g.iota(T.pi[:], [[0, 1]], 0, 1), [], ["pi"])
+    op("p", lambda: g.iota(T.ci[:], [[1, 128]], 0, 0), [], ["ci"])
+
+    def send(dst, out, in_, sem, key):
+        wait("p", deps_of("p", [key], []))
+        rid, pid, _ = topo.addr(dst)
+        ne = len(topo.engines(core, dst))
+        g.remote_dma(out, in_, T.sem[sem], T.sem.loc, pid, rid, topo.mask(core, dst))
+        cnt["loc"] = cnt.get("loc", 0) + ne
+
+    def arrive(sem, key, src):
+        ne = len(topo.engines(src, core))
+        cnt[sem] = ne
+        wr[key] = {sem: ne}
+        rd[key] = {}
+
+    for t in (1, 2, 3):
+        send(T.cores[(rank + t) % n], T["lm%d" % t][:], T.lm0[:], "l%d" % t, "lm0")
+        arrive("l%d" % t, "lm%d" % t, T.cores[(rank - t) % n])
+
+    BITS = (("pg", 3, 7), ("ph", 6, None), ("pk", 0, 7), ("p4", 4, None), ("p2", 1, 7), ("p15", 0, 15))
+    for k, sh, m in BITS:
+        ts(T[k + "i"][:], T.pi[:], sh, A.arith_shift_right, ["pi"], [k + "i"], m, A.bitwise_and if m else None)
+    vcopy(T.pf[:], T.pi[:], ["pi"], ["pf"])
+    for k, sh, m in BITS:
+        vcopy(T[k][:], T[k + "i"][:], [k + "i"], [k])
+    ts(T.c4i[:], T.ci[:], 4, A.arith_shift_right, ["ci"], ["c4i"])
+    ts(T.th[:], T.pg[:], 16.0, A.mult, ["pg"], ["th"])
+    ts(T.pk[:], T.pk[:], 1.0, A.add, ["pk"], ["pk"])
+    ts(T.c15i[:], T.ci[:], 15, A.bitwise_and, ["ci"], ["c15i"])
+    tt(T.th[:], T.th[:], T.ph[:], A.add, ["th", "ph"], ["th"])
+    ts(T.tn[:], T.p4[:], 16.0, A.mult, ["p4"], ["tn"], 2.0, A.add)
+    ts(T.hb2[:], T.ph[:], -2048.0, A.mult, ["ph"], ["hb2"], 2048.0, A.add)
+    ts(T.Z2[:], T.ci[:], T.th[:], A.is_equal, ["ci", "th", "pk"], ["Z2"], T.pk[:], A.mult)
+    tt(T.tn[:], T.tn[:], T.p2[:], A.add, ["tn", "p2"], ["tn"])
+    ts(T.BO[:], T.c4i[:], T.p4[:], A.is_equal, ["c4i", "p4"], ["BO"])
+    ts(T.E8[:], T.c4i[0:8, :], T.pf[0:8, :], A.is_equal, ["c4i", "pf"], ["E8"])
+    for k in range(8):
+        ts(T.WH[:, 128 * k:128 * k + 128], T.Z2[:], float(k + 1), A.is_equal, ["Z2"], ["WH%d" % k])
+    ts(T.hcut[0:64, :], T.heirI[0:64, :], 4080, A.bitwise_and, ["heirA"], ["hcA"])
+    ts(T.hcut[64:128, :], T.heirI[64:128, :], 15, A.bitwise_and, ["heirB"], ["hcB"])
+    ts(T.C01[:], T.c15i[:], 1, A.is_le, ["c15i"], ["C01"])
+    ts(T.Hs[:], T.hcut[:], T.hb2[:], A.subtract, ["hcA", "hcB", "hb2"], ["Hs"])
+    ts(T.l01[:], T.p15[:], 1.0, A.is_le, ["p15"], ["l01"])
+    ts(T.l29[:], T.p15[:], 9.0, A.is_le, ["p15"], ["l29"])
+    ts(T.WN[:], T.ci[:], T.tn[:], A.is_equal, ["ci", "tn"], ["WN"])
+    ts(T.nE8[:], T.E8[:], -1.0, A.mult, ["E8"], ["nE8"])
+    tt(T.l29[:], T.l29[:], T.l01[:], A.subtract, ["l29", "l01"], ["l29"])
+    tt(T.E01[:], T.E8[:], T.C01[0:8, :], A.mult, ["E8", "C01"], ["E01"])
+    ts(T.m1[:], T.p15[:], 1.0, A.is_equal, ["p15"], ["m1"])
+    ts(T.cb[:], T.l29[:], -256.0, A.mult, ["l29"], ["cb"])
+    ts(T.ncb[:], T.l29[:], 256.0, A.mult, ["l29"], ["ncb"])
+    ts(T.maskP[:], T.c15i[:], T.p15[:], A.is_equal, ["c15i", "p15"], ["maskP"])
+
+    XB = (2, 3, 0, 1, 7, 2, 3, 0)
+
+    def x_heir(k):
+        bk = "b%d" % XB[k]
+        mm(T[bk][:], T.WH[:, 128 * k:128 * k + 128], T.Hs[:], True, False, ["WH%d" % k, "Hs"], [bk])
+
+    def x_book(k):
+        bk = "b%d" % XB[k]
+        wk = "Wk%d" % (0 if k < 3 else 1 if k < 5 else 2 if k < 7 else 3)
+        mm(T[bk][:], T.WN[:], T.W[:, 512 * k:512 * k + 512], False, True, ["WN", wk], [bk])
+
+    def x_copy(k):
+        bk = "b%d" % XB[k]
+        if k in VCOPY:
+            ts(T.HN[:, 512 * k:512 * k + 512], T[bk][:], T.cb[:], A.add, [bk, "cb"], ["HN%d" % k])
+        else:
+            act(T.HN[:, 512 * k:512 * k + 512], T[bk][:], [bk, "cb"], ["HN%d" % k], func=F.Identity, bias=T.cb[:])
+
+    CUT = (0, 256, 512, 1280)
+
+    def indices(k, what="ab"):
+        lo, hi = CUT[k], CUT[k + 1]
+        if "a" in what:
+            ts(T.ab[:, lo:hi], T.daI[:, lo:hi], BIAS, A.subtract, ["daI"], ["ab%d" % k])
+        if "b" in what:
+            ts(T.bb[:, lo:hi], T.dbI[:, lo:hi], BIAS, A.subtract, ["dbI"], ["bb%d" % k])
+
+    indices(0)
+    ts(T.ownH[:], T.ownI[:], BIAS, A.subtract, ["ownI"], ["ownH"])
+
+    AK = {0: 1, 1: 2, 3: 3}
+    AR = [(0, 256), (256, 512), (512, 1024), (1024, 1280)]
+
+    def rng(t):
+        return (0, 1, 2, 2, 3)[t]
+
+    def an_t(k):
+        lo, hi = AR[k]
+        w = hi - lo
+        kk = str(min(k, 2))
+        mm(b[5][:, 0:w], T.E8[:], T.ab[:, lo:hi], True, True, ["E8", "ab" + kk], ["b5"])
+        mm(b[6][:, 0:w], T.E8[:], T.bb[:, lo:hi], True, False, ["E8", "bb" + kk], ["b6"])
+        mm(b[6][:, 0:w], T.nE8[:], T.ab[:, lo:hi], False, True, ["nE8", "ab" + kk], ["b6"])
+
+    def an_s(k):
+        lo, hi = AR[k]
+        act(T.AN[:, lo:hi], b[5][:, 0:hi - lo], ["b5"], ["AN%d" % k])
+        act(T.BA[:, lo:hi], b[6][:, 0:hi - lo], ["b6"], ["BA%d" % k])
+
+    def prep_bank(t):
+        return "b4" if t == 0 else "b7"
+
+    def prep_t(t):
+        kk = str(min(t, 2))
+        lk = "lm%d" % (t % n)
+        bk = prep_bank(t)
+        mm(T[bk][:, 0:256], T.WN[:], T[lk][:], True, False, ["WN", lk], [bk])
+        mm(T[bk][:, 0:256], T.E01[:], T.bb[:, 256 * t:256 * t + 256], False, True, ["E01", "bb" + kk], [bk])
+        for ch in range(2):
+            mm(T[bk][:, 256 + 128 * ch:384 + 128 * ch], T.ab[:, 256 * t + 128 * ch:256 * t + 128 * ch + 128], T.E8[:], True, True,
+               ["ab" + kk, "E8"], [bk])
+
+    def prep_s(t):
+        bk = prep_bank(t)
+        act(T.Yn[:], T[bk][:, 0:256], [bk, "m1", "ncb"], ["Yn"], func=F.Identity, scale=T.m1[:], bias=T.ncb[:])
+
+    def prep_nh(t):
+        bk = prep_bank(t)
+        tt(T["NH%d" % (t % 2)][:], T[bk][:, 0:256], T.Yn[:], A.subtract, [bk, "Yn"], ["NH%d" % (t % 2)])
+
+    def prep_ma(t):
+        k, bk = "MA%d" % (t % 2), prep_bank(t)
+        for ch in range(2):
+            tt(T[k][:, 128 * ch:128 * ch + 128], T[bk][:, 256 + 128 * ch:384 + 128 * ch], T.maskP[:], A.mult, [bk, "maskP"], [k + "c%d" % ch])
+
+    def rep(t, qs, who):
+        k = "lm%d" % t
+        for q in qs:
+            if who == "v":
+                vcopy(T["lr%d" % t][:, q:4096:16], T[k][:], [k], ["lr%d_%d" % (t, q)])
+            else:
+                act(T["lr%d" % t][:, q:4096:16], T[k][:], [k], ["lr%d_%d" % (t, q)])
+
+    def own_of(t, ch):
+        if t == 0:
+            return T.ownH[:, 128 * ch:128 * ch + 128], "ownH"
+        return b[2 + ch][:, 0:128], "b%d" % (2 + ch)
+
+    def deeds_hit(t, ch):
+        c = str(ch)
+        k = str(rng(t))
+        cols = slice(256 * t + 128 * ch, 256 * t + 128 * ch + 128)
+        if t:
+            rk = "R%d%d" % (t, ch)
+            mm(b[2 + ch][:, 0:128], T[rk][:], T.IdH[:], True, True, [rk, "IdH"], ["b%d" % (2 + ch)])
+        own, ok = own_of(t, ch)
+        tt(T["HT" + c][:], own, T.AN[:, cols], A.is_equal, [ok, "AN" + k], ["HT" + c])
+        mm(b[5 + ch][:, 0:128], T["HT" + c][:], T.BO[:], True, True, ["HT" + c, "BO"], ["b%d" % (5 + ch)])
+        tt(T["hb" + c][:], T["HT" + c][:], T.BA[:, cols], A.mult, ["HT" + c, "BA" + k], ["hb" + c])
+
+    def deeds_list(t, ch):
+        c = str(ch)
+        loc = slice(128 * ch, 128 * ch + 128)
+        own, ok = own_of(t, ch)
+        tt(T["X" + c][:], b[5 + ch][:, 0:128], T.maskP[:], A.min, ["b%d" % (5 + ch), "maskP"], ["X" + c])
+        m = "MA%d" % (t % 2)
+        lst = b[4][:, 8 * ch:8 * ch + 8]
+        mm(lst, T[m][:, loc], T.K1[:], True, False, [m + "c" + c, "K1"], ["b4"])
+        mm(lst, T["X" + c][:], T.K4[:], False, True, ["X" + c, "K4"], ["b4"])
+        tt(T["ownN" + c][:], own, T["hb" + c][:], A.add, [ok, "hb" + c], ["ownN" + c])
+
+    def deeds_end(ch):
+        c = str(ch)
+        ts(T["LS" + c][:], b[4][:, 8 * ch:8 * ch + 8], BIAS, A.add, ["b4"], ["LS" + c])
+
+    def scatter_h(t, ch):
+        c = str(ch)
+        h = "NH%d" % (t % 2)
+        loc = slice(128 * ch, 128 * ch + 128)
+        vcopy(T.HN[:, 0:8192].indirect(T["LS" + c][:, 0:8]), T[h][:, loc], ["LS" + c, h], HK)
+
+    def scatter_w(t, ch):
+        c = str(ch)
+        l = "lm%d" % (t % n)
+        loc = slice(128 * ch, 128 * ch + 128)
+        vcopy(T.W[:, 0:8192].indirect(T["LS" + c][:, 0:8]), T[l][:, loc], ["LS" + c, l], WK)
+
+    def offs(ch):
+        ts(T.off[:, 128 * ch:128 * ch + 128], T["ownN%d" % ch][:], BIAS, A.add, ["ownN%d" % ch], ["off%d" % ch])
+
+    def gv(t, ch, lo, hi):
+        a, z = 128 * ch + lo, 128 * ch + hi
+        m, l = "M%d" % ch, "lr%d" % (t % n)
+        op("v", lambda: g.vector.tensor_tensor(out=T[m][:, 16 * lo:16 * hi], in0=T.W[:, 0:4096].indirect(T.off[:, a:z]),
+                                               in1=T[l][:, 16 * a:16 * z], op=A.max),
+           WK + ["off%d" % ch] + [l + "_%d" % q for q in range(16)], [m + "_%d" % lo])
+
+    def gs(ch, lo, hi):
+        a, z = 128 * ch + lo, 128 * ch + hi
+        act(T["H%d" % ch][:, 16 * lo:16 * hi], T.HN[:, 0:4096].indirect(T.off[:, a:z]), HK + ["off%d" % ch], ["H%d_%d" % (ch, lo)])
+
+    MK = {c: ["M%d_0" % c, "M%d_%d" % (c, VS)] for c in (0, 1)}
+    HHK = {c: ["H%d_0" % c, "H%d_%d" % (c, SS)] for c in (0, 1)}
+
+    def gather_whole(t, ch):
+        gv(t, ch, 0, 128)
+        wr[MK[ch][1]] = dict(wr[MK[ch][0]])
+        gs(ch, 0, 128)
+        wr[HHK[ch][1]] = dict(wr[HHK[ch][0]])
+
+    def init(t, ch, p):
+        l, bk = "lm%d" % (t % n), "b%d" % ch
+        mm(b[ch][:, 0:128], T[l][:, 128 * ch:128 * ch + 128], T.nBO[:], True, False, [l, "nBO"], [bk])
+        if p == 0:
+            mm(b[ch][:, 128:384], T["ownN%d" % ch][:], T.HI2[:], False, False, ["ownN%d" % ch, "HI2"], [bk])
+        else:
+            for k in (1, 2):
+                mm(b[ch][:, 128 * k:128 * k + 128], T.HI2[:, 0:128], T["OT%d" % ch][:], False, False, ["HI2", "OT%d" % ch], [bk])
+
+    def sums(ch):
+        for q in range(16):
+            mm(b[ch][:, q:384:16], T["H%d" % ch][:, q:2048:16], T.RH[:], False, False, HHK[ch] + ["RH"], ["b%d" % ch])
+        for q in range(16):
+            mm(b[ch][:, q:128:16], T["M%d" % ch][:, q:2048:16], T.RM[:], False, q == 15, MK[ch] + ["RM"], ["b%d" % ch])
+
+    def sign(ch):
+        act(T["SG%d" % ch][:], b[ch][:, 0:128], ["b%d" % ch], ["SG%d" % ch], func=F.Sign, bias=-TH)
+
+    def upd(ch, dst):
+        c = str(ch)
+        tt(T["tt" + c][:], T["SG" + c][:], b[ch][:, 128:256], A.mult, ["SG" + c, "b" + c], ["tt" + c])
+        tt(T[dst][:], b[ch][:, 256:384], T["tt" + c][:], A.add, ["b" + c, "tt" + c], [dst])
+
+    def turn(ch, src):
+        mm(b[2 + ch][:, 0:128], T[src][:], T.IdH[:], True, True, [src, "IdH"], ["b%d" % (2 + ch)])
+
+    def conv(ch):
+        ts(T.off[:, 128 * ch:128 * ch + 128], b[2 + ch][:, 0:128], BIAS, A.add, ["b%d" % (2 + ch)], ["off%d" % ch])
+
+    act(T.nBO[:], T.BO[:], ["BO"], ["nBO"], scale=-1.0)
+    act(T.RM[:], T.BO[:, 0:128:16], ["BO"], ["RM"], scale=2.0)
+    act(T.K4[:], T.BO[:, 0:128:16], ["BO"], ["K4"], scale=4096.0)
+    for k in (0, 1):
+        x_heir(k)
+    an_t(0)
+    an_s(0)
+    prep_t(0)
+    prep_s(0)
+    for k in (2, 3, 4):
+        x_heir(k)
+    ts(T.K1[:], T.BO[:, 0:128:16], 1.0, A.mult, ["BO"], ["K1"])
+    indices(1)
+    prep_ma(0)
+    prep_nh(0)
+    for k in (0, 1, 2):
+        x_book(k)
+    rep(0, range(6), "s")
+    x_copy(0)
+    deeds_hit(0, 0)
+    deeds_hit(0, 1)
+    x_heir(5)
+    x_copy(1)
+    x_copy(2)
+    ts(T.HI2[:, 0:128], T.ci[:], T.pf[:], A.is_equal, ["ci", "pf"], ["HI2"], 0.5, A.mult)
+    ts(T.HI2[:, 128:256], T.ci[:], T.pf[:], A.is_equal, ["ci", "pf"], ["HI2"], 0.5, A.mult)
+    deeds_list(0, 0)
+    deeds_list(0, 1)
+    x_heir(6)
+    x_heir(7)
+    rep(0, range(6, 16 - VR0), "s")
+    ts(T.RH[:, 0:8], T.BO[:, 0:128:16], T.l29[:], A.mult, ["BO", "l29"], ["RH"], -1.0, A.mult)
+    ts(T.RH[:, 8:16], T.BO[:, 0:128:16], T.l01[:], A.mult, ["BO", "l01"], ["RH"], -0.5, A.mult)
+    ts(T.RH[:, 16:24], T.BO[:, 0:128:16], T.l01[:], A.mult, ["BO", "l01"], ["RH"], 0.5, A.mult)
+    ts(T.IdH[:], T.ci[:], T.pf[:], A.is_equal, ["ci", "pf"], ["IdH"])
+    offs(0)
+    offs(1)
+    deeds_end(0)
+    deeds_end(1)
+    for k in range(3, 8):
+        x_book(k)
+        x_copy(k)
+    rep(0, range(16 - VR0, 16), "v")
+    scatter_w(0, 0)
+    scatter_h(0, 0)
+    scatter_h(0, 1)
+    scatter_w(0, 1)
+
+    nxt = T.cores[(rank + 1) % n]
+    prv = T.cores[(rank - 1) % n]
+    for t in range(1, R):
+        for ch in range(2):
+            arrive("r%d%d" % (t, ch), "R%d%d" % (t, ch), prv)
+
+    def out_yo(ch):
+        loc = slice(128 * ch, 128 * ch + 128)
+        ts(T.yof[:, loc], b[2 + ch][:, 0:128], float(BIAS), A.add, ["b%d" % (2 + ch)], ["yof%d" % ch])
+        op("y", lambda: g.sync.dma_start(out=T.yo[:, loc], in_=T.yof[:, loc]), ["yof%d" % ch], [], "dout", 16)
+
+    for t in range(R):
+        last = t == R - 1
+        if t:
+            for ch in (0, 1):
+                deeds_hit(t, ch)
+                deeds_list(t, ch)
+                if ch == 0:
+                    offs(0)
+                deeds_end(ch)
+                scatter_h(t, ch)
+                scatter_w(t, ch)
+        init(t, 0, 0)
+        init(t, 1, 0)
+        if not last:
+            prep_t(t + 1)
+        if t in AK:
+            an_t(AK[t])
+        gather_whole(t, 0)
+        if t:
+            offs(1)
+        if last:
+            for k, lane in (("yha", 0), ("yhb", 1)):
+                op("y", lambda: g.sync.dma_start(out=T[k][:], in_=T.HN[lane:128:16, 0:4096]), HK, [k], "d_" + k, 16)
+            op("y", lambda: g.sync.dma_start(out=T.yd[:], in_=T.W[:, 0:4096]), WK, [], "dout", 16)
+        sums(0)
+        gv(t, 1, 0, VS)
+        gs(1, 0, SS)
+        sign(0)
+        gs(1, SS, 128)
+        upd(0, "OT0")
+        turn(0, "OT0")
+        init(t, 0, 1)
+        gv(t, 1, VS, 128)
+        conv(0)
+        sums(1)
+        gv(t, 0, 0, VS)
+        gs(0, 0, SS)
+        sign(1)
+        gs(0, SS, 128)
+        if last:
+            act(T.yh2[:], T.yha[:], ["yha"], ["yh2"], bias=float(BIAS))
+        upd(1, "OT1")
+        turn(1, "OT1")
+        conv(1)
+        init(t, 1, 1)
+        gv(t, 0, VS, 128)
+        sums(0)
+        gather_whole(t, 1)
+        sign(0)
+        sums(1)
+        if not last:
+            upd(0, "SD%d0" % t)
+            send(nxt, T["R%d0" % (t + 1)][:], T["SD%d0" % t][:], "r%d0" % (t + 1), "SD%d0" % t)
+            prep_s(t + 1)
+            if t in AK:
+                an_s(AK[t])
+            prep_ma(t + 1)
+            if t == 0:
+                indices(2, "a")
+            sign(1)
+            upd(1, "SD%d1" % t)
+            send(nxt, T["R%d1" % (t + 1)][:], T["SD%d1" % t][:], "r%d1" % (t + 1), "SD%d1" % t)
+            prep_nh(t + 1)
+            if t + 1 < n:
+                rep(t + 1, range(16 - VR, 16), "v")
+                rep(t + 1, range(16 - VR), "s")
+            if t == 0:
+                indices(2, "b")
+        else:
+            tt(T.yhf[:], T.yh2[:], T.yhb[:], A.add, ["yh2", "yhb"], ["yhf"])
+            op("y", lambda: g.sync.dma_start(out=T.yh[:], in_=T.yhf[:]), ["yhf"], [], "dout", 16)
+            upd(0, "OT0")
+            turn(0, "OT0")
+            out_yo(0)
+            sign(1)
+            upd(1, "OT1")
+            turn(1, "OT1")
+            out_yo(1)
+
+    g.sync.wait_ge(T.sem.dout, cnt["dout"])
+    wait("p", {s: c for s, c in cnt.items() if s != "dout"})

@@ -2,10 +2,15 @@ from concourse.mybir import AluOpType as A, ActivationFunctionType as F
 
 BIAS = 2048
 TH = 136.5 + 2048
+FAR = 256.0
 R = 5
-VS, SS = 104, 88
-VR0, VR = 2, 3
-VCOPY = (1, 4, 6)
+WIN = 8192
+VS, SS = 96, 80
+VL, SL = 64, 48
+REP0 = {"v": range(0, 7), "s": range(7, 12), "p": range(12, 16)}
+REP = {"s": range(0, 4), "p": range(4, 16)}
+VCOPY = (1, 3, 5, 7)
+PIECE = (0, 1536, 2560, 3584, 4096)
 
 SCRATCH = {}
 SEMAPHORES = ["v", "s", "t", "p", "loc", "dout"]
@@ -15,27 +20,24 @@ def _buf(name, cols, dtype, where="sbuf", rows=128):
     SCRATCH[name] = (where, [rows, cols], dtype)
 
 
-for _n, _c in (("pi", 1), ("ci", 128), ("p15i", 1), ("p4i", 1), ("p2i", 1), ("pki", 1), ("pgi", 1), ("phi", 1),
-               ("c15i", 128), ("c4i", 128), ("ownI", 256), ("heirI", 512), ("hcut", 512)):
+for _n, _c in (("pi", 1), ("p15i", 1), ("gi", 8), ("g4i", 8), ("ownI", 256), ("heirI", 512)):
     _buf(_n, _c, "int32")
-_buf("daI", 1280, "int32", rows=8)
-_buf("dbI", 1280, "int32", rows=8)
-for _n in ("pf", "p15", "p4", "p2", "pk", "pg", "ph", "tn", "th", "hb2", "l01", "l29", "m1", "cb", "ncb"):
+_buf("abI", 1280, "int32", rows=24)
+for _n in ("p15", "c8", "wN", "wh", "wh1", "cb", "cb1", "cb2", "cb3", "gb", "e64", "hs", "hb", "e16", "fs", "fb"):
     _buf(_n, 1, "float32")
-for _n, _c in (("BO", 128), ("nBO", 128), ("maskP", 128), ("C01", 128), ("WN", 128), ("Z2", 128),
-               ("RM", 8), ("RH", 24), ("K4", 8), ("yha", 256), ("yhb", 256),
-               ("W", 8192), ("HN", 8192), ("M0", 2048), ("M1", 2048), ("H0", 2048), ("H1", 2048),
-               ("Yn", 256), ("NH0", 256), ("NH1", 256), ("HT0", 128), ("HT1", 128), ("X0", 128), ("X1", 128),
-               ("SG0", 128), ("SG1", 128), ("lm0", 256), ("lm1", 256), ("lm2", 256), ("lm3", 256),
+for _n, _c in (("dv", 128), ("ev", 128), ("c15", 128), ("maskP", 128), ("B8", 8), ("K4", 8), ("nK4", 8), ("nBO", 128), ("WN", 128), ("WH", 1024),
+               ("Id", 128), ("HI", 256), ("BI", 128), ("I16", 128), ("RM", 8), ("RH0", 24), ("RH1", 24), ("yha", 256), ("yhb", 256),
+               ("W", WIN), ("M0", 2048), ("M1", 2048), ("H0", 2048), ("H1", 2048), ("HT0", 128), ("HT1", 128), ("XM0", 128), ("XM1", 128),
+               ("SA0", 128), ("SA1", 128), ("SB0", 128), ("SB1", 128), ("lm0", 256), ("lm1", 256), ("lm2", 256), ("lm3", 256),
                ("lr0", 4096), ("lr1", 4096), ("lr2", 4096), ("lr3", 4096)):
     _buf(_n, _c, "bfloat16")
-for _n, _c in (("IdH", 128), ("HI2", 256), ("WH", 1024), ("K1", 8), ("Hs", 512), ("ownH", 256), ("ownN0", 128), ("ownN1", 128),
-               ("OT0", 128), ("OT1", 128), ("MA0", 256), ("MA1", 256)):
+for _n, _c in (("nEA", 128), ("EB", 128), ("EN", 128), ("BigA", 144)):
+    _buf(_n, _c, "bfloat16", rows=24)
+_buf("ab", 1280, "float16", rows=24)
+for _n, _c in (("Hs", 512), ("ownH", 256), ("ownN0", 128), ("ownN1", 128), ("hT0", 128), ("hT1", 128), ("OT0", 128), ("OT1", 128)):
     _buf(_n, _c, "float16")
-for _n, _c in (("E8", 128), ("nE8", 128), ("E01", 128), ("ab", 1280), ("bb", 1280)):
-    _buf(_n, _c, "float16", rows=8)
-for _n, _c in (("AN", 1280), ("BA", 1280), ("hb0", 128), ("hb1", 128), ("tt0", 128), ("tt1", 128),
-               ("yof", 256), ("yh2", 256), ("yhf", 256)):
+for _n, _c in (("HN", WIN), ("NH0", 256), ("NH1", 256), ("OH", 3), ("I32", 128), ("hb0", 128), ("hb1", 128), ("ta0", 128), ("ta1", 128),
+               ("tb0", 128), ("tb1", 128), ("yof", 256), ("yhf", 256)):
     _buf(_n, _c, "float32")
 _buf("off", 256, "uint16")
 _buf("LS0", 8, "uint16")
@@ -47,11 +49,11 @@ for _t in range(4):
         SEMAPHORES.append("r%d%d" % (_t + 1, _c))
 for _t in (1, 2, 3):
     SEMAPHORES.append("l%d" % _t)
-for _n in ("own", "lm", "heir", "heir2", "da", "db", "yha", "yhb", "bk0", "bk1", "bk2", "bk3"):
+for _n in ("own", "lm", "heir", "ab", "yh", "bk0", "bk1", "bk2", "bk3"):
     SEMAPHORES.append("d_" + _n)
-for _k in range(8):
-    _buf("b%d" % _k, 512, "float32", "psum")
-BANKS = ["b%d" % _k for _k in range(8)]
+BANKS = ["X0", "X1", "Y0", "Y1", "T0", "T1", "L", "N"]
+for _n in BANKS:
+    _buf(_n, 512, "float32", "psum")
 
 
 def rank_program(g, core, T, topo):
@@ -126,6 +128,9 @@ def rank_program(g, core, T, topo):
     def vcopy(out, in_, reads, writes):
         op("v", lambda: g.vector.tensor_copy(out=out, in_=in_), reads, writes)
 
+    def zero(k):
+        op("v", lambda: g.vector.memset(T[k][:], 0.0), [], [k])
+
     def act(out, in_, reads, writes, func=F.Copy, **kw):
         op("s", lambda: g.scalar.activation(out=out, in_=in_, func=func, **kw), reads, writes)
 
@@ -135,23 +140,69 @@ def rank_program(g, core, T, topo):
     def load(q, out, in_, sem, key):
         op(q, lambda: eng[q].dma_start(out=out, in_=in_), [], [key], sem, 16)
 
-    b = [T[k] for k in BANKS]
+    def iota(k, pattern, base, cm):
+        small = SCRATCH[k][2] != "int32"
+        op("p", lambda: g.iota(T[k][:], pattern, base, cm, allow_small_or_imprecise_dtypes=True) if small
+           else g.iota(T[k][:], pattern, base, cm), [], [k])
 
-    load("y", T.lm0[:], T.lm[:], "d_lm", "lm0")
+    def mark(ap, key, pattern, base, value):
+        op("p", lambda: g.affine_select(ap, ap, pattern, A.not_equal, value, base, 1), [key], [key])
+
     load("s", T.heirI[0:64, :], T.heir[:], "d_heir", "heirA")
-    load("s", T.heirI[64:128, :], T.heir[:], "d_heir2", "heirB")
-    load("y", T.daI[:], T.da[:], "d_da", "daI")
-    load("s", T.dbI[:], T.db[:], "d_db", "dbI")
-    load("y", T.ownI[:], T.own[:], "d_own", "ownI")
-    PIECE = (0, 1536, 2560, 3584, 4096)
+    load("y", T.heirI[64:128, :], T.heir[:], "d_heir", "heirI")
+    load("s", T.abI[0:8, :], T.da[:], "d_ab", "abA")
+    load("y", T.abI[8:16, :], T.db[:], "d_ab", "abB")
+    load("s", T.abI[16:24, :], T.db[:], "d_ab", "abI")
+    load("y", T.lm0[:], T.lm[:], "d_lm", "lm0")
+    load("s", T.ownI[:], T.own[:], "d_own", "ownI")
     for k in range(4):
         lo, hi = PIECE[k], PIECE[k + 1]
-        load("s" if k % 2 == 0 else "y", T.W[:, lo:hi], T.bk[:, lo:hi], "d_bk%d" % k, "Wk%d" % k)
+        load("y" if k % 2 == 0 else "s", T.W[:, lo:hi], T.bk[:, lo:hi], "d_bk%d" % k, "Wk%d" % k)
     WK = ["Wk%d" % k for k in range(4)]
     HK = ["HN%d" % k for k in range(8)]
 
-    op("p", lambda: g.iota(T.pi[:], [[0, 1]], 0, 1), [], ["pi"])
-    op("p", lambda: g.iota(T.ci[:], [[1, 128]], 0, 0), [], ["ci"])
+    iota("pi", [[0, 1]], 0, 1)
+    iota("gi", [[-16, 8]], 0, 1)
+    for k in ("WH", "EN", "BigA", "HI"):
+        zero(k)
+    iota("c15", [[0, 8], [1, 16]], 0, 0)
+    mark(T.WH[:, 0:1024:16], "WH", [[-1, 8], [-8, 8]], -64, 16.0)
+    mark(T.WH[:, 1:1024:16], "WH", [[-1, 8], [-8, 8]], 0, 16.0)
+    mark(T.WH[:, 1:1024:16], "WH", [[-1, 8], [-8, 8]], -64, -256.0)
+    iota("ev", [[-1, 8], [0, 16]], 0, 1)
+    iota("dv", [[1, 128]], 0, -1)
+    mark(T.EN[:, 0:128:16], "EN", [[-1, 8]], -16, 16.0)
+    mark(T.EN[:, 1:128:16], "EN", [[-1, 8]], -8, 16.0)
+    mark(T.EN[:, 1:128:16], "EN", [[-1, 8]], -16, -256.0)
+    mark(T.BigA[:, 15:128:16], "BigA", [[-1, 8]], 0, 1.0)
+
+    ts(T.p15i[:], T.pi[:], 15, A.bitwise_and, ["pi"], ["p15i"])
+    ts(T.e64[:], T.pi[:], 64.0, A.is_ge, ["pi"], ["e64"])
+    ts(T.g4i[:], T.gi[:], 4, A.arith_shift_right, ["gi"], ["g4i"])
+    vcopy(T.p15[:], T.p15i[:], ["p15i"], ["p15"])
+    ts(T.e16[:], T.pi[:], 16.0, A.is_ge, ["pi"], ["e16"])
+    ts(T.B8[:], T.g4i[:], 0.0, A.is_equal, ["g4i"], ["B8"])
+    ts(T.OH[:], T.c15[:, 0:3], T.p15[:], A.is_equal, ["c15", "p15"], ["OH"])
+    ts(T.wN[:], T.p15[:], 8.0, A.is_ge, ["p15"], ["wN"])
+    ts(T.c8[:], T.p15[:], 7.0, A.is_le, ["p15"], ["c8"], 8.0, A.mult)
+    ts(T.maskP[:], T.c15[:], T.p15[:], A.is_equal, ["c15", "p15"], ["maskP"], -1.0, A.mult)
+    for e, s, b in (("e64", "hs", "hb"), ("e16", "fs", "fb")):
+        act(T[s][:], T[e][:], [e], [s], scale=-15.0 / 16, bias=1.0)
+        act(T[b][:], T[e][:], [e], [b], scale=3072.0, bias=-2048.0)
+    act(T.cb1[:], T.wN[:], ["wN"], ["cb1"], scale=16.0)
+    act(T.gb[:], T.wN[:], ["wN"], ["gb"], scale=-272.0)
+    act(T.cb2[:], T.OH[:, 0:1], ["OH", "cb1"], ["cb2"], func=F.Identity, scale=-16384.0, bias=T.cb1[:])
+    act(T.wh1[:], T.OH[:, 1:2], ["OH"], ["wh1"], func=F.Identity, scale=1.0 / 16, bias=T.OH[:, 0:1])
+    act(T.cb3[:], T.OH[:, 1:2], ["OH", "cb2"], ["cb3"], func=F.Identity, scale=16.0 * (2048 + 16384 + 16), bias=T.cb2[:])
+    act(T.wh[:], T.OH[:, 2:3], ["OH", "wh1"], ["wh"], func=F.Identity, scale=-1.0, bias=T.wh1[:])
+    act(T.cb[:], T.OH[:, 2:3], ["OH", "cb3"], ["cb"], func=F.Identity, scale=2064.0, bias=T.cb3[:])
+    act(T.K4[:], T.B8[:], ["B8"], ["K4"], func=F.Silu, scale=4096.0)
+    act(T.RM[:], T.B8[:], ["B8"], ["RM"], scale=2.0)
+    ts(T.Hs[:], T.heirI[:], T.hs[:], A.mult, ["heirI", "hs", "hb"], ["Hs"], T.hb[:], A.add)
+    ts(T.nEA[:], T.ev[0:24, :], 0.0, A.is_equal, ["ev"], ["nEA"], -1.0, A.mult)
+    ts(T.EB[:], T.ev[0:24, :], 8.0, A.is_equal, ["ev"], ["EB"])
+    ts(T.Id[:], T.dv[:], 0.0, A.is_equal, ["dv"], ["Id"])
+    ts(T.WN[:], T.dv[:], T.c8[:], A.is_equal, ["dv", "c8"], ["WN"])
 
     def send(dst, out, in_, sem, key):
         wait("p", deps_of("p", [key], []))
@@ -166,359 +217,334 @@ def rank_program(g, core, T, topo):
         wr[key] = {sem: ne}
         rd[key] = {}
 
-    for t in (1, 2, 3):
-        send(T.cores[(rank + t) % n], T["lm%d" % t][:], T.lm0[:], "l%d" % t, "lm0")
+    nxt = T.cores[(rank + 1) % n]
+    prv = T.cores[(rank - 1) % n]
+    for t in range(1, n):
         arrive("l%d" % t, "lm%d" % t, T.cores[(rank - t) % n])
+    for t in range(1, R):
+        for ch in range(2):
+            arrive("r%d%d" % (t, ch), "R%d%d" % (t, ch), prv)
 
-    BITS = (("pg", 3, 7), ("ph", 6, None), ("pk", 0, 7), ("p4", 4, None), ("p2", 1, 7), ("p15", 0, 15))
-    for k, sh, m in BITS:
-        ts(T[k + "i"][:], T.pi[:], sh, A.arith_shift_right, ["pi"], [k + "i"], m, A.bitwise_and if m else None)
-    vcopy(T.pf[:], T.pi[:], ["pi"], ["pf"])
-    for k, sh, m in BITS:
-        vcopy(T[k][:], T[k + "i"][:], [k + "i"], [k])
-    ts(T.c4i[:], T.ci[:], 4, A.arith_shift_right, ["ci"], ["c4i"])
-    ts(T.th[:], T.pg[:], 16.0, A.mult, ["pg"], ["th"])
-    ts(T.pk[:], T.pk[:], 1.0, A.add, ["pk"], ["pk"])
-    ts(T.c15i[:], T.ci[:], 15, A.bitwise_and, ["ci"], ["c15i"])
-    tt(T.th[:], T.th[:], T.ph[:], A.add, ["th", "ph"], ["th"])
-    ts(T.tn[:], T.p4[:], 16.0, A.mult, ["p4"], ["tn"], 2.0, A.add)
-    ts(T.hb2[:], T.ph[:], -2048.0, A.mult, ["ph"], ["hb2"], 2048.0, A.add)
-    ts(T.Z2[:], T.ci[:], T.th[:], A.is_equal, ["ci", "th", "pk"], ["Z2"], T.pk[:], A.mult)
-    tt(T.tn[:], T.tn[:], T.p2[:], A.add, ["tn", "p2"], ["tn"])
-    ts(T.BO[:], T.c4i[:], T.p4[:], A.is_equal, ["c4i", "p4"], ["BO"])
-    ts(T.E8[:], T.c4i[0:8, :], T.pf[0:8, :], A.is_equal, ["c4i", "pf"], ["E8"])
-    for k in range(8):
-        ts(T.WH[:, 128 * k:128 * k + 128], T.Z2[:], float(k + 1), A.is_equal, ["Z2"], ["WH%d" % k])
-    ts(T.hcut[0:64, :], T.heirI[0:64, :], 4080, A.bitwise_and, ["heirA"], ["hcA"])
-    ts(T.hcut[64:128, :], T.heirI[64:128, :], 15, A.bitwise_and, ["heirB"], ["hcB"])
-    ts(T.C01[:], T.c15i[:], 1, A.is_le, ["c15i"], ["C01"])
-    ts(T.Hs[:], T.hcut[:], T.hb2[:], A.subtract, ["hcA", "hcB", "hb2"], ["Hs"])
-    ts(T.l01[:], T.p15[:], 1.0, A.is_le, ["p15"], ["l01"])
-    ts(T.l29[:], T.p15[:], 9.0, A.is_le, ["p15"], ["l29"])
-    ts(T.WN[:], T.ci[:], T.tn[:], A.is_equal, ["ci", "tn"], ["WN"])
-    ts(T.nE8[:], T.E8[:], -1.0, A.mult, ["E8"], ["nE8"])
-    tt(T.l29[:], T.l29[:], T.l01[:], A.subtract, ["l29", "l01"], ["l29"])
-    tt(T.E01[:], T.E8[:], T.C01[0:8, :], A.mult, ["E8", "C01"], ["E01"])
-    ts(T.m1[:], T.p15[:], 1.0, A.is_equal, ["p15"], ["m1"])
-    ts(T.cb[:], T.l29[:], -256.0, A.mult, ["l29"], ["cb"])
-    ts(T.ncb[:], T.l29[:], 256.0, A.mult, ["l29"], ["ncb"])
-    ts(T.maskP[:], T.c15i[:], T.p15[:], A.is_equal, ["c15i", "p15"], ["maskP"])
-
-    XB = (2, 3, 0, 1, 7, 2, 3, 0)
+    XB = ("Y0", "Y1", "X0", "X1", "Y0", "Y1", "N", "T0")
 
     def x_heir(k):
-        bk = "b%d" % XB[k]
-        mm(T[bk][:], T.WH[:, 128 * k:128 * k + 128], T.Hs[:], True, False, ["WH%d" % k, "Hs"], [bk])
+        mm(T[XB[k]][:], T.WH[:, 128 * k:128 * k + 128], T.Hs[:], True, False, ["WH", "Hs"], [XB[k]])
 
     def x_book(k):
-        bk = "b%d" % XB[k]
-        wk = "Wk%d" % (0 if k < 3 else 1 if k < 5 else 2 if k < 7 else 3)
-        mm(T[bk][:], T.WN[:], T.W[:, 512 * k:512 * k + 512], False, True, ["WN", wk], [bk])
+        wk = [WK[j] for j in range(4) if PIECE[j] < 512 * k + 512 and PIECE[j + 1] > 512 * k]
+        mm(T[XB[k]][:], T.WN[:], T.W[:, 512 * k:512 * k + 512], False, True, ["WN"] + wk, [XB[k]])
 
     def x_copy(k):
-        bk = "b%d" % XB[k]
+        bk = XB[k]
         if k in VCOPY:
             ts(T.HN[:, 512 * k:512 * k + 512], T[bk][:], T.cb[:], A.add, [bk, "cb"], ["HN%d" % k])
         else:
             act(T.HN[:, 512 * k:512 * k + 512], T[bk][:], [bk, "cb"], ["HN%d" % k], func=F.Identity, bias=T.cb[:])
 
-    CUT = (0, 256, 512, 1280)
+    def indices(t):
+        cols = slice(256 * t, 256 * t + 256)
+        ts(T.ab[:, cols], T.abI[:, cols], T.fs[0:24, :], A.mult, ["abI", "fs", "fb"], ["ab%d" % t], T.fb[0:24, :], A.add)
 
-    def indices(k, what="ab"):
-        lo, hi = CUT[k], CUT[k + 1]
-        if "a" in what:
-            ts(T.ab[:, lo:hi], T.daI[:, lo:hi], BIAS, A.subtract, ["daI"], ["ab%d" % k])
-        if "b" in what:
-            ts(T.bb[:, lo:hi], T.dbI[:, lo:hi], BIAS, A.subtract, ["dbI"], ["bb%d" % k])
-
-    indices(0)
-    ts(T.ownH[:], T.ownI[:], BIAS, A.subtract, ["ownI"], ["ownH"])
-
-    AK = {0: 1, 1: 2, 3: 3}
-    AR = [(0, 256), (256, 512), (512, 1024), (1024, 1280)]
-
-    def rng(t):
-        return (0, 1, 2, 2, 3)[t]
-
-    def an_t(k):
-        lo, hi = AR[k]
-        w = hi - lo
-        kk = str(min(k, 2))
-        mm(b[5][:, 0:w], T.E8[:], T.ab[:, lo:hi], True, True, ["E8", "ab" + kk], ["b5"])
-        mm(b[6][:, 0:w], T.E8[:], T.bb[:, lo:hi], True, False, ["E8", "bb" + kk], ["b6"])
-        mm(b[6][:, 0:w], T.nE8[:], T.ab[:, lo:hi], False, True, ["nE8", "ab" + kk], ["b6"])
-
-    def an_s(k):
-        lo, hi = AR[k]
-        act(T.AN[:, lo:hi], b[5][:, 0:hi - lo], ["b5"], ["AN%d" % k])
-        act(T.BA[:, lo:hi], b[6][:, 0:hi - lo], ["b6"], ["BA%d" % k])
-
-    def prep_bank(t):
-        return "b4" if t == 0 else "b7"
-
-    def prep_t(t):
-        kk = str(min(t, 2))
-        lk = "lm%d" % (t % n)
-        bk = prep_bank(t)
-        mm(T[bk][:, 0:256], T.WN[:], T[lk][:], True, False, ["WN", lk], [bk])
-        mm(T[bk][:, 0:256], T.E01[:], T.bb[:, 256 * t:256 * t + 256], False, True, ["E01", "bb" + kk], [bk])
-        for ch in range(2):
-            mm(T[bk][:, 256 + 128 * ch:384 + 128 * ch], T.ab[:, 256 * t + 128 * ch:256 * t + 128 * ch + 128], T.E8[:], True, True,
-               ["ab" + kk, "E8"], [bk])
-
-    def prep_s(t):
-        bk = prep_bank(t)
-        act(T.Yn[:], T[bk][:, 0:256], [bk, "m1", "ncb"], ["Yn"], func=F.Identity, scale=T.m1[:], bias=T.ncb[:])
-
-    def prep_nh(t):
-        bk = prep_bank(t)
-        tt(T["NH%d" % (t % 2)][:], T[bk][:, 0:256], T.Yn[:], A.subtract, [bk, "Yn"], ["NH%d" % (t % 2)])
-
-    def prep_ma(t):
-        k, bk = "MA%d" % (t % 2), prep_bank(t)
-        for ch in range(2):
-            tt(T[k][:, 128 * ch:128 * ch + 128], T[bk][:, 256 + 128 * ch:384 + 128 * ch], T.maskP[:], A.mult, [bk, "maskP"], [k + "c%d" % ch])
-
-    def rep(t, qs, who):
-        k = "lm%d" % t
-        for q in qs:
-            if who == "v":
-                vcopy(T["lr%d" % t][:, q:4096:16], T[k][:], [k], ["lr%d_%d" % (t, q)])
-            else:
-                act(T["lr%d" % t][:, q:4096:16], T[k][:], [k], ["lr%d_%d" % (t, q)])
-
-    def own_of(t, ch):
-        if t == 0:
-            return T.ownH[:, 128 * ch:128 * ch + 128], "ownH"
-        return b[2 + ch][:, 0:128], "b%d" % (2 + ch)
-
-    def deeds_hit(t, ch):
-        c = str(ch)
-        k = str(rng(t))
+    def prep_deeds(t, ch):
+        bk, k = "T%d" % ch, "ab%d" % t
         cols = slice(256 * t + 128 * ch, 256 * t + 128 * ch + 128)
-        if t:
-            rk = "R%d%d" % (t, ch)
-            mm(b[2 + ch][:, 0:128], T[rk][:], T.IdH[:], True, True, [rk, "IdH"], ["b%d" % (2 + ch)])
-        own, ok = own_of(t, ch)
-        tt(T["HT" + c][:], own, T.AN[:, cols], A.is_equal, [ok, "AN" + k], ["HT" + c])
-        mm(b[5 + ch][:, 0:128], T["HT" + c][:], T.BO[:], True, True, ["HT" + c, "BO"], ["b%d" % (5 + ch)])
-        tt(T["hb" + c][:], T["HT" + c][:], T.BA[:, cols], A.mult, ["HT" + c, "BA" + k], ["hb" + c])
+        mm(T[bk][:, 0:128], T.nEA[:], T.ab[:, cols], True, False, ["nEA", k], [bk])
+        mm(T[bk][:, 256:384], T.nEA[:], T.ab[:, cols], False, False, ["nEA", k], [bk])
+        mm(T[bk][:, 256:384], T.EB[:], T.ab[:, cols], False, False, ["EB", k], [bk])
 
-    def deeds_list(t, ch):
-        c = str(ch)
-        loc = slice(128 * ch, 128 * ch + 128)
-        own, ok = own_of(t, ch)
-        tt(T["X" + c][:], b[5 + ch][:, 0:128], T.maskP[:], A.min, ["b%d" % (5 + ch), "maskP"], ["X" + c])
-        m = "MA%d" % (t % 2)
-        lst = b[4][:, 8 * ch:8 * ch + 8]
-        mm(lst, T[m][:, loc], T.K1[:], True, False, [m + "c" + c, "K1"], ["b4"])
-        mm(lst, T["X" + c][:], T.K4[:], False, True, ["X" + c, "K4"], ["b4"])
-        tt(T["ownN" + c][:], own, T["hb" + c][:], A.add, [ok, "hb" + c], ["ownN" + c])
+    def prep_list(t, bk, lo, hi):
+        for r in range(16):
+            mm(T[bk][:, lo // 16:hi // 16], T.BigA[:, 15 - r:143 - r], T.ab[:, 256 * t + lo + r:256 * t + hi:16], r == 0, False,
+               ["BigA", "ab%d" % t], [bk])
 
-    def deeds_end(ch):
+    def prep_nh_t(t):
+        lk = "lm%d" % (t % n)
+        mm(T.N[:, 0:256], T.WN[:], T[lk][:], True, False, ["WN", lk], ["N"])
+        mm(T.N[:, 0:256], T.EN[:], T.ab[:, 256 * t:256 * t + 256], False, True, ["EN", "ab%d" % t], ["N"])
+
+    def prep_nh_s(t):
+        k = "NH%d" % (t % 2)
+        act(T[k][:], T.N[:, 0:256], ["N", "cb"], [k], func=F.Identity, bias=T.cb[:])
+
+    def rep(t, who, qs=None):
+        k = "lm%d" % t
+        for q in qs if qs is not None else (REP0 if t == 0 else REP)[who]:
+            out, key = T["lr%d" % t][:, q:4096:16], "lr%d_%d" % (t, q)
+            if who == "v":
+                vcopy(out, T[k][:], [k], [key])
+            elif who == "s":
+                act(out, T[k][:], [k], [key])
+            else:
+                op("p", lambda: g.affine_select(out, T[k][:], [[0, 256]], A.is_ge, 0.0, 0, 0), [k], [key])
+
+    def deeds_turn(t, ch):
+        bk = "T%d" % ch
+        for lo, stop in ((0, False), (128, True)):
+            if t:
+                rk = "R%d%d" % (t, ch)
+                mm(T[bk][:, lo:lo + 128], T[rk][:], T.Id[:], False, stop, [rk, "Id"], [bk])
+            else:
+                mm(T[bk][:, lo:lo + 128], T.Id[:], T.ownH[:, 128 * ch:128 * ch + 128], False, stop, ["ownH", "Id"], [bk])
+
+    def deeds_hit(ch):
         c = str(ch)
-        ts(T["LS" + c][:], b[4][:, 8 * ch:8 * ch + 8], BIAS, A.add, ["b4"], ["LS" + c])
+        ts(T["HT" + c][:], T["T" + c][:, 0:128], 0.0, A.is_equal, ["T" + c], ["HT" + c])
+
+    def deeds_count(ch, bk, lo):
+        mm(T[bk][:, lo:lo + 128], T["HT%d" % ch][:], T.nBO[:], True, True, ["HT%d" % ch, "nBO"], [bk])
+
+    def deeds_gain(ch):
+        c = str(ch)
+        tt(T["hb" + c][:], T["HT" + c][:], T["T" + c][:, 256:384], A.mult, ["HT" + c, "T" + c], ["hb" + c])
+
+    def deeds_own(ch):
+        c = str(ch)
+        tt(T["ownN" + c][:], T["T" + c][:, 128:256], T["hb" + c][:], A.add, ["T" + c, "hb" + c], ["ownN" + c])
+
+    def deeds_list(ch, bk, lo, lb, stop=True):
+        c = str(ch)
+        tt(T["XM" + c][:], T[bk][:, lo:lo + 128], T.maskP[:], A.max, [bk, "maskP"], ["XM" + c])
+        mm(T[lb][:, 8 * ch:8 * ch + 8], T["XM" + c][:], T.nK4[:], False, stop, ["XM" + c, "nK4"], [lb])
+
+    def deeds_end(ch, lb):
+        ts(T["LS%d" % ch][:], T[lb][:, 8 * ch:8 * ch + 8], float(BIAS), A.add, [lb], ["LS%d" % ch])
 
     def scatter_h(t, ch):
         c = str(ch)
         h = "NH%d" % (t % 2)
-        loc = slice(128 * ch, 128 * ch + 128)
-        vcopy(T.HN[:, 0:8192].indirect(T["LS" + c][:, 0:8]), T[h][:, loc], ["LS" + c, h], HK)
+        act(T.HN[:, 0:WIN].indirect(T["LS" + c][:, 0:8]), T[h][:, 128 * ch:128 * ch + 128], ["LS" + c, h], HK, func=F.Silu)
 
     def scatter_w(t, ch):
         c = str(ch)
         l = "lm%d" % (t % n)
-        loc = slice(128 * ch, 128 * ch + 128)
-        vcopy(T.W[:, 0:8192].indirect(T["LS" + c][:, 0:8]), T[l][:, loc], ["LS" + c, l], WK)
+        vcopy(T.W[:, 0:WIN].indirect(T["LS" + c][:, 0:8]), T[l][:, 128 * ch:128 * ch + 128], ["LS" + c, l], WK)
 
     def offs(ch):
         ts(T.off[:, 128 * ch:128 * ch + 128], T["ownN%d" % ch][:], BIAS, A.add, ["ownN%d" % ch], ["off%d" % ch])
+
+    def parts(k, lo, hi):
+        return [k + "a"] if hi < 128 else [k + "b"] if lo else [k + "a", k + "b"]
 
     def gv(t, ch, lo, hi):
         a, z = 128 * ch + lo, 128 * ch + hi
         m, l = "M%d" % ch, "lr%d" % (t % n)
         op("v", lambda: g.vector.tensor_tensor(out=T[m][:, 16 * lo:16 * hi], in0=T.W[:, 0:4096].indirect(T.off[:, a:z]),
                                                in1=T[l][:, 16 * a:16 * z], op=A.max),
-           WK + ["off%d" % ch] + [l + "_%d" % q for q in range(16)], [m + "_%d" % lo])
+           WK + ["off%d" % ch] + [l + "_%d" % q for q in range(16)], parts(m, lo, hi))
 
     def gs(ch, lo, hi):
         a, z = 128 * ch + lo, 128 * ch + hi
-        act(T["H%d" % ch][:, 16 * lo:16 * hi], T.HN[:, 0:4096].indirect(T.off[:, a:z]), HK + ["off%d" % ch], ["H%d_%d" % (ch, lo)])
-
-    MK = {c: ["M%d_0" % c, "M%d_%d" % (c, VS)] for c in (0, 1)}
-    HHK = {c: ["H%d_0" % c, "H%d_%d" % (c, SS)] for c in (0, 1)}
-
-    def gather_whole(t, ch):
-        gv(t, ch, 0, 128)
-        wr[MK[ch][1]] = dict(wr[MK[ch][0]])
-        gs(ch, 0, 128)
-        wr[HHK[ch][1]] = dict(wr[HHK[ch][0]])
+        h = "H%d" % ch
+        act(T[h][:, 16 * lo:16 * hi], T.HN[:, 0:4096].indirect(T.off[:, a:z]), HK + ["off%d" % ch, "gb"], parts(h, lo, hi),
+            func=F.Identity, bias=T.gb[:])
 
     def init(t, ch, p):
-        l, bk = "lm%d" % (t % n), "b%d" % ch
-        mm(b[ch][:, 0:128], T[l][:, 128 * ch:128 * ch + 128], T.nBO[:], True, False, [l, "nBO"], [bk])
-        if p == 0:
-            mm(b[ch][:, 128:384], T["ownN%d" % ch][:], T.HI2[:], False, False, ["ownN%d" % ch, "HI2"], [bk])
-        else:
-            for k in (1, 2):
-                mm(b[ch][:, 128 * k:128 * k + 128], T.HI2[:, 0:128], T["OT%d" % ch][:], False, False, ["HI2", "OT%d" % ch], [bk])
+        l, bk, o = "lm%d" % (t % n), "XY"[p] + str(ch), "ownN%d" % ch
+        mm(T[bk][:, 0:128], T[l][:, 128 * ch:128 * ch + 128], T.nBO[:], True, False, [l, "nBO"], [bk])
+        lo = 128 + 128 * p
+        mm(T[bk][:, lo:384], T[o][:], T.HI[:, 0:384 - lo], False, False, [o, "HI"], [bk])
 
-    def sums(ch):
+    def sums_h(ch, p):
+        bk, h, rh = "XY"[p] + str(ch), "H%d" % ch, "RH%d" % p
         for q in range(16):
-            mm(b[ch][:, q:384:16], T["H%d" % ch][:, q:2048:16], T.RH[:], False, False, HHK[ch] + ["RH"], ["b%d" % ch])
+            mm(T[bk][:, q:384:16], T[h][:, q:2048:16], T[rh][:], False, False, [h + "a", h + "b", rh], [bk])
+
+    def sums_m(ch, p):
+        bk, m = "XY"[p] + str(ch), "M%d" % ch
         for q in range(16):
-            mm(b[ch][:, q:128:16], T["M%d" % ch][:, q:2048:16], T.RM[:], False, q == 15, MK[ch] + ["RM"], ["b%d" % ch])
+            mm(T[bk][:, q:128:16], T[m][:, q:2048:16], T.RM[:], False, q == 15, [m + "a", m + "b", "RM"], [bk])
 
-    def sign(ch):
-        act(T["SG%d" % ch][:], b[ch][:, 0:128], ["b%d" % ch], ["SG%d" % ch], func=F.Sign, bias=-TH)
-
-    def upd(ch, dst):
+    def heirs(ch):
         c = str(ch)
-        tt(T["tt" + c][:], T["SG" + c][:], b[ch][:, 128:256], A.mult, ["SG" + c, "b" + c], ["tt" + c])
-        tt(T[dst][:], b[ch][:, 256:384], T["tt" + c][:], A.add, ["b" + c, "tt" + c], [dst])
-
-    def turn(ch, src):
-        mm(b[2 + ch][:, 0:128], T[src][:], T.IdH[:], True, True, [src, "IdH"], ["b%d" % (2 + ch)])
+        act(T["hT" + c][:], T["X" + c][:, 256:384], ["X" + c], ["hT" + c])
+        act(T["SA" + c][:], T["X" + c][:, 0:128], ["X" + c], ["SA" + c], func=F.Sign, bias=-TH)
+        mm(T["T" + c][:, 384:512], T["hT" + c][:], T.Id[:], True, True, ["hT" + c, "Id"], ["T" + c])
+        mm(T["Y" + c][:, 128:256], T.HI[:, 0:128], T["hT" + c][:], False, False, ["hT" + c, "HI"], ["Y" + c])
+        mm(T["Y" + c][:, 0:128], T.BI[:], T["SA" + c][:], False, False, ["SA" + c, "BI"], ["Y" + c])
 
     def conv(ch):
-        ts(T.off[:, 128 * ch:128 * ch + 128], b[2 + ch][:, 0:128], BIAS, A.add, ["b%d" % (2 + ch)], ["off%d" % ch])
+        ts(T.off[:, 128 * ch:128 * ch + 128], T["T%d" % ch][:, 384:512], BIAS, A.add, ["T%d" % ch], ["off%d" % ch])
 
-    act(T.nBO[:], T.BO[:], ["BO"], ["nBO"], scale=-1.0)
-    act(T.RM[:], T.BO[:, 0:128:16], ["BO"], ["RM"], scale=2.0)
-    act(T.K4[:], T.BO[:, 0:128:16], ["BO"], ["K4"], scale=4096.0)
-    for k in (0, 1):
+    def first(ch):
+        c = str(ch)
+        tt(T["ta" + c][:], T["SA" + c][:], T["X" + c][:, 128:256], A.mult, ["SA" + c, "X" + c], ["ta" + c])
+        mm(T["Y" + c][:, 256:384], T.I32[:], T["ta" + c][:], False, False, ["ta" + c, "I32"], ["Y" + c])
+
+    def sign(ch):
+        act(T["SB%d" % ch][:], T["Y%d" % ch][:, 0:128], ["Y%d" % ch], ["SB%d" % ch], func=F.Sign, bias=FAR - TH)
+
+    def upd_a(ch):
+        c = str(ch)
+        tt(T["tb" + c][:], T["SB" + c][:], T["Y" + c][:, 128:256], A.mult, ["SB" + c, "Y" + c], ["tb" + c])
+
+    def upd_b(ch, dst):
+        c = str(ch)
+        tt(T[dst][:], T["Y" + c][:, 256:384], T["tb" + c][:], A.add, ["Y" + c, "tb" + c], [dst])
+
+    def pass_on(t, ch):
+        sd = "SD%d%d" % (t, ch)
+        upd_b(ch, sd)
+        send(nxt, T["R%d%d" % (t + 1, ch)][:], T[sd][:], "r%d%d" % (t + 1, ch), sd)
+
+    for k in range(4):
         x_heir(k)
-    an_t(0)
-    an_s(0)
-    prep_t(0)
-    prep_s(0)
-    for k in (2, 3, 4):
-        x_heir(k)
-    ts(T.K1[:], T.BO[:, 0:128:16], 1.0, A.mult, ["BO"], ["K1"])
-    indices(1)
-    prep_ma(0)
-    prep_nh(0)
-    for k in (0, 1, 2):
-        x_book(k)
-    rep(0, range(6), "s")
-    x_copy(0)
-    deeds_hit(0, 0)
-    deeds_hit(0, 1)
-    x_heir(5)
-    x_copy(1)
-    x_copy(2)
-    ts(T.HI2[:, 0:128], T.ci[:], T.pf[:], A.is_equal, ["ci", "pf"], ["HI2"], 0.5, A.mult)
-    ts(T.HI2[:, 128:256], T.ci[:], T.pf[:], A.is_equal, ["ci", "pf"], ["HI2"], 0.5, A.mult)
-    deeds_list(0, 0)
-    deeds_list(0, 1)
+    mm(T.L[:, 128:256], T.EB[:], T.EB[:], True, True, ["EB"], ["L"])
+    indices(0)
+    ts(T.ownH[:], T.ownI[:], BIAS, A.subtract, ["ownI"], ["ownH"])
+    act(T.nBO[:], T.L[:, 128:256], ["L"], ["nBO"], scale=-1.0)
+    act(T.nK4[:], T.K4[:], ["K4"], ["nK4"], scale=-1.0)
+    for ch in (0, 1):
+        prep_deeds(0, ch)
+        deeds_turn(0, ch)
+    prep_nh_t(0)
+    prep_nh_s(0)
+    prep_list(0, "L", 0, 256)
+    rep(0, "p")
+    for t in range(1, n):
+        send(T.cores[(rank + t) % n], T["lm%d" % t][:], T.lm0[:], "l%d" % t, "lm0")
+    for ch in (0, 1):
+        deeds_hit(ch)
+    for ch in (0, 1):
+        deeds_gain(ch)
+    for ch in (0, 1):
+        deeds_own(ch)
+    rep(0, "s")
+    for ch in (0, 1):
+        deeds_count(ch, "T1", 128 * ch)
     x_heir(6)
     x_heir(7)
-    rep(0, range(6, 16 - VR0), "s")
-    ts(T.RH[:, 0:8], T.BO[:, 0:128:16], T.l29[:], A.mult, ["BO", "l29"], ["RH"], -1.0, A.mult)
-    ts(T.RH[:, 8:16], T.BO[:, 0:128:16], T.l01[:], A.mult, ["BO", "l01"], ["RH"], -0.5, A.mult)
-    ts(T.RH[:, 16:24], T.BO[:, 0:128:16], T.l01[:], A.mult, ["BO", "l01"], ["RH"], 0.5, A.mult)
-    ts(T.IdH[:], T.ci[:], T.pf[:], A.is_equal, ["ci", "pf"], ["IdH"])
-    offs(0)
-    offs(1)
-    deeds_end(0)
-    deeds_end(1)
-    for k in range(3, 8):
+    for k in (0, 1, 2):
+        x_book(k)
+    for ch in (0, 1):
+        deeds_list(ch, "T1", 128 * ch, "L", ch == 1)
+    for p in (0, 1):
+        ts(T["RH%d" % p][:, 0:8], T.B8[:], T.wN[:], A.mult, ["B8", "wN"], ["RH%da" % p], -1.0, A.mult)
+        ts(T["RH%d" % p][:, 8:16], T.B8[:], T.wh[:], A.mult, ["B8", "wh"], ["RH%db" % p], -0.5, A.mult)
+        ts(T["RH%d" % p][:, 16:24], T.B8[:], T.wh[:], A.mult, ["B8", "wh"], ["RH%d" % p], 1.0 - 0.5 * p, A.mult)
+    x_copy(0)
+    x_copy(1)
+    x_heir(4)
+    x_heir(5)
+    x_copy(2)
+    for ch in (0, 1):
+        deeds_end(ch, "L")
+        offs(ch)
+    rep(0, "v")
+    for k in (3, 4, 5, 6, 7):
         x_book(k)
         x_copy(k)
-    rep(0, range(16 - VR0, 16), "v")
-    scatter_w(0, 0)
-    scatter_h(0, 0)
-    scatter_h(0, 1)
-    scatter_w(0, 1)
-
-    nxt = T.cores[(rank + 1) % n]
-    prv = T.cores[(rank - 1) % n]
-    for t in range(1, R):
-        for ch in range(2):
-            arrive("r%d%d" % (t, ch), "R%d%d" % (t, ch), prv)
+    for ch in (0, 1):
+        scatter_w(0, ch)
+        scatter_h(0, ch)
 
     def out_yo(ch):
+        c = str(ch)
         loc = slice(128 * ch, 128 * ch + 128)
-        ts(T.yof[:, loc], b[2 + ch][:, 0:128], float(BIAS), A.add, ["b%d" % (2 + ch)], ["yof%d" % ch])
-        op("y", lambda: g.sync.dma_start(out=T.yo[:, loc], in_=T.yof[:, loc]), ["yof%d" % ch], [], "dout", 16)
+        upd_b(ch, "OT" + c)
+        mm(T["T" + c][:, 0:128], T["OT" + c][:], T.Id[:], True, True, ["OT" + c, "Id"], ["T" + c])
+        act(T.yof[:, loc], T["T" + c][:, 0:128], ["T" + c], ["yof" + c], bias=float(BIAS))
+        op("y", lambda: g.sync.dma_start(out=T.yo[:, loc], in_=T.yof[:, loc]), ["yof" + c], [], "dout", 16)
 
     for t in range(R):
         last = t == R - 1
-        if t:
-            for ch in (0, 1):
-                deeds_hit(t, ch)
-                deeds_list(t, ch)
-                if ch == 0:
-                    offs(0)
-                deeds_end(ch)
-                scatter_h(t, ch)
-                scatter_w(t, ch)
-        init(t, 0, 0)
-        init(t, 1, 0)
-        if not last:
-            prep_t(t + 1)
-        if t in AK:
-            an_t(AK[t])
-        gather_whole(t, 0)
-        if t:
+        if t + 1 < n:
+            rep(t + 1, "p")
+        gv(t, 0, 0, 128)
+        if t == 0:
+            act(T.HI[:, 0:128], T.Id[:], ["Id"], ["HI"], scale=0.5)
+        gs(0, 0, 128)
+        if t == 0:
+            act(T.BI[:], T.Id[:], ["Id"], ["BI"], scale=FAR)
+            act(T.I32[:], T.Id[:], ["Id"], ["I32"])
+            indices(1)
+        else:
             offs(1)
+        for p in (0, 1):
+            init(t, 0, p)
+            init(t, 1, p)
         if last:
             for k, lane in (("yha", 0), ("yhb", 1)):
-                op("y", lambda: g.sync.dma_start(out=T[k][:], in_=T.HN[lane:128:16, 0:4096]), HK, [k], "d_" + k, 16)
+                op("p", lambda: g.dma_start(out=T[k][:], in_=T.HN[lane:128:16, 0:4096]), HK, ["yhab" if lane else "yha0"], "d_yh", 16)
             op("y", lambda: g.sync.dma_start(out=T.yd[:], in_=T.W[:, 0:4096]), WK, [], "dout", 16)
-        sums(0)
+        sums_h(0, 0)
+        sums_m(0, 0)
+        if not last:
+            prep_nh_t(t + 1)
+            prep_list(t + 1, "L", 0, 128)
         gv(t, 1, 0, VS)
         gs(1, 0, SS)
-        sign(0)
+        heirs(0)
         gs(1, SS, 128)
-        upd(0, "OT0")
-        turn(0, "OT0")
-        init(t, 0, 1)
-        gv(t, 1, VS, 128)
         conv(0)
-        sums(1)
+        first(0)
+        gv(t, 1, VS, 128)
+        if not last:
+            prep_deeds(t + 1, 0)
+        sums_h(1, 0)
+        sums_m(1, 0)
         gv(t, 0, 0, VS)
         gs(0, 0, SS)
-        sign(1)
+        heirs(1)
         gs(0, SS, 128)
-        if last:
-            act(T.yh2[:], T.yha[:], ["yha"], ["yh2"], bias=float(BIAS))
-        upd(1, "OT1")
-        turn(1, "OT1")
         conv(1)
-        init(t, 1, 1)
+        first(1)
         gv(t, 0, VS, 128)
-        sums(0)
-        gather_whole(t, 1)
-        sign(0)
-        sums(1)
         if not last:
-            upd(0, "SD%d0" % t)
-            send(nxt, T["R%d0" % (t + 1)][:], T["SD%d0" % t][:], "r%d0" % (t + 1), "SD%d0" % t)
-            prep_s(t + 1)
-            if t in AK:
-                an_s(AK[t])
-            prep_ma(t + 1)
-            if t == 0:
-                indices(2, "a")
-            sign(1)
-            upd(1, "SD%d1" % t)
-            send(nxt, T["R%d1" % (t + 1)][:], T["SD%d1" % t][:], "r%d1" % (t + 1), "SD%d1" % t)
-            prep_nh(t + 1)
-            if t + 1 < n:
-                rep(t + 1, range(16 - VR, 16), "v")
-                rep(t + 1, range(16 - VR), "s")
-            if t == 0:
-                indices(2, "b")
+            prep_deeds(t + 1, 1)
+        sums_h(0, 1)
+        sums_m(0, 1)
+        if last:
+            act(T.I16[:], T.Id[:], ["Id"], ["I16"], scale=1.0 / 16)
+            mm(T.N[:, 0:256], T.Id[:], T.yha[:], True, False, ["Id", "yhab"], ["N"])
+            mm(T.N[:, 0:256], T.I16[:], T.yhb[:], False, True, ["I16", "yhab"], ["N"])
         else:
-            tt(T.yhf[:], T.yh2[:], T.yhb[:], A.add, ["yh2", "yhb"], ["yhf"])
-            op("y", lambda: g.sync.dma_start(out=T.yh[:], in_=T.yhf[:]), ["yhf"], [], "dout", 16)
-            upd(0, "OT0")
-            turn(0, "OT0")
-            out_yo(0)
+            prep_list(t + 1, "X1", 128, 256)
+        gv(t, 1, 0, VL)
+        gs(1, 0, SL)
+        sign(0)
+        gs(1, SL, 128)
+        upd_a(0)
+        if not last:
+            pass_on(t, 0)
+            gv(t, 1, VL, 128)
+            prep_nh_s(t + 1)
+            sums_h(1, 1)
+            deeds_turn(t + 1, 0)
+            sums_m(1, 1)
+            deeds_hit(0)
+            deeds_count(0, "X0", 384)
+            deeds_gain(0)
             sign(1)
-            upd(1, "OT1")
-            turn(1, "OT1")
+            upd_a(1)
+            deeds_own(0)
+            pass_on(t, 1)
+            deeds_list(0, "X0", 384, "L")
+            offs(0)
+            deeds_end(0, "L")
+            if t + 1 < n:
+                rep(t + 1, "s")
+            scatter_h(t + 1, 0)
+            scatter_w(t + 1, 0)
+            if t + 2 < R:
+                indices(t + 2)
+            deeds_turn(t + 1, 1)
+            deeds_hit(1)
+            deeds_count(1, "X0", 384)
+            deeds_gain(1)
+            deeds_list(1, "X0", 384, "X1")
+            deeds_own(1)
+            deeds_end(1, "X1")
+            scatter_h(t + 1, 1)
+            scatter_w(t + 1, 1)
+        else:
+            gv(t, 1, VL, 128)
+            out_yo(0)
+            act(T.yhf[:], T.N[:, 0:256], ["N"], ["yhf"], bias=-16.0)
+            op("y", lambda: g.sync.dma_start(out=T.yh[:], in_=T.yhf[:]), ["yhf"], [], "dout", 16)
+            sums_h(1, 1)
+            sums_m(1, 1)
+            sign(1)
+            upd_a(1)
             out_yo(1)
 
     g.sync.wait_ge(T.sem.dout, cnt["dout"])

@@ -5,11 +5,11 @@ TH = 136.5 + 2048
 FAR = 256.0
 R = 5
 WIN = 8192
-VS, SS = 96, 80
-VL, SL = 64, 48
-REP0 = {"v": range(0, 7), "s": range(7, 12), "p": range(12, 16)}
-REP = {"s": range(0, 4), "p": range(4, 16)}
-VCOPY = (1, 3, 5, 7)
+SS = 88
+VL = (0, 64, 80, 96, 128)
+REP0 = {"v": range(0, 8), "s": range(8, 12), "p": range(12, 16)}
+REP = {"s": range(0, 5), "p": range(5, 16)}
+VCOPY = (1, 4, 6)
 PIECE = (0, 1536, 2560, 3584, 4096)
 
 SCRATCH = {}
@@ -20,40 +20,41 @@ def _buf(name, cols, dtype, where="sbuf", rows=128):
     SCRATCH[name] = (where, [rows, cols], dtype)
 
 
-for _n, _c in (("pi", 1), ("p15i", 1), ("gi", 8), ("g4i", 8), ("ownI", 256), ("heirI", 512)):
+for _n, _c in (("pi", 1), ("p15i", 1), ("gi", 8), ("g4i", 8), ("ownI", 256)):
     _buf(_n, _c, "int32")
+_buf("heirI", 512, "int32", rows=64)
 _buf("abI", 1280, "int32", rows=24)
-for _n in ("p15", "c8", "wN", "wh", "wh1", "cb", "cb1", "cb2", "cb3", "gb", "e64", "hs", "hb", "e16", "fs", "fb"):
+for _n in ("p15", "c8", "wN", "wh", "wh1", "cb", "cb1", "cb2", "cb3", "gb", "e16", "fs", "fb"):
     _buf(_n, 1, "float32")
-for _n, _c in (("dv", 128), ("ev", 128), ("c15", 128), ("maskP", 128), ("B8", 8), ("K4", 8), ("nK4", 8), ("nBO", 128), ("WN", 128), ("WH", 1024),
-               ("Id", 128), ("HI", 256), ("BI", 128), ("I16", 128), ("RM", 8), ("RH0", 24), ("RH1", 24), ("yha", 256), ("yhb", 256),
-               ("W", WIN), ("M0", 2048), ("M1", 2048), ("H0", 2048), ("H1", 2048), ("HT0", 128), ("HT1", 128), ("XM0", 128), ("XM1", 128),
-               ("SA0", 128), ("SA1", 128), ("SB0", 128), ("SB1", 128), ("lm0", 256), ("lm1", 256), ("lm2", 256), ("lm3", 256),
-               ("lr0", 4096), ("lr1", 4096), ("lr2", 4096), ("lr3", 4096)):
+for _n, _c in (("dv", 128), ("ev", 128), ("c15", 128), ("i3", 3), ("maskP", 128), ("B8", 8), ("nK4", 8), ("nBO", 128), ("WN", 128),
+               ("WH", 1024), ("Id", 128), ("HI", 128), ("BI", 128), ("I16", 128), ("Z", 144), ("RM", 8), ("RH", 24),
+               ("yha", 256), ("yhb", 256), ("W", WIN), ("M0", 2048), ("M1", 2048), ("H0", 2048), ("H1", 2048),
+               ("HT0", 128), ("HT1", 128), ("XM0", 128), ("XM1", 128), ("SA0", 128), ("SA1", 128), ("SB0", 128), ("SB1", 128),
+               ("lm0", 256), ("lm1", 256), ("lm2", 256), ("lm3", 256)):
     _buf(_n, _c, "bfloat16")
 for _n, _c in (("nEA", 128), ("EB", 128), ("EN", 128), ("BigA", 144)):
     _buf(_n, _c, "bfloat16", rows=24)
 _buf("ab", 1280, "float16", rows=24)
-for _n, _c in (("Hs", 512), ("ownH", 256), ("ownN0", 128), ("ownN1", 128), ("hT0", 128), ("hT1", 128), ("OT0", 128), ("OT1", 128)):
+for _n, _c in (("Hs", 512), ("Ih", 128), ("ownH", 256), ("ownN0", 128), ("ownN1", 128), ("hT0", 128), ("hT1", 128), ("OT0", 128), ("OT1", 128)):
     _buf(_n, _c, "float16")
-for _n, _c in (("HN", WIN), ("NH0", 256), ("NH1", 256), ("OH", 3), ("I32", 128), ("hb0", 128), ("hb1", 128), ("ta0", 128), ("ta1", 128),
+for _n, _c in (("HN", WIN), ("NH0", 256), ("NH1", 256), ("OH", 3), ("H32", 128), ("hb0", 128), ("hb1", 128), ("ta0", 128), ("ta1", 128),
                ("tb0", 128), ("tb1", 128), ("yof", 256), ("yhf", 256)):
     _buf(_n, _c, "float32")
 _buf("off", 256, "uint16")
-_buf("LS0", 8, "uint16")
-_buf("LS1", 8, "uint16")
+_buf("LS", 16, "uint16")
 for _t in range(4):
+    _buf("lr%d" % _t, 4096, "bfloat16")
     for _c in range(2):
         _buf("SD%d%d" % (_t, _c), 128, "float16")
         _buf("R%d%d" % (_t + 1, _c), 128, "float16")
         SEMAPHORES.append("r%d%d" % (_t + 1, _c))
 for _t in (1, 2, 3):
     SEMAPHORES.append("l%d" % _t)
-for _n in ("own", "lm", "heir", "ab", "yh", "bk0", "bk1", "bk2", "bk3"):
+for _n in ("own", "lm", "heir", "ab", "ac", "yh", "bk0", "bk1", "bk2", "bk3"):
     SEMAPHORES.append("d_" + _n)
-BANKS = ["X0", "X1", "Y0", "Y1", "T0", "T1", "L", "N"]
+BANKS = ["X0", "X1", "Y0", "Y1", "T0", "T1", "L", "P"]
 for _n in BANKS:
-    _buf(_n, 512, "float32", "psum")
+    _buf(_n, 512, "float16" if _n == "P" else "float32", "psum")
 
 
 def rank_program(g, core, T, topo):
@@ -137,68 +138,68 @@ def rank_program(g, core, T, topo):
     def mm(out, lhsT, rhs, start, stop, reads, writes):
         op("t", lambda: g.tensor.matmul(out=out, lhsT=lhsT, rhs=rhs, start=start, stop=stop), reads, writes)
 
-    def load(q, out, in_, sem, key):
-        op(q, lambda: eng[q].dma_start(out=out, in_=in_), [], [key], sem, 16)
+    def load(out, in_, sem, key):
+        op("y", lambda: g.sync.dma_start(out=out, in_=in_), [], [key], sem, 16)
+
+    def store(out, in_, reads):
+        op("y", lambda: g.sync.dma_start(out=out, in_=in_), reads, [], "dout", 16)
 
     def iota(k, pattern, base, cm):
         small = SCRATCH[k][2] != "int32"
         op("p", lambda: g.iota(T[k][:], pattern, base, cm, allow_small_or_imprecise_dtypes=True) if small
            else g.iota(T[k][:], pattern, base, cm), [], [k])
 
-    def mark(ap, key, pattern, base, value):
-        op("p", lambda: g.affine_select(ap, ap, pattern, A.not_equal, value, base, 1), [key], [key])
+    def mark(ap, key, pattern, base, value, whole):
+        op("p", lambda: g.affine_select(ap, ap, pattern, A.not_equal, value, base, 1), [key, whole], [key])
 
-    load("s", T.heirI[0:64, :], T.heir[:], "d_heir", "heirA")
-    load("y", T.heirI[64:128, :], T.heir[:], "d_heir", "heirI")
-    load("s", T.abI[0:8, :], T.da[:], "d_ab", "abA")
-    load("y", T.abI[8:16, :], T.db[:], "d_ab", "abB")
-    load("s", T.abI[16:24, :], T.db[:], "d_ab", "abI")
-    load("y", T.lm0[:], T.lm[:], "d_lm", "lm0")
-    load("s", T.ownI[:], T.own[:], "d_own", "ownI")
+    def diagonal(k, value):
+        op("p", lambda: g.affine_select(T[k][:], T.Z[:, 0:128], [[-1, 128]], A.not_equal, value, 0, 1), ["Z"], [k])
+
+    def deeds_in(lo, hi, sem, key):
+        for row, src in ((0, T.da), (8, T.db), (16, T.db)):
+            load(T.abI[row:row + 8, lo:hi], src[:, lo:hi], sem, key if row == 16 else key + str(row))
+
+    load(T.heirI[:], T.heir[:], "d_heir", "heirI")
+    load(T.lm0[:], T.lm[:], "d_lm", "lm0")
+    deeds_in(0, 512, "d_ab", "abI")
+    load(T.ownI[:], T.own[:], "d_own", "ownI")
     for k in range(4):
-        lo, hi = PIECE[k], PIECE[k + 1]
-        load("y" if k % 2 == 0 else "s", T.W[:, lo:hi], T.bk[:, lo:hi], "d_bk%d" % k, "Wk%d" % k)
+        load(T.W[:, PIECE[k]:PIECE[k + 1]], T.bk[:, PIECE[k]:PIECE[k + 1]], "d_bk%d" % k, "Wk%d" % k)
+    deeds_in(512, 1280, "d_ac", "acI")
     WK = ["Wk%d" % k for k in range(4)]
     HK = ["HN%d" % k for k in range(8)]
 
     iota("pi", [[0, 1]], 0, 1)
     iota("gi", [[-16, 8]], 0, 1)
-    for k in ("WH", "EN", "BigA", "HI"):
+    iota("i3", [[1, 3]], 0, 0)
+    for k in ("Z", "WH", "EN"):
         zero(k)
-    iota("c15", [[0, 8], [1, 16]], 0, 0)
-    mark(T.WH[:, 0:1024:16], "WH", [[-1, 8], [-8, 8]], -64, 16.0)
-    mark(T.WH[:, 1:1024:16], "WH", [[-1, 8], [-8, 8]], 0, 16.0)
-    mark(T.WH[:, 1:1024:16], "WH", [[-1, 8], [-8, 8]], -64, -256.0)
+    act(T.BigA[:], T.Z[0:24, :], ["Z"], ["BigA"], func=F.Silu)
+    mark(T.WH[:, 0:1024:16], "WH0", [[-1, 8], [-8, 8]], -64, 16.0, "WH")
+    mark(T.WH[:, 1:1024:16], "WH1", [[-1, 8], [-8, 8]], 0, 16.0, "WH")
     iota("ev", [[-1, 8], [0, 16]], 0, 1)
+    mark(T.WH[:, 1:1024:16], "WH1", [[-1, 8], [-8, 8]], -64, -256.0, "WH")
     iota("dv", [[1, 128]], 0, -1)
-    mark(T.EN[:, 0:128:16], "EN", [[-1, 8]], -16, 16.0)
-    mark(T.EN[:, 1:128:16], "EN", [[-1, 8]], -8, 16.0)
-    mark(T.EN[:, 1:128:16], "EN", [[-1, 8]], -16, -256.0)
-    mark(T.BigA[:, 15:128:16], "BigA", [[-1, 8]], 0, 1.0)
+    mark(T.EN[:, 0:128:16], "EN0", [[-1, 8]], -16, 16.0, "EN")
+    mark(T.EN[:, 1:128:16], "EN1", [[-1, 8]], -8, 16.0, "EN")
+    mark(T.BigA[:, 15:128:16], "BigA", [[-1, 8]], 0, 1.0, "BigA")
+    mark(T.EN[:, 1:128:16], "EN1", [[-1, 8]], -16, -256.0, "EN")
+    iota("c15", [[0, 8], [1, 16]], 0, 0)
 
     ts(T.p15i[:], T.pi[:], 15, A.bitwise_and, ["pi"], ["p15i"])
-    ts(T.e64[:], T.pi[:], 64.0, A.is_ge, ["pi"], ["e64"])
+    ts(T.e16[:], T.pi[:], 16.0, A.is_ge, ["pi"], ["e16"])
     ts(T.g4i[:], T.gi[:], 4, A.arith_shift_right, ["gi"], ["g4i"])
     vcopy(T.p15[:], T.p15i[:], ["p15i"], ["p15"])
-    ts(T.e16[:], T.pi[:], 16.0, A.is_ge, ["pi"], ["e16"])
-    ts(T.B8[:], T.g4i[:], 0.0, A.is_equal, ["g4i"], ["B8"])
-    ts(T.OH[:], T.c15[:, 0:3], T.p15[:], A.is_equal, ["c15", "p15"], ["OH"])
+    ts(T.fs[:], T.e16[:], -15.0 / 16, A.mult, ["e16"], ["fs"], 1.0, A.add)
+    ts(T.fb[:], T.e16[:], 3072.0, A.mult, ["e16"], ["fb"], -2048.0, A.add)
+    ts(T.OH[:], T.i3[:], T.p15[:], A.is_equal, ["i3", "p15"], ["OH"])
     ts(T.wN[:], T.p15[:], 8.0, A.is_ge, ["p15"], ["wN"])
+    ts(T.Hs[0:64, :], T.heirI[:], BIAS, A.subtract, ["heirI"], ["Hs0"])
+    act(T.Hs[64:128, :], T.heirI[:], ["heirI"], ["Hs1"], scale=1.0 / 16, bias=1024.0)
+    ts(T.B8[:], T.g4i[:], 0.0, A.is_equal, ["g4i"], ["B8"])
     ts(T.c8[:], T.p15[:], 7.0, A.is_le, ["p15"], ["c8"], 8.0, A.mult)
-    ts(T.maskP[:], T.c15[:], T.p15[:], A.is_equal, ["c15", "p15"], ["maskP"], -1.0, A.mult)
-    for e, s, b in (("e64", "hs", "hb"), ("e16", "fs", "fb")):
-        act(T[s][:], T[e][:], [e], [s], scale=-15.0 / 16, bias=1.0)
-        act(T[b][:], T[e][:], [e], [b], scale=3072.0, bias=-2048.0)
-    act(T.cb1[:], T.wN[:], ["wN"], ["cb1"], scale=16.0)
-    act(T.gb[:], T.wN[:], ["wN"], ["gb"], scale=-272.0)
-    act(T.cb2[:], T.OH[:, 0:1], ["OH", "cb1"], ["cb2"], func=F.Identity, scale=-16384.0, bias=T.cb1[:])
-    act(T.wh1[:], T.OH[:, 1:2], ["OH"], ["wh1"], func=F.Identity, scale=1.0 / 16, bias=T.OH[:, 0:1])
-    act(T.cb3[:], T.OH[:, 1:2], ["OH", "cb2"], ["cb3"], func=F.Identity, scale=16.0 * (2048 + 16384 + 16), bias=T.cb2[:])
-    act(T.wh[:], T.OH[:, 2:3], ["OH", "wh1"], ["wh"], func=F.Identity, scale=-1.0, bias=T.wh1[:])
-    act(T.cb[:], T.OH[:, 2:3], ["OH", "cb3"], ["cb"], func=F.Identity, scale=2064.0, bias=T.cb3[:])
-    act(T.K4[:], T.B8[:], ["B8"], ["K4"], func=F.Silu, scale=4096.0)
-    act(T.RM[:], T.B8[:], ["B8"], ["RM"], scale=2.0)
-    ts(T.Hs[:], T.heirI[:], T.hs[:], A.mult, ["heirI", "hs", "hb"], ["Hs"], T.hb[:], A.add)
+    ts(T.cb1[:], T.wN[:], 16.0, A.mult, ["wN"], ["cb1"])
+    ts(T.wh1[:], T.OH[:, 1:2], 1.0 / 16, A.mult, ["OH"], ["wh1"], T.OH[:, 0:1], A.add)
     ts(T.nEA[:], T.ev[0:24, :], 0.0, A.is_equal, ["ev"], ["nEA"], -1.0, A.mult)
     ts(T.EB[:], T.ev[0:24, :], 8.0, A.is_equal, ["ev"], ["EB"])
     ts(T.Id[:], T.dv[:], 0.0, A.is_equal, ["dv"], ["Id"])
@@ -225,10 +226,10 @@ def rank_program(g, core, T, topo):
         for ch in range(2):
             arrive("r%d%d" % (t, ch), "R%d%d" % (t, ch), prv)
 
-    XB = ("Y0", "Y1", "X0", "X1", "Y0", "Y1", "N", "T0")
+    XB = ("Y0", "Y1", "X0", "X1", "Y0", "Y1", "T1", "T0")
 
     def x_heir(k):
-        mm(T[XB[k]][:], T.WH[:, 128 * k:128 * k + 128], T.Hs[:], True, False, ["WH", "Hs"], [XB[k]])
+        mm(T[XB[k]][:], T.WH[:, 128 * k:128 * k + 128], T.Hs[:], True, False, ["WH0", "WH1", "Hs0", "Hs1"], [XB[k]])
 
     def x_book(k):
         wk = [WK[j] for j in range(4) if PIECE[j] < 512 * k + 512 and PIECE[j + 1] > 512 * k]
@@ -243,13 +244,19 @@ def rank_program(g, core, T, topo):
 
     def indices(t):
         cols = slice(256 * t, 256 * t + 256)
-        ts(T.ab[:, cols], T.abI[:, cols], T.fs[0:24, :], A.mult, ["abI", "fs", "fb"], ["ab%d" % t], T.fb[0:24, :], A.add)
+        act(T.ab[:, cols], T.abI[:, cols], ["abI" if t < 2 else "acI", "fs", "fb"], ["ab%d" % t], func=F.Identity,
+            scale=T.fs[0:24, :], bias=T.fb[0:24, :])
 
-    def prep_deeds(t, ch):
+    def prep_diff(t, ch, bk):
+        cols = slice(256 * t + 128 * ch, 256 * t + 128 * ch + 128)
+        mm(T[bk][:, 0:128], T.nEA[:], T.ab[:, cols], True, False, ["nEA", "ab%d" % t], [bk])
+
+    def prep_deeds(t, ch, apart=False):
         bk, k = "T%d" % ch, "ab%d" % t
         cols = slice(256 * t + 128 * ch, 256 * t + 128 * ch + 128)
-        mm(T[bk][:, 0:128], T.nEA[:], T.ab[:, cols], True, False, ["nEA", k], [bk])
-        mm(T[bk][:, 256:384], T.nEA[:], T.ab[:, cols], False, False, ["nEA", k], [bk])
+        if not apart:
+            prep_diff(t, ch, bk)
+        mm(T[bk][:, 256:384], T.nEA[:], T.ab[:, cols], apart, False, ["nEA", k], [bk])
         mm(T[bk][:, 256:384], T.EB[:], T.ab[:, cols], False, False, ["EB", k], [bk])
 
     def prep_list(t, bk, lo, hi):
@@ -259,16 +266,16 @@ def rank_program(g, core, T, topo):
 
     def prep_nh_t(t):
         lk = "lm%d" % (t % n)
-        mm(T.N[:, 0:256], T.WN[:], T[lk][:], True, False, ["WN", lk], ["N"])
-        mm(T.N[:, 0:256], T.EN[:], T.ab[:, 256 * t:256 * t + 256], False, True, ["EN", "ab%d" % t], ["N"])
+        mm(T.L[:, 256:512], T.WN[:], T[lk][:], True, False, ["WN", lk], ["L"])
+        mm(T.L[:, 256:512], T.EN[:], T.ab[:, 256 * t:256 * t + 256], False, True, ["EN0", "EN1", "ab%d" % t], ["L"])
 
     def prep_nh_s(t):
         k = "NH%d" % (t % 2)
-        act(T[k][:], T.N[:, 0:256], ["N", "cb"], [k], func=F.Identity, bias=T.cb[:])
+        act(T[k][:], T.L[:, 256:512], ["L", "cb"], [k], func=F.Identity, bias=T.cb[:])
 
-    def rep(t, who, qs=None):
+    def rep(t, who, qs):
         k = "lm%d" % t
-        for q in qs if qs is not None else (REP0 if t == 0 else REP)[who]:
+        for q in qs:
             out, key = T["lr%d" % t][:, q:4096:16], "lr%d_%d" % (t, q)
             if who == "v":
                 vcopy(out, T[k][:], [k], [key])
@@ -277,18 +284,17 @@ def rank_program(g, core, T, topo):
             else:
                 op("p", lambda: g.affine_select(out, T[k][:], [[0, 256]], A.is_ge, 0.0, 0, 0), [k], [key])
 
-    def deeds_turn(t, ch):
-        bk = "T%d" % ch
-        for lo, stop in ((0, False), (128, True)):
+    def deeds_turn(t, ch, db=None):
+        for bk, lo, stop in ((db or "T%d" % ch, 0, bool(db)), ("T%d" % ch, 128, True)):
             if t:
                 rk = "R%d%d" % (t, ch)
                 mm(T[bk][:, lo:lo + 128], T[rk][:], T.Id[:], False, stop, [rk, "Id"], [bk])
             else:
                 mm(T[bk][:, lo:lo + 128], T.Id[:], T.ownH[:, 128 * ch:128 * ch + 128], False, stop, ["ownH", "Id"], [bk])
 
-    def deeds_hit(ch):
-        c = str(ch)
-        ts(T["HT" + c][:], T["T" + c][:, 0:128], 0.0, A.is_equal, ["T" + c], ["HT" + c])
+    def deeds_hit(ch, db=None):
+        bk = db or "T%d" % ch
+        ts(T["HT%d" % ch][:], T[bk][:, 0:128], 0.0, A.is_equal, [bk], ["HT%d" % ch])
 
     def deeds_count(ch, bk, lo):
         mm(T[bk][:, lo:lo + 128], T["HT%d" % ch][:], T.nBO[:], True, True, ["HT%d" % ch, "nBO"], [bk])
@@ -306,24 +312,27 @@ def rank_program(g, core, T, topo):
         tt(T["XM" + c][:], T[bk][:, lo:lo + 128], T.maskP[:], A.max, [bk, "maskP"], ["XM" + c])
         mm(T[lb][:, 8 * ch:8 * ch + 8], T["XM" + c][:], T.nK4[:], False, stop, ["XM" + c, "nK4"], [lb])
 
-    def deeds_end(ch, lb):
-        ts(T["LS%d" % ch][:], T[lb][:, 8 * ch:8 * ch + 8], float(BIAS), A.add, [lb], ["LS%d" % ch])
+    def deeds_end(ch, lb, who):
+        cols = slice(8 * ch, 8 * ch + 8)
+        if who == "v":
+            ts(T.LS[:, cols], T[lb][:, cols], float(BIAS), A.add, [lb], ["LS%d" % ch])
+        else:
+            act(T.LS[:, cols], T[lb][:, cols], [lb], ["LS%d" % ch], bias=float(BIAS))
 
-    def scatter_h(t, ch):
-        c = str(ch)
+    def scatter_h(t, lo, hi):
         h = "NH%d" % (t % 2)
-        act(T.HN[:, 0:WIN].indirect(T["LS" + c][:, 0:8]), T[h][:, 128 * ch:128 * ch + 128], ["LS" + c, h], HK, func=F.Silu)
+        act(T.HN[:, 0:WIN].indirect(T.LS[:, 8 * lo:8 * hi]), T[h][:, 128 * lo:128 * hi], ["LS%d" % c for c in range(lo, hi)] + [h], HK,
+            func=F.Silu)
 
-    def scatter_w(t, ch):
-        c = str(ch)
+    def scatter_w(t, lo, hi):
         l = "lm%d" % (t % n)
-        vcopy(T.W[:, 0:WIN].indirect(T["LS" + c][:, 0:8]), T[l][:, 128 * ch:128 * ch + 128], ["LS" + c, l], WK)
+        vcopy(T.W[:, 0:WIN].indirect(T.LS[:, 8 * lo:8 * hi]), T[l][:, 128 * lo:128 * hi], ["LS%d" % c for c in range(lo, hi)] + [l], WK)
 
     def offs(ch):
         ts(T.off[:, 128 * ch:128 * ch + 128], T["ownN%d" % ch][:], BIAS, A.add, ["ownN%d" % ch], ["off%d" % ch])
 
     def parts(k, lo, hi):
-        return [k + "a"] if hi < 128 else [k + "b"] if lo else [k + "a", k + "b"]
+        return [k + "_%d" % j for j in range(lo // 8, hi // 8)]
 
     def gv(t, ch, lo, hi):
         a, z = 128 * ch + lo, 128 * ch + hi
@@ -341,211 +350,237 @@ def rank_program(g, core, T, topo):
     def init(t, ch, p):
         l, bk, o = "lm%d" % (t % n), "XY"[p] + str(ch), "ownN%d" % ch
         mm(T[bk][:, 0:128], T[l][:, 128 * ch:128 * ch + 128], T.nBO[:], True, False, [l, "nBO"], [bk])
-        lo = 128 + 128 * p
-        mm(T[bk][:, lo:384], T[o][:], T.HI[:, 0:384 - lo], False, False, [o, "HI"], [bk])
+        if p == 0:
+            mm(T[bk][:, 256:384], T.Z[:, 0:128], T.Z[:, 0:128], False, False, ["Z"], [bk])
+        mm(T[bk][:, 128 + 128 * p:256 + 128 * p], T[o][:], T.HI[:], False, False, [o, "HI"], [bk])
 
-    def sums_h(ch, p):
-        bk, h, rh = "XY"[p] + str(ch), "H%d" % ch, "RH%d" % p
+    def sums_h(ch, p, lo=0, hi=128, stop=True):
+        bk, h = "XY"[p] + str(ch), "H%d" % ch
+        w = 2 if bk == "Y0" else 3
         for q in range(16):
-            mm(T[bk][:, q:384:16], T[h][:, q:2048:16], T[rh][:], False, False, [h + "a", h + "b", rh], [bk])
+            mm(T[bk][lo:hi, q:128 * w:16], T[h][:, 16 * lo + q:16 * hi:16], T.RH[:, 0:8 * w], False, stop and q == 15,
+               parts(h, lo, hi) + ["RH%d" % k for k in range(3)], [bk])
 
-    def sums_m(ch, p):
+    def sums_m(ch, p, lo=0, hi=128, stop=False):
         bk, m = "XY"[p] + str(ch), "M%d" % ch
         for q in range(16):
-            mm(T[bk][:, q:128:16], T[m][:, q:2048:16], T.RM[:], False, q == 15, [m + "a", m + "b", "RM"], [bk])
+            mm(T[bk][lo:hi, q:128:16], T[m][:, 16 * lo + q:16 * hi:16], T.RM[:], False, stop and q == 15, parts(m, lo, hi) + ["RM"], [bk])
 
     def heirs(ch):
         c = str(ch)
-        act(T["hT" + c][:], T["X" + c][:, 256:384], ["X" + c], ["hT" + c])
+        act(T["hT" + c][:], T["X" + c][:, 256:384], ["X" + c], ["hT" + c], scale=2.0)
         act(T["SA" + c][:], T["X" + c][:, 0:128], ["X" + c], ["SA" + c], func=F.Sign, bias=-TH)
-        mm(T["T" + c][:, 384:512], T["hT" + c][:], T.Id[:], True, True, ["hT" + c, "Id"], ["T" + c])
-        mm(T["Y" + c][:, 128:256], T.HI[:, 0:128], T["hT" + c][:], False, False, ["hT" + c, "HI"], ["Y" + c])
+        op("t", lambda: g.tensor.transpose(T.P[:, 128 * ch:128 * ch + 128], T["hT" + c][:], T.Ih[:]), ["hT" + c, "Ih"], ["P"])
+        mm(T["Y" + c][:, 128:256], T.HI[:], T["hT" + c][:], False, False, ["hT" + c, "HI"], ["Y" + c])
+        if ch == 0:
+            mm(T.Y0[:, 256:384], T.HI[:], T.hT0[:], False, False, ["hT0", "HI"], ["Y0"])
         mm(T["Y" + c][:, 0:128], T.BI[:], T["SA" + c][:], False, False, ["SA" + c, "BI"], ["Y" + c])
 
     def conv(ch):
-        ts(T.off[:, 128 * ch:128 * ch + 128], T["T%d" % ch][:, 384:512], BIAS, A.add, ["T%d" % ch], ["off%d" % ch])
+        ts(T.off[:, 128 * ch:128 * ch + 128], T.P[:, 128 * ch:128 * ch + 128], BIAS, A.add, ["P"], ["off%d" % ch])
 
-    def first(ch):
+    def first_v(ch):
         c = str(ch)
         tt(T["ta" + c][:], T["SA" + c][:], T["X" + c][:, 128:256], A.mult, ["SA" + c, "X" + c], ["ta" + c])
-        mm(T["Y" + c][:, 256:384], T.I32[:], T["ta" + c][:], False, False, ["ta" + c, "I32"], ["Y" + c])
+
+    def first_t(ch):
+        c = str(ch)
+        mm(T["Y" + c][:, 256:384], T.H32[:], T["ta" + c][:], False, False, ["ta" + c, "H32"], ["Y" + c])
 
     def sign(ch):
         act(T["SB%d" % ch][:], T["Y%d" % ch][:, 0:128], ["Y%d" % ch], ["SB%d" % ch], func=F.Sign, bias=FAR - TH)
 
-    def upd_a(ch):
+    def second(ch):
         c = str(ch)
         tt(T["tb" + c][:], T["SB" + c][:], T["Y" + c][:, 128:256], A.mult, ["SB" + c, "Y" + c], ["tb" + c])
 
-    def upd_b(ch, dst):
+    def update(ch, dst):
         c = str(ch)
         tt(T[dst][:], T["Y" + c][:, 256:384], T["tb" + c][:], A.add, ["Y" + c, "tb" + c], [dst])
 
     def pass_on(t, ch):
         sd = "SD%d%d" % (t, ch)
-        upd_b(ch, sd)
+        update(ch, sd)
         send(nxt, T["R%d%d" % (t + 1, ch)][:], T[sd][:], "r%d%d" % (t + 1, ch), sd)
+
+    def store_yo(ch):
+        c = str(ch)
+        loc = slice(128 * ch, 128 * ch + 128)
+        mm(T["T" + c][:, 0:128], T["OT" + c][:], T.Id[:], True, True, ["OT" + c, "Id"], ["T" + c])
+        act(T.yof[:, loc], T["T" + c][:, 0:128], ["T" + c], ["yof" + c], bias=float(BIAS))
+        store(T.yo[:, loc], T.yof[:, loc], ["yof" + c])
 
     for k in range(4):
         x_heir(k)
-    mm(T.L[:, 128:256], T.EB[:], T.EB[:], True, True, ["EB"], ["L"])
+        if k == 1:
+            mm(T.L[:, 128:256], T.EB[:], T.EB[:], True, True, ["EB"], ["L"])
     indices(0)
-    ts(T.ownH[:], T.ownI[:], BIAS, A.subtract, ["ownI"], ["ownH"])
+    act(T.ownH[:], T.ownI[:], ["ownI"], ["ownH"], bias=-float(BIAS))
+    act(T.cb2[:], T.OH[:, 0:1], ["OH", "cb1"], ["cb2"], func=F.Identity, scale=-16384.0, bias=T.cb1[:])
     act(T.nBO[:], T.L[:, 128:256], ["L"], ["nBO"], scale=-1.0)
-    act(T.nK4[:], T.K4[:], ["K4"], ["nK4"], scale=-1.0)
+    act(T.cb3[:], T.OH[:, 1:2], ["OH", "cb2"], ["cb3"], func=F.Identity, scale=16.0 * (2048 + 16384 + 16), bias=T.cb2[:])
+    act(T.nK4[:], T.B8[:], ["B8"], ["nK4"], scale=-4096.0)
+    act(T.cb[:], T.OH[:, 2:3], ["OH", "cb3"], ["cb"], func=F.Identity, scale=2064.0, bias=T.cb3[:])
+    ts(T.wh[:], T.OH[:, 2:3], -1.0, A.mult, ["OH", "wh1"], ["wh"], T.wh1[:], A.add)
+    ts(T.gb[:], T.wN[:], -272.0, A.mult, ["wN"], ["gb"])
+    ts(T.RM[:], T.B8[:], 2.0, A.mult, ["B8"], ["RM"])
     for ch in (0, 1):
         prep_deeds(0, ch)
         deeds_turn(0, ch)
-    prep_nh_t(0)
-    prep_nh_s(0)
-    prep_list(0, "L", 0, 256)
-    rep(0, "p")
     for t in range(1, n):
         send(T.cores[(rank + t) % n], T["lm%d" % t][:], T.lm0[:], "l%d" % t, "lm0")
+        if t == 1:
+            rep(0, "p", REP0["p"])
+            diagonal("HI", 0.5)
+    diagonal("Ih", 1.0)
+    diagonal("BI", FAR)
+    diagonal("H32", 1.0)
+    rep(0, "v", REP0["v"][:3])
+    ts(T.maskP[:], T.c15[:], T.p15[:], A.is_equal, ["c15", "p15"], ["maskP"], -1.0, A.mult)
     for ch in (0, 1):
         deeds_hit(ch)
+    prep_nh_t(0)
+    x_book(0)
+    x_book(1)
     for ch in (0, 1):
         deeds_gain(ch)
+    rep(0, "s", REP0["s"][:2])
+    prep_nh_s(0)
+    x_copy(0)
     for ch in (0, 1):
         deeds_own(ch)
-    rep(0, "s")
+    x_book(2)
     for ch in (0, 1):
         deeds_count(ch, "T1", 128 * ch)
-    x_heir(6)
-    x_heir(7)
-    for k in (0, 1, 2):
-        x_book(k)
+    x_copy(1)
+    x_copy(2)
+    prep_list(0, "L", 0, 256)
+    x_heir(4)
+    x_book(3)
     for ch in (0, 1):
         deeds_list(ch, "T1", 128 * ch, "L", ch == 1)
-    for p in (0, 1):
-        ts(T["RH%d" % p][:, 0:8], T.B8[:], T.wN[:], A.mult, ["B8", "wN"], ["RH%da" % p], -1.0, A.mult)
-        ts(T["RH%d" % p][:, 8:16], T.B8[:], T.wh[:], A.mult, ["B8", "wh"], ["RH%db" % p], -0.5, A.mult)
-        ts(T["RH%d" % p][:, 16:24], T.B8[:], T.wh[:], A.mult, ["B8", "wh"], ["RH%d" % p], 1.0 - 0.5 * p, A.mult)
-    x_copy(0)
-    x_copy(1)
-    x_heir(4)
+    for k, (w, val) in enumerate((("wN", -1.0), ("wh", -0.5), ("wh", 0.5))):
+        ts(T.RH[:, 8 * k:8 * k + 8], T.B8[:], T[w][:], A.mult, ["B8", w], ["RH%d" % k], val, A.mult)
+    indices(1)
+    x_book(4)
     x_heir(5)
-    x_copy(2)
+    x_heir(7)
+    x_heir(6)
+    x_copy(3)
     for ch in (0, 1):
-        deeds_end(ch, "L")
+        deeds_end(ch, "L", "v")
         offs(ch)
-    rep(0, "v")
-    for k in (3, 4, 5, 6, 7):
+    x_copy(4)
+    rep(0, "v", REP0["v"][3:])
+    rep(0, "s", REP0["s"][2:])
+    for k in (5, 6, 7):
         x_book(k)
+    for k in (5, 6, 7):
         x_copy(k)
-    for ch in (0, 1):
-        scatter_w(0, ch)
-        scatter_h(0, ch)
-
-    def out_yo(ch):
-        c = str(ch)
-        loc = slice(128 * ch, 128 * ch + 128)
-        upd_b(ch, "OT" + c)
-        mm(T["T" + c][:, 0:128], T["OT" + c][:], T.Id[:], True, True, ["OT" + c, "Id"], ["T" + c])
-        act(T.yof[:, loc], T["T" + c][:, 0:128], ["T" + c], ["yof" + c], bias=float(BIAS))
-        op("y", lambda: g.sync.dma_start(out=T.yo[:, loc], in_=T.yof[:, loc]), ["yof" + c], [], "dout", 16)
+    scatter_w(0, 0, 2)
+    scatter_h(0, 0, 2)
 
     for t in range(R):
         last = t == R - 1
         if t + 1 < n:
-            rep(t + 1, "p")
+            rep(t + 1, "p", REP["p"])
+        elif not last:
+            diagonal("I16", 1.0 / 16)
         gv(t, 0, 0, 128)
-        if t == 0:
-            act(T.HI[:, 0:128], T.Id[:], ["Id"], ["HI"], scale=0.5)
         gs(0, 0, 128)
-        if t == 0:
-            act(T.BI[:], T.Id[:], ["Id"], ["BI"], scale=FAR)
-            act(T.I32[:], T.Id[:], ["Id"], ["I32"])
-            indices(1)
-        else:
-            offs(1)
         for p in (0, 1):
             init(t, 0, p)
             init(t, 1, p)
         if last:
             for k, lane in (("yha", 0), ("yhb", 1)):
                 op("p", lambda: g.dma_start(out=T[k][:], in_=T.HN[lane:128:16, 0:4096]), HK, ["yhab" if lane else "yha0"], "d_yh", 16)
-            op("y", lambda: g.sync.dma_start(out=T.yd[:], in_=T.W[:, 0:4096]), WK, [], "dout", 16)
-        sums_h(0, 0)
-        sums_m(0, 0)
-        if not last:
+            store(T.yd[:], T.W[:, 0:4096], WK)
+        else:
             prep_nh_t(t + 1)
-            prep_list(t + 1, "L", 0, 128)
-        gv(t, 1, 0, VS)
+        sums_m(0, 0)
+        sums_h(0, 0)
+        gv(t, 1, 0, 128)
         gs(1, 0, SS)
         heirs(0)
         gs(1, SS, 128)
         conv(0)
-        first(0)
-        gv(t, 1, VS, 128)
+        first_v(0)
+        sums_m(1, 0)
+        sums_h(1, 0)
+        first_t(0)
         if not last:
             prep_deeds(t + 1, 0)
-        sums_h(1, 0)
-        sums_m(1, 0)
-        gv(t, 0, 0, VS)
+        else:
+            mm(T.L[:, 0:256], T.Id[:], T.yha[:], True, False, ["Id", "yhab"], ["L"])
+            mm(T.L[:, 0:256], T.I16[:], T.yhb[:], False, True, ["I16", "yhab"], ["L"])
+        gv(t, 0, 0, 128)
         gs(0, 0, SS)
         heirs(1)
         gs(0, SS, 128)
         conv(1)
-        first(1)
-        gv(t, 0, VS, 128)
-        if not last:
-            prep_deeds(t + 1, 1)
-        sums_h(0, 1)
+        first_v(1)
         sums_m(0, 1)
+        sums_h(0, 1)
+        first_t(1)
+        gs(1, 0, 96)
+        gs(1, 96, 128)
+        gv(t, 1, VL[0], VL[1])
+        ts(T.SB0[:], T.Y0[:, 0:128], TH - FAR, A.is_le, ["Y0"], ["SB0"], -2.0, A.mult)
+        gv(t, 1, VL[1], VL[2])
+        second(0)
+        if VL[2] < VL[3]:
+            gv(t, 1, VL[2], VL[3])
         if last:
-            act(T.I16[:], T.Id[:], ["Id"], ["I16"], scale=1.0 / 16)
-            mm(T.N[:, 0:256], T.Id[:], T.yha[:], True, False, ["Id", "yhab"], ["N"])
-            mm(T.N[:, 0:256], T.I16[:], T.yhb[:], False, True, ["I16", "yhab"], ["N"])
+            update(0, "OT0")
         else:
-            prep_list(t + 1, "X1", 128, 256)
-        gv(t, 1, 0, VL)
-        gs(1, 0, SL)
-        sign(0)
-        gs(1, SL, 128)
-        upd_a(0)
-        if not last:
             pass_on(t, 0)
-            gv(t, 1, VL, 128)
-            prep_nh_s(t + 1)
-            sums_h(1, 1)
-            deeds_turn(t + 1, 0)
-            sums_m(1, 1)
-            deeds_hit(0)
-            deeds_count(0, "X0", 384)
-            deeds_gain(0)
+            prep_deeds(t + 1, 1, True)
+        gv(t, 1, VL[3], VL[4])
+        sums_m(1, 1, 0, 64)
+        sums_m(1, 1, 64, 96)
+        sums_h(1, 1, 0, 96)
+        sums_h(1, 1, 96, 128, False)
+        sums_m(1, 1, 96, 128, True)
+        if last:
+            act(T.yhf[:], T.L[:, 0:256], ["L"], ["yhf"], bias=-16.0)
+            store(T.yh[:], T.yhf[:], ["yhf"])
             sign(1)
-            upd_a(1)
-            deeds_own(0)
-            pass_on(t, 1)
-            deeds_list(0, "X0", 384, "L")
-            offs(0)
-            deeds_end(0, "L")
-            if t + 1 < n:
-                rep(t + 1, "s")
-            scatter_h(t + 1, 0)
-            scatter_w(t + 1, 0)
-            if t + 2 < R:
-                indices(t + 2)
-            deeds_turn(t + 1, 1)
-            deeds_hit(1)
-            deeds_count(1, "X0", 384)
-            deeds_gain(1)
-            deeds_list(1, "X0", 384, "X1")
-            deeds_own(1)
-            deeds_end(1, "X1")
-            scatter_h(t + 1, 1)
-            scatter_w(t + 1, 1)
-        else:
-            gv(t, 1, VL, 128)
-            out_yo(0)
-            act(T.yhf[:], T.N[:, 0:256], ["N"], ["yhf"], bias=-16.0)
-            op("y", lambda: g.sync.dma_start(out=T.yh[:], in_=T.yhf[:]), ["yhf"], [], "dout", 16)
-            sums_h(1, 1)
-            sums_m(1, 1)
-            sign(1)
-            upd_a(1)
-            out_yo(1)
+            store_yo(0)
+            second(1)
+            update(1, "OT1")
+            store_yo(1)
+            break
+        prep_nh_s(t + 1)
+        prep_list(t + 1, "L", 0, 128)
+        deeds_turn(t + 1, 0)
+        sign(1)
+        second(1)
+        pass_on(t, 1)
+        if t + 2 < R:
+            indices(t + 2)
+        if t + 1 < n:
+            rep(t + 1, "s", REP["s"])
+        deeds_hit(0)
+        deeds_count(0, "X0", 384)
+        deeds_gain(0)
+        deeds_list(0, "X0", 384, "L")
+        deeds_own(0)
+        deeds_end(0, "L", "s")
+        offs(0)
+        scatter_w(t + 1, 0, 1)
+        scatter_h(t + 1, 0, 1)
+        prep_list(t + 1, "X1", 128, 256)
+        prep_diff(t + 1, 1, "L")
+        deeds_turn(t + 1, 1, "L")
+        deeds_hit(1, "L")
+        deeds_count(1, "X0", 384)
+        deeds_list(1, "X0", 384, "X1")
+        deeds_gain(1)
+        deeds_end(1, "X1", "s")
+        deeds_own(1)
+        scatter_h(t + 1, 1, 2)
+        scatter_w(t + 1, 1, 2)
+        offs(1)
 
     g.sync.wait_ge(T.sem.dout, cnt["dout"])
     wait("p", {s: c for s, c in cnt.items() if s != "dout"})

@@ -1,56 +1,59 @@
 from concourse.mybir import AluOpType as A, ActivationFunctionType as F
 
 BIAS = 2048
-TH = 136.5 + 2048
+TH = 136.5 + 4096
 FAR = 256.0
 R = 5
-WIN = 8192
+WIN = 6144
 SS = 88
-VL = (0, 64, 80, 96, 128)
-REP0 = {"v": range(0, 8), "s": range(8, 12), "p": range(12, 16)}
-REP = {"s": range(0, 5), "p": range(5, 16)}
 VCOPY = (1, 4, 6)
 PIECE = (0, 1536, 2560, 3584, 4096)
+OWN, LIST = (0, 144), (128, 136)
 
 SCRATCH = {}
-SEMAPHORES = ["v", "s", "t", "p", "loc", "dout"]
+SEMAPHORES = ["v", "s", "t", "p", "loc", "dout", "pk"]
 
 
 def _buf(name, cols, dtype, where="sbuf", rows=128):
     SCRATCH[name] = (where, [rows, cols], dtype)
 
 
-for _n, _c in (("pi", 1), ("p15i", 1), ("gi", 8), ("g4i", 8), ("ownI", 256)):
+for _n, _c in (("pi", 1), ("p15i", 1), ("gi", 8), ("g4i", 8), ("ownI", 256), ("PK", 128), ("PR", 128)):
     _buf(_n, _c, "int32")
 _buf("heirI", 512, "int32", rows=64)
-_buf("abI", 1280, "int32", rows=24)
-for _n in ("p15", "c8", "wN", "wh", "wh1", "cb", "cb1", "cb2", "cb3", "gb", "e16", "fs", "fb"):
+_buf("abI", 1280, "int32", rows=32)
+for _n in ("p15", "c8", "wN", "wh", "wh1", "cb", "cb1", "cb2", "cb3", "gb", "e24", "fs", "fb"):
     _buf(_n, 1, "float32")
-for _n, _c in (("dv", 128), ("ev", 128), ("c15", 128), ("i3", 3), ("maskP", 128), ("B8", 8), ("nK4", 8), ("nBO", 128), ("WN", 128),
-               ("WH", 1024), ("Id", 128), ("HI", 128), ("BI", 128), ("I16", 128), ("Z", 144), ("RM", 8), ("RH", 24),
-               ("yha", 256), ("yhb", 256), ("W", WIN), ("M0", 2048), ("M1", 2048), ("H0", 2048), ("H1", 2048),
-               ("HT0", 128), ("HT1", 128), ("XM0", 128), ("XM1", 128), ("SA0", 128), ("SA1", 128), ("SB0", 128), ("SB1", 128),
-               ("lm0", 256), ("lm1", 256), ("lm2", 256), ("lm3", 256)):
+for _n, _c in (("dv", 128), ("i3", 3), ("nB8", 8), ("U8", 8), ("WN", 128), ("WH", 1024), ("Id", 128), ("HI", 128), ("BI", 128), ("I16", 128),
+               ("Z", 128), ("RM", 8), ("RH", 24), ("yha", 256), ("yhb", 256), ("W", WIN), ("M0", 2048), ("M1", 2048),
+               ("H0", 2048), ("H1", 2048), ("HT0", 128), ("HT1", 128), ("SA0", 128), ("SA1", 128), ("SB0", 128), ("SB1", 128)):
     _buf(_n, _c, "bfloat16")
-for _n, _c in (("nEA", 128), ("EB", 128), ("EN", 128), ("BigA", 144)):
-    _buf(_n, _c, "bfloat16", rows=24)
-_buf("ab", 1280, "float16", rows=24)
-for _n, _c in (("Hs", 512), ("Ih", 128), ("ownH", 256), ("ownN0", 128), ("ownN1", 128), ("hT0", 128), ("hT1", 128), ("OT0", 128), ("OT1", 128)):
+_buf("EN", 128, "bfloat16", rows=32)
+for _n in ("ev", "E0", "E1", "nE0", "nE1", "C2"):
+    _buf(_n, 128, "bfloat16", rows=16)
+_buf("ab", 1280, "float16", rows=32)
+_buf("aT", 1280, "float16", rows=16)
+_buf("Ls", 512, "float16", rows=16)
+for _n, _c in (("Hs", 512), ("Ih", 128), ("ownH", 256), ("hT0", 128), ("hT1", 128), ("SD0", 128), ("SD1", 128)):
     _buf(_n, _c, "float16")
-for _n, _c in (("HN", WIN), ("NH0", 256), ("NH1", 256), ("OH", 3), ("H32", 128), ("hb0", 128), ("hb1", 128), ("ta0", 128), ("ta1", 128),
-               ("tb0", 128), ("tb1", 128), ("yof", 256), ("yhf", 256)):
+for _n, _c in (("HN", WIN), ("NH0", 256), ("NH1", 256), ("OH", 3), ("I32", 128), ("nI32", 128), ("D", 16),
+               ("hb0", 128), ("hb1", 128), ("ta0", 128), ("ta1", 128), ("tb0", 128), ("tb1", 128), ("yof", 256), ("yhf", 256)):
     _buf(_n, _c, "float32")
 _buf("off", 256, "uint16")
-_buf("LS", 16, "uint16")
+for _t in range(5):
+    _buf("OF%d" % _t, 272, "uint16")
+    _buf("OW%d" % _t, 256, "float16")
+    if _t:
+        _buf("SF%d" % _t, 272, "uint16")
+        _buf("SW%d" % _t, 256, "float16")
+        SEMAPHORES.extend("%s%d%d" % (_k, _t, _c) for _k in "dfw" for _c in (0, 1))
 for _t in range(4):
+    _buf("lm%d" % _t, 256, "bfloat16")
     _buf("lr%d" % _t, 4096, "bfloat16")
-    for _c in range(2):
-        _buf("SD%d%d" % (_t, _c), 128, "float16")
-        _buf("R%d%d" % (_t + 1, _c), 128, "float16")
-        SEMAPHORES.append("r%d%d" % (_t + 1, _c))
-for _t in (1, 2, 3):
-    SEMAPHORES.append("l%d" % _t)
-for _n in ("own", "lm", "heir", "ab", "ac", "yh", "bk0", "bk1", "bk2", "bk3"):
+    SEMAPHORES.extend(["ra%d" % _t, "rb%d" % _t])
+    if _t:
+        SEMAPHORES.append("l%d" % _t)
+for _n in ("own0", "own1", "lm", "heir", "ab", "ac", "ad", "pk", "yh", "bk0", "bk1", "bk2", "bk3"):
     SEMAPHORES.append("d_" + _n)
 BANKS = ["X0", "X1", "Y0", "Y1", "T0", "T1", "L", "P"]
 for _n in BANKS:
@@ -129,8 +132,8 @@ def rank_program(g, core, T, topo):
     def vcopy(out, in_, reads, writes):
         op("v", lambda: g.vector.tensor_copy(out=out, in_=in_), reads, writes)
 
-    def zero(k):
-        op("v", lambda: g.vector.memset(T[k][:], 0.0), [], [k])
+    def fill(k, value):
+        op("v", lambda: g.vector.memset(T[k][:], value), [], [k])
 
     def act(out, in_, reads, writes, func=F.Copy, **kw):
         op("s", lambda: g.scalar.activation(out=out, in_=in_, func=func, **kw), reads, writes)
@@ -138,11 +141,12 @@ def rank_program(g, core, T, topo):
     def mm(out, lhsT, rhs, start, stop, reads, writes):
         op("t", lambda: g.tensor.matmul(out=out, lhsT=lhsT, rhs=rhs, start=start, stop=stop), reads, writes)
 
-    def load(out, in_, sem, key):
-        op("y", lambda: g.sync.dma_start(out=out, in_=in_), [], [key], sem, 16)
+    def dmas(pairs, sem, key, reads=()):
+        for k, (out, in_) in enumerate(pairs):
+            op("y", lambda: g.sync.dma_start(out=out, in_=in_), reads, [key if k == len(pairs) - 1 else key + "." + str(k)], sem, 16)
 
-    def store(out, in_, reads):
-        op("y", lambda: g.sync.dma_start(out=out, in_=in_), reads, [], "dout", 16)
+    def store(q, out, in_, reads):
+        op(q, lambda: eng[q].dma_start(out=out, in_=in_), reads, [], "dout", 16)
 
     def iota(k, pattern, base, cm):
         small = SCRATCH[k][2] != "int32"
@@ -153,57 +157,7 @@ def rank_program(g, core, T, topo):
         op("p", lambda: g.affine_select(ap, ap, pattern, A.not_equal, value, base, 1), [key, whole], [key])
 
     def diagonal(k, value):
-        op("p", lambda: g.affine_select(T[k][:], T.Z[:, 0:128], [[-1, 128]], A.not_equal, value, 0, 1), ["Z"], [k])
-
-    def deeds_in(lo, hi, sem, key):
-        for row, src in ((0, T.da), (8, T.db), (16, T.db)):
-            load(T.abI[row:row + 8, lo:hi], src[:, lo:hi], sem, key if row == 16 else key + str(row))
-
-    load(T.heirI[:], T.heir[:], "d_heir", "heirI")
-    load(T.lm0[:], T.lm[:], "d_lm", "lm0")
-    deeds_in(0, 512, "d_ab", "abI")
-    load(T.ownI[:], T.own[:], "d_own", "ownI")
-    for k in range(4):
-        load(T.W[:, PIECE[k]:PIECE[k + 1]], T.bk[:, PIECE[k]:PIECE[k + 1]], "d_bk%d" % k, "Wk%d" % k)
-    deeds_in(512, 1280, "d_ac", "acI")
-    WK = ["Wk%d" % k for k in range(4)]
-    HK = ["HN%d" % k for k in range(8)]
-
-    iota("pi", [[0, 1]], 0, 1)
-    iota("gi", [[-16, 8]], 0, 1)
-    iota("i3", [[1, 3]], 0, 0)
-    for k in ("Z", "WH", "EN"):
-        zero(k)
-    act(T.BigA[:], T.Z[0:24, :], ["Z"], ["BigA"], func=F.Silu)
-    mark(T.WH[:, 0:1024:16], "WH0", [[-1, 8], [-8, 8]], -64, 16.0, "WH")
-    mark(T.WH[:, 1:1024:16], "WH1", [[-1, 8], [-8, 8]], 0, 16.0, "WH")
-    iota("ev", [[-1, 8], [0, 16]], 0, 1)
-    mark(T.WH[:, 1:1024:16], "WH1", [[-1, 8], [-8, 8]], -64, -256.0, "WH")
-    iota("dv", [[1, 128]], 0, -1)
-    mark(T.EN[:, 0:128:16], "EN0", [[-1, 8]], -16, 16.0, "EN")
-    mark(T.EN[:, 1:128:16], "EN1", [[-1, 8]], -8, 16.0, "EN")
-    mark(T.BigA[:, 15:128:16], "BigA", [[-1, 8]], 0, 1.0, "BigA")
-    mark(T.EN[:, 1:128:16], "EN1", [[-1, 8]], -16, -256.0, "EN")
-    iota("c15", [[0, 8], [1, 16]], 0, 0)
-
-    ts(T.p15i[:], T.pi[:], 15, A.bitwise_and, ["pi"], ["p15i"])
-    ts(T.e16[:], T.pi[:], 16.0, A.is_ge, ["pi"], ["e16"])
-    ts(T.g4i[:], T.gi[:], 4, A.arith_shift_right, ["gi"], ["g4i"])
-    vcopy(T.p15[:], T.p15i[:], ["p15i"], ["p15"])
-    ts(T.fs[:], T.e16[:], -15.0 / 16, A.mult, ["e16"], ["fs"], 1.0, A.add)
-    ts(T.fb[:], T.e16[:], 3072.0, A.mult, ["e16"], ["fb"], -2048.0, A.add)
-    ts(T.OH[:], T.i3[:], T.p15[:], A.is_equal, ["i3", "p15"], ["OH"])
-    ts(T.wN[:], T.p15[:], 8.0, A.is_ge, ["p15"], ["wN"])
-    ts(T.Hs[0:64, :], T.heirI[:], BIAS, A.subtract, ["heirI"], ["Hs0"])
-    act(T.Hs[64:128, :], T.heirI[:], ["heirI"], ["Hs1"], scale=1.0 / 16, bias=1024.0)
-    ts(T.B8[:], T.g4i[:], 0.0, A.is_equal, ["g4i"], ["B8"])
-    ts(T.c8[:], T.p15[:], 7.0, A.is_le, ["p15"], ["c8"], 8.0, A.mult)
-    ts(T.cb1[:], T.wN[:], 16.0, A.mult, ["wN"], ["cb1"])
-    ts(T.wh1[:], T.OH[:, 1:2], 1.0 / 16, A.mult, ["OH"], ["wh1"], T.OH[:, 0:1], A.add)
-    ts(T.nEA[:], T.ev[0:24, :], 0.0, A.is_equal, ["ev"], ["nEA"], -1.0, A.mult)
-    ts(T.EB[:], T.ev[0:24, :], 8.0, A.is_equal, ["ev"], ["EB"])
-    ts(T.Id[:], T.dv[:], 0.0, A.is_equal, ["dv"], ["Id"])
-    ts(T.WN[:], T.dv[:], T.c8[:], A.is_equal, ["dv", "c8"], ["WN"])
+        op("p", lambda: g.affine_select(T[k][:], T.Z[:], [[-1, 128]], A.not_equal, value, 0, 1), ["Z"], [k])
 
     def send(dst, out, in_, sem, key):
         wait("p", deps_of("p", [key], []))
@@ -220,49 +174,135 @@ def rank_program(g, core, T, topo):
 
     nxt = T.cores[(rank + 1) % n]
     prv = T.cores[(rank - 1) % n]
+    arrive("pk", "PR", nxt)
     for t in range(1, n):
         arrive("l%d" % t, "lm%d" % t, T.cores[(rank - t) % n])
     for t in range(1, R):
-        for ch in range(2):
-            arrive("r%d%d" % (t, ch), "R%d%d" % (t, ch), prv)
+        for ch in (0, 1):
+            for k in "dfw":
+                arrive("%s%d%d" % (k, t, ch), "%s%d%d" % (k, t, ch), prv)
 
-    XB = ("Y0", "Y1", "X0", "X1", "Y0", "Y1", "T1", "T0")
+    def sec(ch):
+        return slice(128 * ch, 128 * ch + 128)
+
+    def book_in(k):
+        dmas([(T.W[:, PIECE[k]:PIECE[k + 1]], T.bk[:, PIECE[k]:PIECE[k + 1]])], "d_bk%d" % k, "Wk%d" % k)
+
+    def own_in(ch):
+        dmas([(T.ownI[:, 128 * ch + 16 * k:128 * ch + 16 * k + 16], T.own[16 * k:16 * k + 16, sec(ch)]) for k in range(8)],
+             "d_own%d" % ch, "ownI%d" % ch)
+
+    def repeat(t, src, chunks, reads):
+        lr = T["lr%d" % t]
+        dmas([(lr[:, 2048 * ch + 128 * q:2048 * ch + 128 * q + 128], src[:, sec(ch)]) for ch in chunks for q in range(4)],
+             "ra%d" % t, "lr%da" % t, reads)
+        dmas([(lr[:, 2048 * ch + 512 * k:2048 * ch + 512 * k + 512], lr[:, 2048 * ch:2048 * ch + 512]) for ch in chunks for k in (1, 2, 3)],
+             "rb%d" % t, "lr%d1" % t, ["lr%da" % t])
+        if 0 in chunks:
+            wr["lr%d0" % t] = dict(wr["lr%d1" % t])
+
+    dmas([(T.heirI[:], T.heir[:])], "d_heir", "heirI")
+    dmas([(T.lm0[:], T.lm[:])], "d_lm", "lm0")
+    dmas([(T.abI[8 * k:8 * k + 8, 0:256], src[:, 0:256]) for k, src in enumerate((T.da, T.db, T.db, T.db))], "d_ab", "abI")
+    book_in(0)
+    dmas([(T.PK[:, 0:64], T.da[:, 256:1280]), (T.PK[:, 64:128], T.db[:, 256:1280])], "d_pk", "PK")
+    book_in(1)
+    own_in(0)
+    book_in(2)
+    book_in(3)
+    own_in(1)
+    dmas([(T.abI[16:24, 256:1280], T.db[:, 256:1280]), (T.abI[24:32, 256:1280], T.db[:, 256:1280])], "d_ac", "acI")
+    repeat(0, T.lm, (1,), [])
+    dmas([(T.abI[0:8, 256:1280], T.PR[:, 0:64]), (T.abI[8:16, 256:1280], T.PR[:, 64:128])], "d_ad", "adI", ["PR"])
+    WK = ["Wk%d" % k for k in range(4)]
+    HK = ["HN%d" % k for k in range(8)]
+
+    iota("pi", [[0, 1]], 0, 1)
+    iota("gi", [[-16, 8]], 0, 1)
+    iota("i3", [[1, 3]], 0, 0)
+    for k, val in (("Z", 0.0), ("WH", 0.0), ("C2", float(BIAS))):
+        fill(k, val)
+    act(T.EN[:], T.Z[0:32, :], ["Z"], ["EN"], func=F.Silu)
+    mark(T.WH[:, 0:1024:16], "WH0", [[-1, 8], [-8, 8]], -64, 16.0, "WH")
+    mark(T.WH[:, 1:1024:16], "WH1", [[-1, 8], [-8, 8]], 0, 16.0, "WH")
+    iota("dv", [[1, 128]], 0, -1)
+    mark(T.WH[:, 1:1024:16], "WH1", [[-1, 8], [-8, 8]], -64, -256.0, "WH")
+    iota("ev", [[0, 16], [-1, 8]], 0, 1)
+    mark(T.EN[:, 0:128:16], "EN0", [[-1, 8]], -24, 16.0, "EN")
+    mark(T.EN[:, 1:128:16], "EN1", [[-1, 8]], -16, 16.0, "EN")
+    iota("D", [[1, 16]], 4096, 16)
+    mark(T.EN[:, 1:128:16], "EN1", [[-1, 8]], -24, -256.0, "EN")
+    diagonal("I32", 1.0)
+
+    ts(T.p15i[:], T.pi[:], 15, A.bitwise_and, ["pi"], ["p15i"])
+    ts(T.e24[:], T.pi[:], 24.0, A.is_ge, ["pi"], ["e24"])
+    ts(T.g4i[:], T.gi[:], 4, A.arith_shift_right, ["gi"], ["g4i"])
+    vcopy(T.p15[:], T.p15i[:], ["p15i"], ["p15"])
+    ts(T.fs[:], T.e24[:], -15.0 / 16, A.mult, ["e24"], ["fs"], 1.0, A.add)
+    ts(T.fb[:], T.e24[:], 3072.0, A.mult, ["e24"], ["fb"], -2048.0, A.add)
+    ts(T.OH[:], T.i3[:], T.p15[:], A.is_equal, ["i3", "p15"], ["OH"])
+    ts(T.wN[:], T.p15[:], 8.0, A.is_ge, ["p15"], ["wN"])
+    ts(T.Hs[0:64, :], T.heirI[:], BIAS, A.subtract, ["heirI"], ["Hs0"])
+    act(T.Hs[64:128, :], T.heirI[:], ["heirI"], ["Hs1"], scale=1.0 / 16, bias=1024.0)
+    ts(T.Id[:], T.dv[:], 0.0, A.is_equal, ["dv"], ["Id"])
+    ts(T.nB8[:], T.g4i[:], 0.0, A.is_equal, ["g4i"], ["nB8"], -1.0, A.mult)
+    ts(T.c8[:], T.p15[:], 7.0, A.is_le, ["p15"], ["c8"], 8.0, A.mult)
+    ts(T.cb1[:], T.wN[:], 16.0, A.mult, ["wN"], ["cb1"])
+    ts(T.WN[:], T.dv[:], T.c8[:], A.is_equal, ["dv", "c8"], ["WN"])
+    for ch in (0, 1):
+        ts(T["E%d" % ch][:], T.ev[:], 8.0 * ch, A.is_equal, ["ev"], ["E%d" % ch])
+        ts(T["nE%d" % ch][:], T.ev[:], 8.0 * ch, A.is_equal, ["ev"], ["nE%d" % ch], -1.0, A.mult)
+    ts(T.wh1[:], T.OH[:, 1:2], 1.0 / 16, A.mult, ["OH"], ["wh1"], T.OH[:, 0:1], A.add)
+
+    XB = ("Y0", "Y1", "X0", "X1")
 
     def x_heir(k):
-        mm(T[XB[k]][:], T.WH[:, 128 * k:128 * k + 128], T.Hs[:], True, False, ["WH0", "WH1", "Hs0", "Hs1"], [XB[k]])
+        mm(T[XB[k % 4]][:], T.WH[:, 128 * k:128 * k + 128], T.Hs[:], True, False, ["WH0", "WH1", "Hs0", "Hs1"], [XB[k % 4]])
 
     def x_book(k):
         wk = [WK[j] for j in range(4) if PIECE[j] < 512 * k + 512 and PIECE[j + 1] > 512 * k]
-        mm(T[XB[k]][:], T.WN[:], T.W[:, 512 * k:512 * k + 512], False, True, ["WN"] + wk, [XB[k]])
+        mm(T[XB[k % 4]][:], T.WN[:], T.W[:, 512 * k:512 * k + 512], False, True, ["WN"] + wk, [XB[k % 4]])
 
     def x_copy(k):
-        bk = XB[k]
+        bk = XB[k % 4]
         if k in VCOPY:
             ts(T.HN[:, 512 * k:512 * k + 512], T[bk][:], T.cb[:], A.add, [bk, "cb"], ["HN%d" % k])
         else:
             act(T.HN[:, 512 * k:512 * k + 512], T[bk][:], [bk, "cb"], ["HN%d" % k], func=F.Identity, bias=T.cb[:])
 
+    def double(k):
+        w = 64 * 2 ** k
+        if k < 2:
+            vcopy(T.lr0[:, sec(k)], T.lm0[:, 0:128], ["lm0"], ["lr0.%d" % k])
+        else:
+            vcopy(T.lr0[:, w:2 * w], T.lr0[:, 0:w], ["lr0.%d" % j for j in range(k)], ["lr00" if k == 4 else "lr0.%d" % k])
+
     def indices(t):
         cols = slice(256 * t, 256 * t + 256)
-        act(T.ab[:, cols], T.abI[:, cols], ["abI" if t < 2 else "acI", "fs", "fb"], ["ab%d" % t], func=F.Identity,
-            scale=T.fs[0:24, :], bias=T.fb[0:24, :])
+        if t:
+            ts(T.ab[:, cols], T.abI[:, cols], T.fs[0:32, :], A.mult, ["acI", "adI", "fs", "fb"], ["ab%d" % t], T.fb[0:32, :], A.add)
+        else:
+            act(T.ab[:, cols], T.abI[:, cols], ["abI", "fs", "fb"], ["ab0"], func=F.Identity, scale=T.fs[0:32, :], bias=T.fb[0:32, :])
 
-    def prep_diff(t, ch, bk):
-        cols = slice(256 * t + 128 * ch, 256 * t + 128 * ch + 128)
-        mm(T[bk][:, 0:128], T.nEA[:], T.ab[:, cols], True, False, ["nEA", "ab%d" % t], [bk])
-
-    def prep_deeds(t, ch, apart=False):
-        bk, k = "T%d" % ch, "ab%d" % t
-        cols = slice(256 * t + 128 * ch, 256 * t + 128 * ch + 128)
-        if not apart:
-            prep_diff(t, ch, bk)
-        mm(T[bk][:, 256:384], T.nEA[:], T.ab[:, cols], apart, False, ["nEA", k], [bk])
-        mm(T[bk][:, 256:384], T.EB[:], T.ab[:, cols], False, False, ["EB", k], [bk])
-
-    def prep_list(t, bk, lo, hi):
+    def small_t(t, bk):
         for r in range(16):
-            mm(T[bk][:, lo // 16:hi // 16], T.BigA[:, 15 - r:143 - r], T.ab[:, 256 * t + lo + r:256 * t + hi:16], r == 0, False,
-               ["BigA", "ab%d" % t], [bk])
+            mm(T[bk][0:16, r:256:16], T.ab[:, 256 * t + r:256 * t + 256:16], T.Id[0:32, 0:16], r == 0, r == 15, ["ab%d" % t, "Id"], [bk])
+
+    def small_out(t, bk):
+        if t < 2:
+            act(T.aT[:, 256 * t:256 * t + 256], T[bk][0:16, 0:256], [bk], ["aT%d" % t])
+        else:
+            vcopy(T.aT[:, 256 * t:256 * t + 256], T[bk][0:16, 0:256], [bk], ["aT%d" % t])
+
+    def sum_t(t, bk):
+        for r in range(16):
+            mm(T[bk][0:16, 256 + r:384:16], T["lm%d" % t][:, r:256:16], T.nB8[:], r == 0, r == 15, ["lm%d" % t, "nB8"], [bk])
+
+    def sum_out(t, bk):
+        if t:
+            ts(T.Ls[:, sec(t)], T[bk][0:16, 256:384], float(BIAS), A.add, [bk], ["Ls%d" % t])
+        else:
+            act(T.Ls[:, sec(t)], T[bk][0:16, 256:384], [bk], ["Ls%d" % t], bias=float(BIAS))
 
     def prep_nh_t(t):
         lk = "lm%d" % (t % n)
@@ -273,269 +313,278 @@ def rank_program(g, core, T, topo):
         k = "NH%d" % (t % 2)
         act(T[k][:], T.L[:, 256:512], ["L", "cb"], [k], func=F.Identity, bias=T.cb[:])
 
-    def rep(t, who, qs):
-        k = "lm%d" % t
-        for q in qs:
-            out, key = T["lr%d" % t][:, q:4096:16], "lr%d_%d" % (t, q)
-            if who == "v":
-                vcopy(out, T[k][:], [k], [key])
-            elif who == "s":
-                act(out, T[k][:], [k], [key])
-            else:
-                op("p", lambda: g.affine_select(out, T[k][:], [[0, 256]], A.is_ge, 0.0, 0, 0), [k], [key])
+    def gain_t(t, ch, stop):
+        c, k = str(ch), "aT%d" % t
+        mm(T["T" + c][:, 256:384], T["E" + c][:], T.aT[:, 256 * t + 128:256 * t + 256], False, False, ["E" + c, k], ["T" + c])
+        mm(T["T" + c][:, 256:384], T["nE" + c][:], T.aT[:, 256 * t:256 * t + 128], False, stop, ["nE" + c, k], ["T" + c])
 
-    def deeds_turn(t, ch, db=None):
-        for bk, lo, stop in ((db or "T%d" % ch, 0, bool(db)), ("T%d" % ch, 128, True)):
-            if t:
-                rk = "R%d%d" % (t, ch)
-                mm(T[bk][:, lo:lo + 128], T[rk][:], T.Id[:], False, stop, [rk, "Id"], [bk])
-            else:
-                mm(T[bk][:, lo:lo + 128], T.Id[:], T.ownH[:, 128 * ch:128 * ch + 128], False, stop, ["ownH", "Id"], [bk])
+    def places(t, ch, bk):
+        mm(T[bk][:, 0:8], T.aT[:, 256 * t:256 * t + 128], T.Id[0:16, 8 * ch:8 * ch + 8], True, False, ["aT%d" % t, "Id"], [bk])
+        mm(T[bk][:, 0:8], T.E0[:], T.C2[:, 0:8], False, False, ["E0", "C2"], [bk])
 
-    def deeds_hit(ch, db=None):
-        bk = db or "T%d" % ch
-        ts(T["HT%d" % ch][:], T[bk][:, 0:128], 0.0, A.is_equal, [bk], ["HT%d" % ch])
+    def count(ch, bk):
+        mm(T[bk][:, 0:8], T["HT%d" % ch][:], T.U8[:], False, True, ["HT%d" % ch, "U8"], [bk])
 
-    def deeds_count(ch, bk, lo):
-        mm(T[bk][:, lo:lo + 128], T["HT%d" % ch][:], T.nBO[:], True, True, ["HT%d" % ch, "nBO"], [bk])
+    def aside(ch, bk, dst, key):
+        tt(T[dst][:, LIST[ch]:LIST[ch] + 8], T[bk][:, 0:8], T.D[:, 8 * ch:8 * ch + 8], A.min, [bk, "D"], [key])
 
-    def deeds_gain(ch):
+    def gain(ch):
         c = str(ch)
         tt(T["hb" + c][:], T["HT" + c][:], T["T" + c][:, 256:384], A.mult, ["HT" + c, "T" + c], ["hb" + c])
 
-    def deeds_own(ch):
-        c = str(ch)
-        tt(T["ownN" + c][:], T["T" + c][:, 128:256], T["hb" + c][:], A.add, ["T" + c, "hb" + c], ["ownN" + c])
+    def turn_gain(ch, bk):
+        mm(T[bk][:, 0:128], T["hb%d" % ch][:], T.I32[:], True, False, ["hb%d" % ch, "I32"], [bk])
 
-    def deeds_list(ch, bk, lo, lb, stop=True):
-        c = str(ch)
-        tt(T["XM" + c][:], T[bk][:, lo:lo + 128], T.maskP[:], A.max, [bk, "maskP"], ["XM" + c])
-        mm(T[lb][:, 8 * ch:8 * ch + 8], T["XM" + c][:], T.nK4[:], False, stop, ["XM" + c, "nK4"], [lb])
+    def turn_own(src, key, bk):
+        mm(T[bk][:, 0:128], src, T.Id[:], False, True, [key, "Id"], [bk])
 
-    def deeds_end(ch, lb, who):
-        cols = slice(8 * ch, 8 * ch + 8)
-        if who == "v":
-            ts(T.LS[:, cols], T[lb][:, cols], float(BIAS), A.add, [lb], ["LS%d" % ch])
-        else:
-            act(T.LS[:, cols], T[lb][:, cols], [lb], ["LS%d" % ch], bias=float(BIAS))
+    def as_list(ch, bk, dst, key):
+        act(T[dst][:, OWN[ch]:OWN[ch] + 128], T[bk][:, 0:128], [bk], [key], bias=float(BIAS))
+
+    def as_half(ch, bk, dst, key):
+        act(T[dst][:, sec(ch)], T[bk][:, 0:128], [bk], [key])
 
     def scatter_h(t, lo, hi):
         h = "NH%d" % (t % 2)
-        act(T.HN[:, 0:WIN].indirect(T.LS[:, 8 * lo:8 * hi]), T[h][:, 128 * lo:128 * hi], ["LS%d" % c for c in range(lo, hi)] + [h], HK,
-            func=F.Silu)
+        act(T.HN[:, 0:WIN].indirect(T["OF%d" % t][:, 128 + 8 * lo:128 + 8 * hi]), T[h][:, 128 * lo:128 * hi],
+            ["d%d%d" % (t, c) for c in range(lo, hi)] + [h], HK, func=F.Silu)
 
     def scatter_w(t, lo, hi):
         l = "lm%d" % (t % n)
-        vcopy(T.W[:, 0:WIN].indirect(T.LS[:, 8 * lo:8 * hi]), T[l][:, 128 * lo:128 * hi], ["LS%d" % c for c in range(lo, hi)] + [l], WK)
-
-    def offs(ch):
-        ts(T.off[:, 128 * ch:128 * ch + 128], T["ownN%d" % ch][:], BIAS, A.add, ["ownN%d" % ch], ["off%d" % ch])
+        vcopy(T.W[:, 0:WIN].indirect(T["OF%d" % t][:, 128 + 8 * lo:128 + 8 * hi]), T[l][:, 128 * lo:128 * hi],
+              ["d%d%d" % (t, c) for c in range(lo, hi)] + [l], WK + ["gate"])
 
     def parts(k, lo, hi):
         return [k + "_%d" % j for j in range(lo // 8, hi // 8)]
 
-    def gv(t, ch, lo, hi):
-        a, z = 128 * ch + lo, 128 * ch + hi
-        m, l = "M%d" % ch, "lr%d" % (t % n)
-        op("v", lambda: g.vector.tensor_tensor(out=T[m][:, 16 * lo:16 * hi], in0=T.W[:, 0:4096].indirect(T.off[:, a:z]),
-                                               in1=T[l][:, 16 * a:16 * z], op=A.max),
-           WK + ["off%d" % ch] + [l + "_%d" % q for q in range(16)], parts(m, lo, hi))
-
-    def gs(ch, lo, hi):
-        a, z = 128 * ch + lo, 128 * ch + hi
-        h = "H%d" % ch
-        act(T[h][:, 16 * lo:16 * hi], T.HN[:, 0:4096].indirect(T.off[:, a:z]), HK + ["off%d" % ch, "gb"], parts(h, lo, hi),
-            func=F.Identity, bias=T.gb[:])
-
-    def init(t, ch, p):
-        l, bk, o = "lm%d" % (t % n), "XY"[p] + str(ch), "ownN%d" % ch
-        mm(T[bk][:, 0:128], T[l][:, 128 * ch:128 * ch + 128], T.nBO[:], True, False, [l, "nBO"], [bk])
+    def list_of(t, ch, p, lo, hi):
         if p == 0:
-            mm(T[bk][:, 256:384], T.Z[:, 0:128], T.Z[:, 0:128], False, False, ["Z"], [bk])
-        mm(T[bk][:, 128 + 128 * p:256 + 128 * p], T[o][:], T.HI[:], False, False, [o, "HI"], [bk])
+            return T["OF%d" % t][:, OWN[ch] + lo:OWN[ch] + hi], "f%d%d" % (t, ch)
+        return T.off[:, 128 * ch + lo:128 * ch + hi], "off%d" % ch
+
+    def gv(t, ch, p, lo, hi):
+        m, l = "M%d" % ch, "lr%d" % (t % n)
+        lst, key = list_of(t, ch, p, lo, hi)
+        op("v", lambda: g.vector.tensor_tensor(out=T[m][:, 16 * lo:16 * hi], in0=T.W[:, 0:4096].indirect(lst),
+                                               in1=T[l][:, 2048 * ch + 16 * lo:2048 * ch + 16 * hi], op=A.max),
+           WK + [key, l + str(ch)], parts(m, lo, hi))
+
+    def gs(t, ch, p, lo, hi):
+        h = "H%d" % ch
+        lst, key = list_of(t, ch, p, lo, hi)
+        act(T[h][:, 16 * lo:16 * hi], T.HN[:, 0:4096].indirect(lst), HK + [key, "gb"], parts(h, lo, hi), func=F.Identity, bias=T.gb[:])
+
+    def init(t, ch):
+        c, ls, o = str(ch), "Ls%d" % (t % n), "w%d%d" % (t, ch)
+        own = T["OW%d" % t][:, sec(ch)]
+        for bk in ("X" + c, "Y" + c):
+            mm(T[bk][:, 0:128], T["E" + c][:], T.Ls[:, sec(t % n)], True, False, ["E" + c, ls], [bk])
+        mm(T["X" + c][:, 256:384], T.Z[:], T.Z[:], False, False, ["Z"], ["X" + c])
+        mm(T["X" + c][:, 128:256], own, T.HI[:], False, False, [o, "HI"], ["X" + c])
+        mm(T["T" + c][:, 0:128], own, T.HI[:], True, False, [o, "HI"], ["T" + c])
+
+    def init_deeds(t, ch):
+        c = str(ch)
+        mm(T["T" + c][:, 128:256], T["OW%d" % t][:, sec(ch)], T.HI[:], False, False, ["w%d%d" % (t, ch), "HI"], ["T" + c])
+        mm(T["T" + c][:, 128:256], T["nE" + c][:], T.aT[:, 256 * t + 256:256 * t + 384], False, False, ["nE" + c, "aT%d" % (t + 1)], ["T" + c])
+        gain_t(t + 1, ch, False)
 
     def sums_h(ch, p, lo=0, hi=128, stop=True):
-        bk, h = "XY"[p] + str(ch), "H%d" % ch
-        w = 2 if bk == "Y0" else 3
-        for q in range(16):
-            mm(T[bk][lo:hi, q:128 * w:16], T[h][:, 16 * lo + q:16 * hi:16], T.RH[:, 0:8 * w], False, stop and q == 15,
+        bk, h, w = "XY"[p] + str(ch), "H%d" % ch, 3 - p
+        for r in range(16):
+            mm(T[bk][lo:hi, r:128 * w:16], T[h][:, 16 * lo + r:16 * hi:16], T.RH[:, 0:8 * w], False, stop and r == 15,
                parts(h, lo, hi) + ["RH%d" % k for k in range(3)], [bk])
 
     def sums_m(ch, p, lo=0, hi=128, stop=False):
         bk, m = "XY"[p] + str(ch), "M%d" % ch
-        for q in range(16):
-            mm(T[bk][lo:hi, q:128:16], T[m][:, 16 * lo + q:16 * hi:16], T.RM[:], False, stop and q == 15, parts(m, lo, hi) + ["RM"], [bk])
+        for r in range(16):
+            mm(T[bk][lo:hi, r:128:16], T[m][:, 16 * lo + r:16 * hi:16], T.RM[:], False, stop and r == 15, parts(m, lo, hi) + ["RM"], [bk])
 
     def heirs(ch):
         c = str(ch)
-        act(T["hT" + c][:], T["X" + c][:, 256:384], ["X" + c], ["hT" + c], scale=2.0)
-        act(T["SA" + c][:], T["X" + c][:, 0:128], ["X" + c], ["SA" + c], func=F.Sign, bias=-TH)
-        op("t", lambda: g.tensor.transpose(T.P[:, 128 * ch:128 * ch + 128], T["hT" + c][:], T.Ih[:]), ["hT" + c, "Ih"], ["P"])
+        act(T["hT" + c][:], T["X" + c][:, 256:384], ["X" + c], ["hT" + c])
+        act(T["SA" + c][:], T["X" + c][:, 0:128], ["X" + c], ["SA" + c], func=F.Sign, scale=-1.0, bias=TH)
+        op("t", lambda: g.tensor.transpose(T.P[:, sec(ch)], T["hT" + c][:], T.Ih[:]), ["hT" + c, "Ih"], ["P"])
         mm(T["Y" + c][:, 128:256], T.HI[:], T["hT" + c][:], False, False, ["hT" + c, "HI"], ["Y" + c])
-        if ch == 0:
-            mm(T.Y0[:, 256:384], T.HI[:], T.hT0[:], False, False, ["hT0", "HI"], ["Y0"])
-        mm(T["Y" + c][:, 0:128], T.BI[:], T["SA" + c][:], False, False, ["SA" + c, "BI"], ["Y" + c])
 
-    def conv(ch):
-        ts(T.off[:, 128 * ch:128 * ch + 128], T.P[:, 128 * ch:128 * ch + 128], BIAS, A.add, ["P"], ["off%d" % ch])
-
-    def first_v(ch):
+    def first(ch):
         c = str(ch)
+        ts(T.off[:, sec(ch)], T.P[:, sec(ch)], BIAS, A.add, ["P"], ["off" + c])
         tt(T["ta" + c][:], T["SA" + c][:], T["X" + c][:, 128:256], A.mult, ["SA" + c, "X" + c], ["ta" + c])
 
-    def first_t(ch):
+    def first_t(ch, regions):
         c = str(ch)
-        mm(T["Y" + c][:, 256:384], T.H32[:], T["ta" + c][:], False, False, ["ta" + c, "H32"], ["Y" + c])
+        mm(T["Y" + c][:, 0:128], T.BI[:], T["SA" + c][:], False, False, ["SA" + c, "BI"], ["Y" + c])
+        for k in range(regions):
+            mm(T["T" + c][:, sec(k)], T.HI[:], T["hT" + c][:], False, False, ["hT" + c, "HI"], ["T" + c])
+            mm(T["T" + c][:, sec(k)], T.nI32[:], T["ta" + c][:], False, k == regions - 1, ["ta" + c, "nI32"], ["T" + c])
 
-    def sign(ch):
-        act(T["SB%d" % ch][:], T["Y%d" % ch][:, 0:128], ["Y%d" % ch], ["SB%d" % ch], func=F.Sign, bias=FAR - TH)
+    def near(ch):
+        ts(T["SB%d" % ch][:], T["Y%d" % ch][:, 0:128], TH - FAR, A.is_le, ["Y%d" % ch], ["SB%d" % ch], 2.0, A.mult)
 
     def second(ch):
         c = str(ch)
         tt(T["tb" + c][:], T["SB" + c][:], T["Y" + c][:, 128:256], A.mult, ["SB" + c, "Y" + c], ["tb" + c])
 
-    def update(ch, dst):
+    def hit(ch):
         c = str(ch)
-        tt(T[dst][:], T["Y" + c][:, 256:384], T["tb" + c][:], A.add, ["Y" + c, "tb" + c], [dst])
+        tt(T["HT" + c][:], T["T" + c][:, 128:256], T["tb" + c][:], A.is_equal, ["T" + c, "tb" + c], ["HT" + c])
 
-    def pass_on(t, ch):
-        sd = "SD%d%d" % (t, ch)
-        update(ch, sd)
-        send(nxt, T["R%d%d" % (t + 1, ch)][:], T[sd][:], "r%d%d" % (t + 1, ch), sd)
+    def result(ch, out, key):
+        c = str(ch)
+        tt(out, T["T" + c][:, 0:128], T["tb" + c][:], A.subtract, ["T" + c, "tb" + c], [key])
 
     def store_yo(ch):
-        c = str(ch)
-        loc = slice(128 * ch, 128 * ch + 128)
-        mm(T["T" + c][:, 0:128], T["OT" + c][:], T.Id[:], True, True, ["OT" + c, "Id"], ["T" + c])
-        act(T.yof[:, loc], T["T" + c][:, 0:128], ["T" + c], ["yof" + c], bias=float(BIAS))
-        store(T.yo[:, loc], T.yof[:, loc], ["yof" + c])
+        for k in range(8):
+            store("ys"[k % 2] if ch else "y", T.yo[16 * k:16 * k + 16, sec(ch)], T.yof[:, 128 * ch + 16 * k:128 * ch + 16 * k + 16], ["yof%d" % ch])
 
-    for k in range(4):
-        x_heir(k)
-        if k == 1:
-            mm(T.L[:, 128:256], T.EB[:], T.EB[:], True, True, ["EB"], ["L"])
+    def own0(ch):
+        act(T.ownH[:, sec(ch)], T.ownI[:, sec(ch)], ["ownI%d" % ch], ["ownH%d" % ch], bias=-float(BIAS))
+
+    def hit0(ch):
+        c = str(ch)
+        tt(T["HT" + c][:], T["T" + c][:, 128:256], T.ownH[:, sec(ch)], A.is_equal, ["T" + c, "ownH" + c], ["HT" + c])
+        places(0, ch, "L")
+        count(ch, "L")
+
+    def turn0(ch):
+        turn_gain(ch, "T%d" % ch)
+        turn_own(T.ownH[:, sec(ch)], "ownH%d" % ch, "T%d" % ch)
+
+    x_heir(0)
+    x_heir(1)
     indices(0)
-    act(T.ownH[:], T.ownI[:], ["ownI"], ["ownH"], bias=-float(BIAS))
+    mm(T.L[:, 0:8], T.E0[:], T.Id[0:16, 0:8], True, True, ["E0", "Id"], ["L"])
+    small_t(0, "T0")
+    sum_t(0, "T1")
+    x_heir(2)
+    x_heir(3)
     act(T.cb2[:], T.OH[:, 0:1], ["OH", "cb1"], ["cb2"], func=F.Identity, scale=-16384.0, bias=T.cb1[:])
-    act(T.nBO[:], T.L[:, 128:256], ["L"], ["nBO"], scale=-1.0)
+    small_out(0, "T0")
     act(T.cb3[:], T.OH[:, 1:2], ["OH", "cb2"], ["cb3"], func=F.Identity, scale=16.0 * (2048 + 16384 + 16), bias=T.cb2[:])
-    act(T.nK4[:], T.B8[:], ["B8"], ["nK4"], scale=-4096.0)
+    act(T.U8[:], T.L[:, 0:8], ["L"], ["U8"], scale=8192.0)
     act(T.cb[:], T.OH[:, 2:3], ["OH", "cb3"], ["cb"], func=F.Identity, scale=2064.0, bias=T.cb3[:])
+    sum_out(0, "T1")
+    double(0)
+    double(1)
     ts(T.wh[:], T.OH[:, 2:3], -1.0, A.mult, ["OH", "wh1"], ["wh"], T.wh1[:], A.add)
     ts(T.gb[:], T.wN[:], -272.0, A.mult, ["wN"], ["gb"])
-    ts(T.RM[:], T.B8[:], 2.0, A.mult, ["B8"], ["RM"])
-    for ch in (0, 1):
-        prep_deeds(0, ch)
-        deeds_turn(0, ch)
+    double(2)
+    ts(T.RM[:], T.nB8[:], -2.0, A.mult, ["nB8"], ["RM"])
+    for k, (w, val) in enumerate((("wN", 1.0), ("wh", 0.5), ("wh", -1.0))):
+        ts(T.RH[:, 8 * k:8 * k + 8], T.nB8[:], T[w][:], A.mult, ["nB8", w], ["RH%d" % k], val, A.mult)
+    send(prv, T.PR[:], T.PK[:], "pk", "PK")
     for t in range(1, n):
         send(T.cores[(rank + t) % n], T["lm%d" % t][:], T.lm0[:], "l%d" % t, "lm0")
-        if t == 1:
-            rep(0, "p", REP0["p"])
-            diagonal("HI", 0.5)
-    diagonal("Ih", 1.0)
-    diagonal("BI", FAR)
-    diagonal("H32", 1.0)
-    rep(0, "v", REP0["v"][:3])
-    ts(T.maskP[:], T.c15[:], T.p15[:], A.is_equal, ["c15", "p15"], ["maskP"], -1.0, A.mult)
+    for k, val in (("HI", 0.5), ("Ih", 1.0), ("BI", -FAR), ("nI32", -1.0), ("I16", 1.0 / 16)):
+        diagonal(k, val)
+    for k in (0, 1, 2):
+        x_book(k)
     for ch in (0, 1):
-        deeds_hit(ch)
+        mm(T["T%d" % ch][:, 128:256], T["E%d" % ch][:], T.aT[:, 0:128], True, False, ["E%d" % ch, "aT0"], ["T%d" % ch])
+        gain_t(0, ch, True)
     prep_nh_t(0)
-    x_book(0)
-    x_book(1)
-    for ch in (0, 1):
-        deeds_gain(ch)
-    rep(0, "s", REP0["s"][:2])
-    prep_nh_s(0)
     x_copy(0)
-    for ch in (0, 1):
-        deeds_own(ch)
-    x_book(2)
-    for ch in (0, 1):
-        deeds_count(ch, "T1", 128 * ch)
+    double(3)
     x_copy(1)
     x_copy(2)
-    prep_list(0, "L", 0, 256)
+    own0(0)
+    prep_nh_s(0)
     x_heir(4)
     x_book(3)
-    for ch in (0, 1):
-        deeds_list(ch, "T1", 128 * ch, "L", ch == 1)
-    for k, (w, val) in enumerate((("wN", -1.0), ("wh", -0.5), ("wh", 0.5))):
-        ts(T.RH[:, 8 * k:8 * k + 8], T.B8[:], T[w][:], A.mult, ["B8", w], ["RH%d" % k], val, A.mult)
-    indices(1)
-    x_book(4)
     x_heir(5)
-    x_heir(7)
-    x_heir(6)
+    x_book(4)
+    hit0(0)
     x_copy(3)
-    for ch in (0, 1):
-        deeds_end(ch, "L", "v")
-        offs(ch)
+    double(4)
+    gain(0)
+    aside(0, "L", "OF0", "d00")
+    x_heir(6)
+    x_book(5)
+    x_heir(7)
+    own0(1)
     x_copy(4)
-    rep(0, "v", REP0["v"][3:])
-    rep(0, "s", REP0["s"][2:])
-    for k in (5, 6, 7):
-        x_book(k)
-    for k in (5, 6, 7):
-        x_copy(k)
+    turn0(0)
+    x_copy(5)
+    hit0(1)
+    x_book(6)
+    x_book(7)
+    gain(1)
+    aside(1, "L", "OF0", "d01")
+    turn0(1)
+    as_list(0, "T0", "OF0", "f00")
+    as_half(0, "T0", "OW0", "w00")
+    x_copy(6)
+    x_copy(7)
     scatter_w(0, 0, 2)
     scatter_h(0, 0, 2)
+    ts(T.OF0[:, OWN[1]:OWN[1] + 128], T.T1[:, 0:128], float(BIAS), A.add, ["T1"], ["f01"])
+    vcopy(T.OW0[:, sec(1)], T.T1[:, 0:128], ["T1"], ["w01"])
 
     for t in range(R):
         last = t == R - 1
-        if t + 1 < n:
-            rep(t + 1, "p", REP["p"])
-        elif not last:
-            diagonal("I16", 1.0 / 16)
-        gv(t, 0, 0, 128)
-        gs(0, 0, 128)
-        for p in (0, 1):
-            init(t, 0, p)
-            init(t, 1, p)
+        u = t + 1
+        if u < n:
+            repeat(u, T["lm%d" % u], (0, 1), ["lm%d" % u, "gate"])
+        gv(t, 0, 0, 0, 128)
+        gs(t, 0, 0, 0, 128)
+        if t == 0:
+            indices(1)
+        init(t, 0)
+        init(t, 1)
         if last:
             for k, lane in (("yha", 0), ("yhb", 1)):
                 op("p", lambda: g.dma_start(out=T[k][:], in_=T.HN[lane:128:16, 0:4096]), HK, ["yhab" if lane else "yha0"], "d_yh", 16)
-            store(T.yd[:], T.W[:, 0:4096], WK)
-        else:
-            prep_nh_t(t + 1)
+            store("y", T.yd[:], T.W[:, 0:4096], WK)
         sums_m(0, 0)
         sums_h(0, 0)
-        gv(t, 1, 0, 128)
-        gs(1, 0, SS)
+        if t == 0:
+            small_t(1, "L")
+        elif last:
+            for ch in (0, 1):
+                mm(T["T%d" % ch][:, 0:128], T.E0[:], T.C2[:], False, False, ["E0", "C2"], ["T%d" % ch])
+        else:
+            init_deeds(t, 0)
+            init_deeds(t, 1)
+            prep_nh_t(u)
+        gv(t, 1, 0, 0, 128)
+        gs(t, 1, 0, 0, SS)
         heirs(0)
-        gs(1, SS, 128)
-        conv(0)
-        first_v(0)
+        if t == 0:
+            small_out(1, "L")
+        gs(t, 1, 0, SS, 128)
+        first(0)
         sums_m(1, 0)
         sums_h(1, 0)
-        first_t(0)
-        if not last:
-            prep_deeds(t + 1, 0)
-        else:
+        if t == 0:
+            init_deeds(t, 0)
+            init_deeds(t, 1)
+            prep_nh_t(u)
+        first_t(0, 1 if last else 2)
+        if last:
             mm(T.L[:, 0:256], T.Id[:], T.yha[:], True, False, ["Id", "yhab"], ["L"])
             mm(T.L[:, 0:256], T.I16[:], T.yhb[:], False, True, ["I16", "yhab"], ["L"])
-        gv(t, 0, 0, 128)
-        gs(0, 0, SS)
+        gv(t, 0, 1, 0, 128)
+        gs(t, 0, 1, 0, SS)
         heirs(1)
-        gs(0, SS, 128)
-        conv(1)
-        first_v(1)
+        gs(t, 0, 1, SS, 128)
+        first(1)
         sums_m(0, 1)
         sums_h(0, 1)
-        first_t(1)
-        gs(1, 0, 96)
-        gs(1, 96, 128)
-        gv(t, 1, VL[0], VL[1])
-        ts(T.SB0[:], T.Y0[:, 0:128], TH - FAR, A.is_le, ["Y0"], ["SB0"], -2.0, A.mult)
-        gv(t, 1, VL[1], VL[2])
-        second(0)
-        if VL[2] < VL[3]:
-            gv(t, 1, VL[2], VL[3])
+        first_t(1, 1 if last else 2)
+        gs(t, 1, 1, 0, 96)
+        gs(t, 1, 1, 96, 128)
+        gv(t, 1, 1, 0, 64)
+        near(0)
         if last:
-            update(0, "OT0")
+            gv(t, 1, 1, 64, 80)
+            second(0)
+            gv(t, 1, 1, 80, 96)
+            result(0, T.yof[:, 0:128], "yof0")
+            store_yo(0)
         else:
-            pass_on(t, 0)
-            prep_deeds(t + 1, 1, True)
-        gv(t, 1, VL[3], VL[4])
+            gv(t, 1, 1, 64, 96)
+        gv(t, 1, 1, 96, 128)
         sums_m(1, 1, 0, 64)
         sums_m(1, 1, 64, 96)
         sums_h(1, 1, 0, 96)
@@ -543,44 +592,59 @@ def rank_program(g, core, T, topo):
         sums_m(1, 1, 96, 128, True)
         if last:
             act(T.yhf[:], T.L[:, 0:256], ["L"], ["yhf"], bias=-16.0)
-            store(T.yh[:], T.yhf[:], ["yhf"])
-            sign(1)
-            store_yo(0)
+            store("y", T.yh[:], T.yhf[:], ["yhf"])
+            near(1)
             second(1)
-            update(1, "OT1")
+            result(1, T.yof[:, 128:256], "yof1")
             store_yo(1)
             break
-        prep_nh_s(t + 1)
-        prep_list(t + 1, "L", 0, 128)
-        deeds_turn(t + 1, 0)
-        sign(1)
+        sf, sw, of, ow = "SF%d" % u, "SW%d" % u, "OF%d" % u, "OW%d" % u
+
+        def pass_on(k, ch):
+            out, in_, lo, w = (ow, sw, 128 * ch, 128) if k == "w" else (of, sf, OWN[ch], 128) if k == "f" else (of, sf, LIST[ch], 8)
+            send(nxt, T[out][:, lo:lo + w], T[in_][:, lo:lo + w], "%s%d%d" % (k, u, ch), "s%s%d%d" % (k, u, ch))
+
+        prep_nh_s(u)
+        places(u, 0, "L")
+        second(0)
+        places(u, 1, "Y0")
+        hit(0)
+        count(0, "L")
+        gain(0)
+        turn_gain(0, "X0")
+        near(1)
+        aside(0, "L", sf, "sd%d0" % u)
+        pass_on("d", 0)
         second(1)
-        pass_on(t, 1)
-        if t + 2 < R:
-            indices(t + 2)
-        if t + 1 < n:
-            rep(t + 1, "s", REP["s"])
-        deeds_hit(0)
-        deeds_count(0, "X0", 384)
-        deeds_gain(0)
-        deeds_list(0, "X0", 384, "L")
-        deeds_own(0)
-        deeds_end(0, "L", "s")
-        offs(0)
-        scatter_w(t + 1, 0, 1)
-        scatter_h(t + 1, 0, 1)
-        prep_list(t + 1, "X1", 128, 256)
-        prep_diff(t + 1, 1, "L")
-        deeds_turn(t + 1, 1, "L")
-        deeds_hit(1, "L")
-        deeds_count(1, "X0", 384)
-        deeds_list(1, "X0", 384, "X1")
-        deeds_gain(1)
-        deeds_end(1, "X1", "s")
-        deeds_own(1)
-        scatter_h(t + 1, 1, 2)
-        scatter_w(t + 1, 1, 2)
-        offs(1)
+        result(0, T.SD0[:], "SD0")
+        turn_own(T.SD0[:], "SD0", "X0")
+        hit(1)
+        count(1, "Y0")
+        as_list(0, "X0", sf, "sf%d0" % u)
+        aside(1, "Y0", sf, "sd%d1" % u)
+        pass_on("d", 1)
+        pass_on("f", 0)
+        gain(1)
+        turn_gain(1, "X1")
+        result(1, T.SD1[:], "SD1")
+        turn_own(T.SD1[:], "SD1", "X1")
+        as_half(0, "X0", sw, "sw%d0" % u)
+        as_list(1, "X1", sf, "sf%d1" % u)
+        as_half(1, "X1", sw, "sw%d1" % u)
+        pass_on("w", 0)
+        pass_on("f", 1)
+        pass_on("w", 1)
+        if u + 1 < R:
+            indices(u + 1)
+        if u < n:
+            sum_t(u, "Y1")
+            sum_out(u, "Y1")
+        if u + 1 < R:
+            small_t(u + 1, "Y0")
+            small_out(u + 1, "Y0")
+        for ch in (0, 1):
+            scatter_w(u, ch, ch + 1)
+            scatter_h(u, ch, ch + 1)
 
     g.sync.wait_ge(T.sem.dout, cnt["dout"])
     wait("p", {s: c for s, c in cnt.items() if s != "dout"})

@@ -5,66 +5,86 @@ TH = 136.5 + 4096
 FAR = 256.0
 R = 5
 WIN = 6144
-SS = 88
+SS = 64
+S0 = 64
 VCOPY = (1, 4, 6)
 PIECE = (0, 1536, 2560, 3584, 4096)
-OWN, LIST = (0, 144), (128, 136)
+LANES = (0, 1, 3)
+FILL = (0, 2048, 3072, 4096)
+SHIP = (0, 1280, 2304, 3328, 4096)
 
 SCRATCH = {}
-SEMAPHORES = ["v", "s", "t", "p", "loc", "dout", "pk"]
+SEMAPHORES = ["v", "s", "t", "p", "loc", "dout"]
 
 
 def _buf(name, cols, dtype, where="sbuf", rows=128):
     SCRATCH[name] = (where, [rows, cols], dtype)
 
 
-for _n, _c in (("pi", 1), ("p15i", 1), ("gi", 8), ("g4i", 8), ("ownI", 256), ("PK", 128), ("PR", 128)):
+for _n, _c in (("pi", 1), ("p15i", 1), ("p31i", 1), ("gi", 8), ("g4i", 8), ("ownI", 256), ("TI", 256)):
     _buf(_n, _c, "int32")
 _buf("heirI", 512, "int32", rows=64)
-_buf("abI", 1280, "int32", rows=32)
-for _n in ("p15", "c8", "wN", "wh", "wh1", "cb", "cb1", "cb2", "cb3", "gb", "e24", "fs", "fb"):
+for _n in ("p15", "p31", "wh", "wh1", "cb", "cb1", "cb2", "cb3", "gb", "e80", "fs", "fb"):
     _buf(_n, 1, "float32")
-for _n, _c in (("dv", 128), ("i3", 3), ("nB8", 8), ("U8", 8), ("WN", 128), ("WH", 1024), ("Id", 128), ("HI", 128), ("BI", 128), ("I16", 128),
-               ("Z", 128), ("RM", 8), ("RH", 24), ("yha", 256), ("yhb", 256), ("W", WIN), ("M0", 2048), ("M1", 2048),
-               ("H0", 2048), ("H1", 2048), ("HT0", 128), ("HT1", 128), ("SA0", 128), ("SA1", 128), ("SB0", 128), ("SB1", 128)):
+for _n, _c in (("dv", 128), ("i4", 4), ("nB8", 8), ("U8", 8), ("WN", 128), ("WH", 1024), ("EN", 640), ("Id", 128), ("HI", 128), ("BI", 128),
+               ("I8", 128), ("I4", 128), ("Z", 128), ("RM", 8), ("yha", 256), ("yhb", 256), ("M0", 2048), ("M1", 2048), ("lm0", 256), ("lr", 4096),
+               ("HT0", 128), ("HT1", 128), ("SA0", 128), ("SA1", 128), ("SB0", 128), ("SB1", 128),
+               ("ev", 128), ("E0", 128), ("E1", 128), ("nE0", 128), ("nE1", 128)):
     _buf(_n, _c, "bfloat16")
-_buf("EN", 128, "bfloat16", rows=32)
-for _n in ("ev", "E0", "E1", "nE0", "nE1", "C2"):
-    _buf(_n, 128, "bfloat16", rows=16)
-_buf("ab", 1280, "float16", rows=32)
-_buf("aT", 1280, "float16", rows=16)
-_buf("Ls", 512, "float16", rows=16)
-for _n, _c in (("Hs", 512), ("Ih", 128), ("ownH", 256), ("hT0", 128), ("hT1", 128), ("SD0", 128), ("SD1", 128)):
+_buf("C2", 128, "bfloat16")
+_buf("aT0", 256, "float16", rows=16)
+_buf("Ls", 128, "float16", rows=16)
+for _n, _c in (("Hs", 512), ("Ih", 128), ("ownH", 256), ("hT0", 128), ("hT1", 128), ("H0", 2048), ("H1", 2048), ("RH", 24),
+               ("aTA", 256), ("OW", 256)):
     _buf(_n, _c, "float16")
-for _n, _c in (("HN", WIN), ("NH0", 256), ("NH1", 256), ("OH", 3), ("I32", 128), ("nI32", 128), ("D", 16),
+for _n, _c in (("HN0", WIN), ("HN1", WIN), ("NH", 256), ("OH", 4), ("I32", 128), ("nI32", 128), ("D", 16),
                ("hb0", 128), ("hb1", 128), ("ta0", 128), ("ta1", 128), ("tb0", 128), ("tb1", 128), ("yof", 256), ("yhf", 256)):
     _buf(_n, _c, "float32")
-_buf("off", 256, "uint16")
+for _n, _c in (("off", 256), ("OF", 256), ("DL", 16)):
+    _buf(_n, _c, "uint16")
 for _t in range(5):
-    _buf("OF%d" % _t, 272, "uint16")
-    _buf("OW%d" % _t, 256, "float16")
+    _buf("W%d" % _t, WIN, "bfloat16")
     if _t:
-        _buf("SF%d" % _t, 272, "uint16")
-        _buf("SW%d" % _t, 256, "float16")
-        SEMAPHORES.extend("%s%d%d" % (_k, _t, _c) for _k in "dfw" for _c in (0, 1))
+        _buf("CP%d" % _t, 768, "float32")
+        _buf("CR%d" % _t, 768, "float32")
+        SEMAPHORES.extend("%s%d" % (_k, _t) for _k in ("bw", "bh", "cp", "xh"))
+        SEMAPHORES.extend("hw%d%d" % (_t, _k) for _k in range(1, len(SHIP) - 1))
 for _t in range(4):
-    _buf("lm%d" % _t, 256, "bfloat16")
-    _buf("lr%d" % _t, 4096, "bfloat16")
-    SEMAPHORES.extend(["ra%d" % _t, "rb%d" % _t])
+    _buf("TB%d" % _t, 256, "float16")
     if _t:
-        SEMAPHORES.append("l%d" % _t)
-for _n in ("own0", "own1", "lm", "heir", "ab", "ac", "ad", "pk", "yh", "bk0", "bk1", "bk2", "bk3"):
+        SEMAPHORES.append("tb%d" % _t)
+for _n in ("own0", "own1", "lm", "heir", "ti", "yh", "bk0", "bk1", "bk2", "bk3", "ra", "rb"):
     SEMAPHORES.append("d_" + _n)
 BANKS = ["X0", "X1", "Y0", "Y1", "T0", "T1", "L", "P"]
 for _n in BANKS:
     _buf(_n, 512, "float16" if _n == "P" else "float32", "psum")
 
 
+def helper_of(src, dst, T, topo):
+    if topo.chip(src) == topo.chip(dst):
+        return None
+    return [c for c in topo.cores_of(src) if T.rank_of(c) is None and topo.die(c) != topo.die(src) and topo.may_write(c, dst)][0]
+
+
+def hand_on(g, core, dst, src, T, topo):
+    rid, pid, _ = topo.addr(dst)
+    spare = len(topo.engines(src, core)) - len(topo.engines(src, dst))
+    for u in range(1, R):
+        for k in range(1, len(SHIP) - 1):
+            piece = T["W%d" % u][:, SHIP[k]:SHIP[k + 1]]
+            g.wait_ge(T.sem["hw%d%d" % (u, k)], spare)
+            g.remote_dma(piece, piece, T.sem["bw%d" % u], T.sem.loc, pid, rid, topo.mask(core, dst))
+    g.wait_ge(T.sem.loc, (R - 1) * (len(SHIP) - 2) * len(topo.engines(core, dst)))
+
+
 def rank_program(g, core, T, topo):
     rank = T.rank_of(core)
-    if rank is None:
-        return
     n = len(T.cores)
+    if rank is None:
+        for r in range(n):
+            if helper_of(T.cores[r], T.cores[r - 1], T, topo) == core:
+                hand_on(g, core, T.cores[r - 1], T.cores[r], T, topo)
+        return
     eng = {"v": g.vector, "s": g.scalar, "t": g.tensor, "p": g, "y": g.sync}
     know = {q: {} for q in eng}
     cnt = {}
@@ -132,8 +152,8 @@ def rank_program(g, core, T, topo):
     def vcopy(out, in_, reads, writes):
         op("v", lambda: g.vector.tensor_copy(out=out, in_=in_), reads, writes)
 
-    def fill(k, value):
-        op("v", lambda: g.vector.memset(T[k][:], value), [], [k])
+    def fill(ap, key, value):
+        op("v", lambda: g.vector.memset(ap, value), [], [key])
 
     def act(out, in_, reads, writes, func=F.Copy, **kw):
         op("s", lambda: g.scalar.activation(out=out, in_=in_, func=func, **kw), reads, writes)
@@ -141,118 +161,109 @@ def rank_program(g, core, T, topo):
     def mm(out, lhsT, rhs, start, stop, reads, writes):
         op("t", lambda: g.tensor.matmul(out=out, lhsT=lhsT, rhs=rhs, start=start, stop=stop), reads, writes)
 
-    def dmas(pairs, sem, key, reads=()):
-        for k, (out, in_) in enumerate(pairs):
-            op("y", lambda: g.sync.dma_start(out=out, in_=in_), reads, [key if k == len(pairs) - 1 else key + "." + str(k)], sem, 16)
+    def dmas(pairs, sem, writes, reads=(), q="y"):
+        wait(q, deps_of(q, reads, writes))
+        for out, in_ in pairs:
+            eng[q].dma_start(out=out, in_=in_).then_inc(T.sem[sem], 16)
+        note(q, sem, 16 * len(pairs), reads, writes)
 
     def store(q, out, in_, reads):
         op(q, lambda: eng[q].dma_start(out=out, in_=in_), reads, [], "dout", 16)
 
-    def iota(k, pattern, base, cm):
-        small = SCRATCH[k][2] != "int32"
-        op("p", lambda: g.iota(T[k][:], pattern, base, cm, allow_small_or_imprecise_dtypes=True) if small
-           else g.iota(T[k][:], pattern, base, cm), [], [k])
+    def iota(ap, key, pattern, base, cm, small=True):
+        op("p", lambda: g.iota(ap, pattern, base, cm, allow_small_or_imprecise_dtypes=True) if small
+           else g.iota(ap, pattern, base, cm), [], [key])
 
     def mark(ap, key, pattern, base, value, whole):
-        op("p", lambda: g.affine_select(ap, ap, pattern, A.not_equal, value, base, 1), [key, whole], [key])
+        op("p", lambda: g.affine_select(ap, ap, pattern, A.not_equal, value, base, 1), [key] + whole, [key])
 
     def diagonal(k, value):
         op("p", lambda: g.affine_select(T[k][:], T.Z[:], [[-1, 128]], A.not_equal, value, 0, 1), ["Z"], [k])
 
-    def send(dst, out, in_, sem, key):
-        wait("p", deps_of("p", [key], []))
+    def send(dst, out, in_, sem, keys, without=()):
+        wait("p", deps_of("p", keys, []))
         rid, pid, _ = topo.addr(dst)
-        ne = len(topo.engines(core, dst))
-        g.remote_dma(out, in_, T.sem[sem], T.sem.loc, pid, rid, topo.mask(core, dst))
-        cnt["loc"] = cnt.get("loc", 0) + ne
+        use = [e for e in topo.engines(core, dst) if e not in without]
+        g.remote_dma(out, in_, T.sem[sem], T.sem.loc, pid, rid, sum(1 << e for e in use))
+        cnt["loc"] = cnt.get("loc", 0) + len(use)
 
-    def arrive(sem, key, src):
-        ne = len(topo.engines(src, core))
-        cnt[sem] = ne
-        wr[key] = {sem: ne}
+    def arrive(sem, key, src, writes=1):
+        cnt[sem] = writes * len(topo.engines(src, core))
+        wr[key] = {sem: cnt[sem]}
         rd[key] = {}
 
     nxt = T.cores[(rank + 1) % n]
     prv = T.cores[(rank - 1) % n]
-    arrive("pk", "PR", nxt)
+    via = helper_of(core, prv, T, topo)
     for t in range(1, n):
-        arrive("l%d" % t, "lm%d" % t, T.cores[(rank - t) % n])
+        arrive("tb%d" % t, "TB%d" % t, T.cores[(rank + t) % n])
     for t in range(1, R):
-        for ch in (0, 1):
-            for k in "dfw":
-                arrive("%s%d%d" % (k, t, ch), "%s%d%d" % (k, t, ch), prv)
+        arrive("bw%d" % t, "W%d" % t, nxt, len(SHIP) - 1)
+        arrive("bh%d" % t, "CR%d" % t, nxt)
+    WK = [["Wk%d" % k for k in range(4)]] + [["W%d" % t] for t in range(1, R)]
+    HK = [["HA%d" % k for k in range(8)], ["HB%d" % k for k in range(len(FILL) - 1)]]
 
     def sec(ch):
         return slice(128 * ch, 128 * ch + 128)
 
     def book_in(k):
-        dmas([(T.W[:, PIECE[k]:PIECE[k + 1]], T.bk[:, PIECE[k]:PIECE[k + 1]])], "d_bk%d" % k, "Wk%d" % k)
+        dmas([(T.W0[:, PIECE[k]:PIECE[k + 1]], T.bk[:, PIECE[k]:PIECE[k + 1]])], "d_bk%d" % k, ["Wk%d" % k])
 
     def own_in(ch):
         dmas([(T.ownI[:, 128 * ch + 16 * k:128 * ch + 16 * k + 16], T.own[16 * k:16 * k + 16, sec(ch)]) for k in range(8)],
-             "d_own%d" % ch, "ownI%d" % ch)
+             "d_own%d" % ch, ["ownI%d" % ch])
 
-    def repeat(t, src, chunks, reads):
-        lr = T["lr%d" % t]
-        dmas([(lr[:, 2048 * ch + 128 * q:2048 * ch + 128 * q + 128], src[:, sec(ch)]) for ch in chunks for q in range(4)],
-             "ra%d" % t, "lr%da" % t, reads)
-        dmas([(lr[:, 2048 * ch + 512 * k:2048 * ch + 512 * k + 512], lr[:, 2048 * ch:2048 * ch + 512]) for ch in chunks for k in (1, 2, 3)],
-             "rb%d" % t, "lr%d1" % t, ["lr%da" % t])
-        if 0 in chunks:
-            wr["lr%d0" % t] = dict(wr["lr%d1" % t])
-
-    dmas([(T.heirI[:], T.heir[:])], "d_heir", "heirI")
-    dmas([(T.lm0[:], T.lm[:])], "d_lm", "lm0")
-    dmas([(T.abI[8 * k:8 * k + 8, 0:256], src[:, 0:256]) for k, src in enumerate((T.da, T.db, T.db, T.db))], "d_ab", "abI")
+    dmas([(T.heirI[:], T.heir[:])], "d_heir", ["heirI"])
+    dmas([(T.lm0[:], T.lm[:])], "d_lm", ["lm0"])
+    dmas([(T.TI[0:40, :], T.da[:]), (T.TI[40:80, :], T.db[:]), (T.TI[80:120, :], T.db[:]), (T.TI[120:128, :], T.db[:, 0:256])], "d_ti", ["TI"])
     book_in(0)
-    dmas([(T.PK[:, 0:64], T.da[:, 256:1280]), (T.PK[:, 64:128], T.db[:, 256:1280])], "d_pk", "PK")
     book_in(1)
     own_in(0)
     book_in(2)
     book_in(3)
     own_in(1)
-    dmas([(T.abI[16:24, 256:1280], T.db[:, 256:1280]), (T.abI[24:32, 256:1280], T.db[:, 256:1280])], "d_ac", "acI")
-    repeat(0, T.lm, (1,), [])
-    dmas([(T.abI[0:8, 256:1280], T.PR[:, 0:64]), (T.abI[8:16, 256:1280], T.PR[:, 64:128])], "d_ad", "adI", ["PR"])
-    WK = ["Wk%d" % k for k in range(4)]
-    HK = ["HN%d" % k for k in range(8)]
+    dmas([(T.lr[:, 2048 + 128 * q:2048 + 128 * q + 128], T.lm[:, sec(1)]) for q in range(4)], "d_ra", ["lra"])
+    dmas([(T.lr[:, 2048 + 512 * k:2048 + 512 * k + 512], T.lr[:, 2048:2560]) for k in (1, 2, 3)], "d_rb", ["lr1"], ["lra"])
 
-    iota("pi", [[0, 1]], 0, 1)
-    iota("gi", [[-16, 8]], 0, 1)
-    iota("i3", [[1, 3]], 0, 0)
-    for k, val in (("Z", 0.0), ("WH", 0.0), ("C2", float(BIAS))):
-        fill(k, val)
-    act(T.EN[:], T.Z[0:32, :], ["Z"], ["EN"], func=F.Silu)
-    mark(T.WH[:, 0:1024:16], "WH0", [[-1, 8], [-8, 8]], -64, 16.0, "WH")
-    mark(T.WH[:, 1:1024:16], "WH1", [[-1, 8], [-8, 8]], 0, 16.0, "WH")
-    iota("dv", [[1, 128]], 0, -1)
-    mark(T.WH[:, 1:1024:16], "WH1", [[-1, 8], [-8, 8]], -64, -256.0, "WH")
-    iota("ev", [[0, 16], [-1, 8]], 0, 1)
-    mark(T.EN[:, 0:128:16], "EN0", [[-1, 8]], -24, 16.0, "EN")
-    mark(T.EN[:, 1:128:16], "EN1", [[-1, 8]], -16, 16.0, "EN")
-    iota("D", [[1, 16]], 4096, 16)
-    mark(T.EN[:, 1:128:16], "EN1", [[-1, 8]], -24, -256.0, "EN")
+    iota(T.pi[:], "pi", [[0, 1]], 0, 1, False)
+    iota(T.gi[:], "gi", [[-16, 8]], 0, 1, False)
+    iota(T.i4[:], "i4", [[1, 4]], 0, 0)
+    fill(T.Z[:], "Z", 0.0)
+    fill(T.WH[:], "WH", 0.0)
+    fill(T.EN[:, 128:640], "ENb", 0.0)
+    fill(T.C2[:], "C2", float(BIAS))
+    act(T.EN[:, 0:128], T.Z[:], ["Z"], ["ENa"], func=F.Silu)
+    mark(T.WH[:, 0:1024:16], "WH0", [[-1, 8], [-8, 8]], -64, 8.0, ["WH"])
+    mark(T.WH[:, 1:1024:16], "WH1", [[-1, 8], [-8, 8]], 0, 8.0, ["WH"])
+    iota(T.dv[:], "dv", [[1, 128]], 0, -1)
+    mark(T.WH[:, 1:1024:16], "WH1", [[-1, 8], [-8, 8]], -64, -256.0, ["WH"])
+    iota(T.ev[:], "ev", [[0, 16], [1, 8]], 0, 0)
+    mark(T.EN[:, 0:640:16], "EN0", [[-1, 5], [-5, 8]], -80, 8.0, ["ENa", "ENb"])
+    mark(T.EN[:, 1:640:16], "EN1", [[-1, 5], [-5, 8]], -40, 8.0, ["ENa", "ENb"])
+    iota(T.D[:], "D", [[1, 16]], 4096, 16)
+    mark(T.EN[:, 1:640:16], "EN1", [[-1, 5], [-5, 8]], -80, -256.0, ["ENa", "ENb"])
     diagonal("I32", 1.0)
 
     ts(T.p15i[:], T.pi[:], 15, A.bitwise_and, ["pi"], ["p15i"])
-    ts(T.e24[:], T.pi[:], 24.0, A.is_ge, ["pi"], ["e24"])
+    ts(T.e80[:], T.pi[:], 80.0, A.is_ge, ["pi"], ["e80"])
     ts(T.g4i[:], T.gi[:], 4, A.arith_shift_right, ["gi"], ["g4i"])
+    ts(T.p31i[:], T.pi[:], 31, A.bitwise_and, ["pi"], ["p31i"])
     vcopy(T.p15[:], T.p15i[:], ["p15i"], ["p15"])
-    ts(T.fs[:], T.e24[:], -15.0 / 16, A.mult, ["e24"], ["fs"], 1.0, A.add)
-    ts(T.fb[:], T.e24[:], 3072.0, A.mult, ["e24"], ["fb"], -2048.0, A.add)
-    ts(T.OH[:], T.i3[:], T.p15[:], A.is_equal, ["i3", "p15"], ["OH"])
-    ts(T.wN[:], T.p15[:], 8.0, A.is_ge, ["p15"], ["wN"])
+    ts(T.fs[:], T.e80[:], -31.0 / 32, A.mult, ["e80"], ["fs"], 1.0, A.add)
+    ts(T.fb[:], T.e80[:], 3072.0, A.mult, ["e80"], ["fb"], -2048.0, A.add)
+    ts(T.OH[:], T.i4[:], T.p15[:], A.is_equal, ["i4", "p15"], ["OH"])
+    vcopy(T.p31[:], T.p31i[:], ["p31i"], ["p31"])
     ts(T.Hs[0:64, :], T.heirI[:], BIAS, A.subtract, ["heirI"], ["Hs0"])
-    act(T.Hs[64:128, :], T.heirI[:], ["heirI"], ["Hs1"], scale=1.0 / 16, bias=1024.0)
+    act(T.Hs[64:128, :], T.heirI[:], ["heirI"], ["Hs1"], scale=1.0 / 32, bias=1024.0)
     ts(T.Id[:], T.dv[:], 0.0, A.is_equal, ["dv"], ["Id"])
     ts(T.nB8[:], T.g4i[:], 0.0, A.is_equal, ["g4i"], ["nB8"], -1.0, A.mult)
-    ts(T.c8[:], T.p15[:], 7.0, A.is_le, ["p15"], ["c8"], 8.0, A.mult)
-    ts(T.cb1[:], T.wN[:], 16.0, A.mult, ["wN"], ["cb1"])
-    ts(T.WN[:], T.dv[:], T.c8[:], A.is_equal, ["dv", "c8"], ["WN"])
+    ts(T.cb1[:], T.OH[:, 3:4], 16.0, A.mult, ["OH"], ["cb1"])
+    ts(T.WN[:], T.dv[:], T.p15[:], A.add, ["dv", "p15"], ["WN"], 3.0, A.is_equal)
     for ch in (0, 1):
-        ts(T["E%d" % ch][:], T.ev[:], 8.0 * ch, A.is_equal, ["ev"], ["E%d" % ch])
-        ts(T["nE%d" % ch][:], T.ev[:], 8.0 * ch, A.is_equal, ["ev"], ["nE%d" % ch], -1.0, A.mult)
-    ts(T.wh1[:], T.OH[:, 1:2], 1.0 / 16, A.mult, ["OH"], ["wh1"], T.OH[:, 0:1], A.add)
+        ts(T["E%d" % ch][:], T.ev[:], T.p31[:], A.subtract, ["ev", "p31"], ["E%d" % ch], -8.0 * ch, A.is_equal)
+    for ch in (0, 1):
+        ts(T["nE%d" % ch][:], T["E%d" % ch][:], -1.0, A.mult, ["E%d" % ch], ["nE%d" % ch])
+    ts(T.wh1[:], T.OH[:, 1:2], 1.0 / 32, A.mult, ["OH"], ["wh1"], T.OH[:, 0:1], A.add)
 
     XB = ("Y0", "Y1", "X0", "X1")
 
@@ -260,133 +271,146 @@ def rank_program(g, core, T, topo):
         mm(T[XB[k % 4]][:], T.WH[:, 128 * k:128 * k + 128], T.Hs[:], True, False, ["WH0", "WH1", "Hs0", "Hs1"], [XB[k % 4]])
 
     def x_book(k):
-        wk = [WK[j] for j in range(4) if PIECE[j] < 512 * k + 512 and PIECE[j + 1] > 512 * k]
-        mm(T[XB[k % 4]][:], T.WN[:], T.W[:, 512 * k:512 * k + 512], False, True, ["WN"] + wk, [XB[k % 4]])
+        wk = [WK[0][j] for j in range(4) if PIECE[j] < 512 * k + 512 and PIECE[j + 1] > 512 * k]
+        mm(T[XB[k % 4]][:], T.WN[:], T.W0[:, 512 * k:512 * k + 512], False, True, ["WN"] + wk, [XB[k % 4]])
 
     def x_copy(k):
         bk = XB[k % 4]
         if k in VCOPY:
-            ts(T.HN[:, 512 * k:512 * k + 512], T[bk][:], T.cb[:], A.add, [bk, "cb"], ["HN%d" % k])
+            ts(T.HN0[:, 512 * k:512 * k + 512], T[bk][:], T.cb[:], A.add, [bk, "cb"], ["HA%d" % k])
         else:
-            act(T.HN[:, 512 * k:512 * k + 512], T[bk][:], [bk, "cb"], ["HN%d" % k], func=F.Identity, bias=T.cb[:])
+            act(T.HN0[:, 512 * k:512 * k + 512], T[bk][:], [bk, "cb"], ["HA%d" % k], func=F.Identity, bias=T.cb[:])
+
+    def fill_h(k):
+        iota(T.HN1[:, FILL[k]:FILL[k + 1]], "HB%d" % k, [[0, FILL[k + 1] - FILL[k]]], 1024, 0)
 
     def double(k):
         w = 64 * 2 ** k
         if k < 2:
-            vcopy(T.lr0[:, sec(k)], T.lm0[:, 0:128], ["lm0"], ["lr0.%d" % k])
+            vcopy(T.lr[:, sec(k)], T.lm0[:, 0:128], ["lm0"], ["lr.%d" % k])
         else:
-            vcopy(T.lr0[:, w:2 * w], T.lr0[:, 0:w], ["lr0.%d" % j for j in range(k)], ["lr00" if k == 4 else "lr0.%d" % k])
+            vcopy(T.lr[:, w:2 * w], T.lr[:, 0:w], ["lr.%d" % j for j in range(k)], ["lr0" if k == 4 else "lr.%d" % k])
 
-    def indices(t):
-        cols = slice(256 * t, 256 * t + 256)
-        if t:
-            ts(T.ab[:, cols], T.abI[:, cols], T.fs[0:32, :], A.mult, ["acI", "adI", "fs", "fb"], ["ab%d" % t], T.fb[0:32, :], A.add)
-        else:
-            act(T.ab[:, cols], T.abI[:, cols], ["abI", "fs", "fb"], ["ab0"], func=F.Identity, scale=T.fs[0:32, :], bias=T.fb[0:32, :])
+    def block(t):
+        return slice(32 * (t - 1), 32 * (t - 1) + 16) if t else slice(0, 16)
+
+    def table(t, k):
+        return T["aTA" if t else "aT0"][block(t), sec(k)], "aTA" if t else "aT0"
 
     def small_t(t, bk):
+        tb = "TB%d" % (t % n)
         for r in range(16):
-            mm(T[bk][0:16, r:256:16], T.ab[:, 256 * t + r:256 * t + 256:16], T.Id[0:32, 0:16], r == 0, r == 15, ["ab%d" % t, "Id"], [bk])
-
-    def small_out(t, bk):
-        if t < 2:
-            act(T.aT[:, 256 * t:256 * t + 256], T[bk][0:16, 0:256], [bk], ["aT%d" % t])
-        else:
-            vcopy(T.aT[:, 256 * t:256 * t + 256], T[bk][0:16, 0:256], [bk], ["aT%d" % t])
-
-    def sum_t(t, bk):
-        for r in range(16):
-            mm(T[bk][0:16, 256 + r:384:16], T["lm%d" % t][:, r:256:16], T.nB8[:], r == 0, r == 15, ["lm%d" % t, "nB8"], [bk])
-
-    def sum_out(t, bk):
-        if t:
-            ts(T.Ls[:, sec(t)], T[bk][0:16, 256:384], float(BIAS), A.add, [bk], ["Ls%d" % t])
-        else:
-            act(T.Ls[:, sec(t)], T[bk][0:16, 256:384], [bk], ["Ls%d" % t], bias=float(BIAS))
+            mm(T[bk][block(t), r:256:16], T[tb][:, r:256:16], T.Id[:, t:80:5], t == 0 and r == 0, t == 0 and r == 15, [tb, "Id"], [bk])
 
     def prep_nh_t(t):
-        lk = "lm%d" % (t % n)
-        mm(T.L[:, 256:512], T.WN[:], T[lk][:], True, False, ["WN", lk], ["L"])
-        mm(T.L[:, 256:512], T.EN[:], T.ab[:, 256 * t:256 * t + 256], False, True, ["EN0", "EN1", "ab%d" % t], ["L"])
+        tb = "TB%d" % (t % n)
+        mm(T.L[:, 256:512], T.WN[:], T.lm0[:], True, False, ["WN", "lm0"], ["L"])
+        mm(T.L[:, 256:512], T.EN[:, sec(t)], T[tb][:], False, True, ["EN0", "EN1", tb], ["L"])
 
-    def prep_nh_s(t):
-        k = "NH%d" % (t % 2)
-        act(T[k][:], T.L[:, 256:512], ["L", "cb"], [k], func=F.Identity, bias=T.cb[:])
+    def prep_nh_s():
+        act(T.NH[:], T.L[:, 256:512], ["L", "cb"], ["NH"], func=F.Identity, bias=T.cb[:])
+
+    def spread(out, t, ch, k, sign, start, stop):
+        c = str(ch)
+        tab, key = table(t, k)
+        mm(out, T[sign + c][block(t), :], tab, start, stop, [sign + c, key], ["T" + c])
 
     def gain_t(t, ch, stop):
-        c, k = str(ch), "aT%d" % t
-        mm(T["T" + c][:, 256:384], T["E" + c][:], T.aT[:, 256 * t + 128:256 * t + 256], False, False, ["E" + c, k], ["T" + c])
-        mm(T["T" + c][:, 256:384], T["nE" + c][:], T.aT[:, 256 * t:256 * t + 128], False, stop, ["nE" + c, k], ["T" + c])
+        spread(T["T%d" % ch][:, 256:384], t, ch, 1, "E", False, False)
+        spread(T["T%d" % ch][:, 256:384], t, ch, 0, "nE", False, stop)
 
     def places(t, ch, bk):
-        mm(T[bk][:, 0:8], T.aT[:, 256 * t:256 * t + 128], T.Id[0:16, 8 * ch:8 * ch + 8], True, False, ["aT%d" % t, "Id"], [bk])
-        mm(T[bk][:, 0:8], T.E0[:], T.C2[:, 0:8], False, False, ["E0", "C2"], [bk])
+        tab, key = table(t, 0)
+        lo = block(t).start + 8 * ch
+        mm(T[bk][:, 0:8], tab, T.Id[block(t), lo:lo + 8], True, False, [key, "Id"], [bk])
+        mm(T[bk][:, 0:8], T.E0[block(t), :], T.C2[block(t), 0:8], False, False, ["E0", "C2"], [bk])
 
     def count(ch, bk):
         mm(T[bk][:, 0:8], T["HT%d" % ch][:], T.U8[:], False, True, ["HT%d" % ch, "U8"], [bk])
 
-    def aside(ch, bk, dst, key):
-        tt(T[dst][:, LIST[ch]:LIST[ch] + 8], T[bk][:, 0:8], T.D[:, 8 * ch:8 * ch + 8], A.min, [bk, "D"], [key])
+    def aside(ch, bk):
+        tt(T.DL[:, 8 * ch:8 * ch + 8], T[bk][:, 0:8], T.D[:, 8 * ch:8 * ch + 8], A.min, [bk, "D"], ["d%d" % ch])
 
     def gain(ch):
         c = str(ch)
         tt(T["hb" + c][:], T["HT" + c][:], T["T" + c][:, 256:384], A.mult, ["HT" + c, "T" + c], ["hb" + c])
 
-    def turn_gain(ch, bk):
-        mm(T[bk][:, 0:128], T["hb%d" % ch][:], T.I32[:], True, False, ["hb%d" % ch, "I32"], [bk])
+    def turn(ch, k, w, start, stop, bk="X"):
+        c = str(ch)
+        mm(T[bk + c][:, 0:128], T[k + c][:], T[w][:], start, stop, [k + c, w], [bk + c])
 
-    def turn_own(src, key, bk):
-        mm(T[bk][:, 0:128], src, T.Id[:], False, True, [key, "Id"], [bk])
+    def as_list(ch, bk="X"):
+        act(T.OF[:, sec(ch)], T[bk + str(ch)][:, 0:128], [bk + str(ch)], ["f%d" % ch], bias=float(BIAS))
 
-    def as_list(ch, bk, dst, key):
-        act(T[dst][:, OWN[ch]:OWN[ch] + 128], T[bk][:, 0:128], [bk], [key], bias=float(BIAS))
-
-    def as_half(ch, bk, dst, key):
-        act(T[dst][:, sec(ch)], T[bk][:, 0:128], [bk], [key])
+    def as_half(ch, bk="X"):
+        act(T.OW[:, sec(ch)], T[bk + str(ch)][:, 0:128], [bk + str(ch)], ["w%d" % ch])
 
     def scatter_h(t, lo, hi):
-        h = "NH%d" % (t % 2)
-        act(T.HN[:, 0:WIN].indirect(T["OF%d" % t][:, 128 + 8 * lo:128 + 8 * hi]), T[h][:, 128 * lo:128 * hi],
-            ["d%d%d" % (t, c) for c in range(lo, hi)] + [h], HK, func=F.Silu)
+        act(T["HN%d" % (t % 2)][:, 0:WIN].indirect(T.DL[:, 8 * lo:8 * hi]), T.NH[:, 128 * lo:128 * hi],
+            ["d%d" % c for c in range(lo, hi)] + ["NH"], HK[t % 2], func=F.Silu)
 
     def scatter_w(t, lo, hi):
-        l = "lm%d" % (t % n)
-        vcopy(T.W[:, 0:WIN].indirect(T["OF%d" % t][:, 128 + 8 * lo:128 + 8 * hi]), T[l][:, 128 * lo:128 * hi],
-              ["d%d%d" % (t, c) for c in range(lo, hi)] + [l], WK + ["gate"])
+        vcopy(T["W%d" % t][:, 0:WIN].indirect(T.DL[:, 8 * lo:8 * hi]), T.lm0[:, 128 * lo:128 * hi],
+              ["d%d" % c for c in range(lo, hi)] + ["lm0"], WK[t])
+
+    def rows_of(t, buf):
+        hn = T["HN%d" % (t % 2)]
+        return [(hn[lane:128:16, 0:4096], T[buf][:, 256 * k:256 * k + 256]) for k, lane in enumerate(LANES)]
+
+    def ship_w(t, k):
+        u = t + 1
+        out, in_ = T["W%d" % u][:, SHIP[k]:SHIP[k + 1]], T["W%d" % t][:, SHIP[k]:SHIP[k + 1]]
+        if k and via is not None:
+            send(via, out, in_, "hw%d%d" % (u, k), WK[t], topo.engines(core, prv))
+        else:
+            send(prv, out, in_, "bw%d" % u, WK[t])
+
+    def ship_h(t):
+        u = t + 1
+        send(prv, T["CR%d" % u][:], T["CP%d" % u][:], "bh%d" % u, ["CP%d" % u])
+
+    def pack(t):
+        u = t + 1
+        dmas([(b, a) for a, b in rows_of(t, "CP%d" % u)], "cp%d" % u, ["CP%d" % u], HK[t % 2])
+
+    def unpack(u):
+        dmas(rows_of(u, "CR%d" % u), "xh%d" % u, HK[u % 2], ["CR%d" % u])
 
     def parts(k, lo, hi):
         return [k + "_%d" % j for j in range(lo // 8, hi // 8)]
 
-    def list_of(t, ch, p, lo, hi):
-        if p == 0:
-            return T["OF%d" % t][:, OWN[ch] + lo:OWN[ch] + hi], "f%d%d" % (t, ch)
-        return T.off[:, 128 * ch + lo:128 * ch + hi], "off%d" % ch
+    def list_of(ch, p, lo, hi):
+        k = ("OF", "off")[p]
+        return T[k][:, 128 * ch + lo:128 * ch + hi], ("f%d", "off%d")[p] % ch
 
     def gv(t, ch, p, lo, hi):
-        m, l = "M%d" % ch, "lr%d" % (t % n)
-        lst, key = list_of(t, ch, p, lo, hi)
-        op("v", lambda: g.vector.tensor_tensor(out=T[m][:, 16 * lo:16 * hi], in0=T.W[:, 0:4096].indirect(lst),
-                                               in1=T[l][:, 2048 * ch + 16 * lo:2048 * ch + 16 * hi], op=A.max),
-           WK + [key, l + str(ch)], parts(m, lo, hi))
+        m = "M%d" % ch
+        lst, key = list_of(ch, p, lo, hi)
+        op("v", lambda: g.vector.tensor_tensor(out=T[m][:, 16 * lo:16 * hi], in0=T["W%d" % t][:, 0:4096].indirect(lst),
+                                               in1=T.lr[:, 2048 * ch + 16 * lo:2048 * ch + 16 * hi], op=A.max),
+           WK[t] + [key, "lr%d" % ch], parts(m, lo, hi))
 
     def gs(t, ch, p, lo, hi):
         h = "H%d" % ch
-        lst, key = list_of(t, ch, p, lo, hi)
-        act(T[h][:, 16 * lo:16 * hi], T.HN[:, 0:4096].indirect(lst), HK + [key, "gb"], parts(h, lo, hi), func=F.Identity, bias=T.gb[:])
+        lst, key = list_of(ch, p, lo, hi)
+        act(T[h][:, 16 * lo:16 * hi], T["HN%d" % (t % 2)][:, 0:4096].indirect(lst), HK[t % 2] + [key, "gb"], parts(h, lo, hi),
+            func=F.Identity, bias=T.gb[:])
 
     def init(t, ch):
-        c, ls, o = str(ch), "Ls%d" % (t % n), "w%d%d" % (t, ch)
-        own = T["OW%d" % t][:, sec(ch)]
+        c, o = str(ch), "w%d" % ch
+        own = T.OW[:, sec(ch)]
         for bk in ("X" + c, "Y" + c):
-            mm(T[bk][:, 0:128], T["E" + c][:], T.Ls[:, sec(t % n)], True, False, ["E" + c, ls], [bk])
+            mm(T[bk][:, 0:128], T["E" + c][0:16, :], T.Ls[:], True, False, ["E" + c, "Ls"], [bk])
         mm(T["X" + c][:, 256:384], T.Z[:], T.Z[:], False, False, ["Z"], ["X" + c])
         mm(T["X" + c][:, 128:256], own, T.HI[:], False, False, [o, "HI"], ["X" + c])
-        mm(T["T" + c][:, 0:128], own, T.HI[:], True, False, [o, "HI"], ["T" + c])
+        if t == R - 1:
+            mm(T["T" + c][:, 0:128], own, T.HI[:], True, False, [o, "HI"], ["T" + c])
+            mm(T["T" + c][:, 0:128], T.E0[0:16, :], T.C2[0:16, :], False, False, ["E0", "C2"], ["T" + c])
+        else:
+            mm(T["T" + c][:, 128:256], own, T.HI[:], True, False, [o, "HI"], ["T" + c])
 
     def init_deeds(t, ch):
-        c = str(ch)
-        mm(T["T" + c][:, 128:256], T["OW%d" % t][:, sec(ch)], T.HI[:], False, False, ["w%d%d" % (t, ch), "HI"], ["T" + c])
-        mm(T["T" + c][:, 128:256], T["nE" + c][:], T.aT[:, 256 * t + 256:256 * t + 384], False, False, ["nE" + c, "aT%d" % (t + 1)], ["T" + c])
+        spread(T["T%d" % ch][:, 128:256], t + 1, ch, 0, "nE", False, False)
         gain_t(t + 1, ch, False)
 
     def sums_h(ch, p, lo=0, hi=128, stop=True):
@@ -412,12 +436,16 @@ def rank_program(g, core, T, topo):
         ts(T.off[:, sec(ch)], T.P[:, sec(ch)], BIAS, A.add, ["P"], ["off" + c])
         tt(T["ta" + c][:], T["SA" + c][:], T["X" + c][:, 128:256], A.mult, ["SA" + c, "X" + c], ["ta" + c])
 
-    def first_t(ch, regions):
+    def first_t(ch, last):
         c = str(ch)
+        lo = 0 if last else 128
         mm(T["Y" + c][:, 0:128], T.BI[:], T["SA" + c][:], False, False, ["SA" + c, "BI"], ["Y" + c])
-        for k in range(regions):
-            mm(T["T" + c][:, sec(k)], T.HI[:], T["hT" + c][:], False, False, ["hT" + c, "HI"], ["T" + c])
-            mm(T["T" + c][:, sec(k)], T.nI32[:], T["ta" + c][:], False, k == regions - 1, ["ta" + c, "nI32"], ["T" + c])
+        mm(T["T" + c][:, lo:lo + 128], T.HI[:], T["hT" + c][:], False, False, ["hT" + c, "HI"], ["T" + c])
+        mm(T["T" + c][:, lo:lo + 128], T.nI32[:], T["ta" + c][:], False, True, ["ta" + c, "nI32"], ["T" + c])
+        if not last:
+            mm(T["X" + c][:, 0:128], T.HI[:], T.OW[:, sec(ch)], True, False, ["w" + c, "HI"], ["X" + c])
+            turn(ch, "hT", "HI", False, False)
+            turn(ch, "ta", "nI32", False, False)
 
     def near(ch):
         ts(T["SB%d" % ch][:], T["Y%d" % ch][:, 0:128], TH - FAR, A.is_le, ["Y%d" % ch], ["SB%d" % ch], 2.0, A.mult)
@@ -430,9 +458,13 @@ def rank_program(g, core, T, topo):
         c = str(ch)
         tt(T["HT" + c][:], T["T" + c][:, 128:256], T["tb" + c][:], A.is_equal, ["T" + c, "tb" + c], ["HT" + c])
 
-    def result(ch, out, key):
+    def result(ch):
         c = str(ch)
-        tt(out, T["T" + c][:, 0:128], T["tb" + c][:], A.subtract, ["T" + c, "tb" + c], [key])
+        tt(T.yof[:, sec(ch)], T["T" + c][:, 0:128], T["tb" + c][:], A.subtract, ["T" + c, "tb" + c], ["yof" + c])
+
+    def owners(ch):
+        turn(ch, "tb", "nI32", False, False)
+        turn(ch, "hb", "I32", False, True)
 
     def store_yo(ch):
         for k in range(8):
@@ -448,40 +480,41 @@ def rank_program(g, core, T, topo):
         count(ch, "L")
 
     def turn0(ch):
-        turn_gain(ch, "T%d" % ch)
-        turn_own(T.ownH[:, sec(ch)], "ownH%d" % ch, "T%d" % ch)
+        turn(ch, "hb", "I32", True, False, "T")
+        mm(T["T%d" % ch][:, 0:128], T.ownH[:, sec(ch)], T.Id[:], False, True, ["ownH%d" % ch, "Id"], ["T%d" % ch])
 
+    fill_h(0)
     x_heir(0)
     x_heir(1)
-    indices(0)
-    mm(T.L[:, 0:8], T.E0[:], T.Id[0:16, 0:8], True, True, ["E0", "Id"], ["L"])
+    act(T.TB0[:], T.TI[:], ["TI", "fs", "fb"], ["TB0"], func=F.Identity, scale=T.fs[:], bias=T.fb[:])
+    mm(T.L[:, 0:8], T.E0[0:16, :], T.Id[0:16, 0:8], True, True, ["E0", "Id"], ["L"])
     small_t(0, "T0")
-    sum_t(0, "T1")
+    for r in range(16):
+        mm(T.T1[0:16, 256 + r:384:16], T.lm0[:, r:256:16], T.nB8[:], r == 0, r == 15, ["lm0", "nB8"], ["T1"])
     x_heir(2)
     x_heir(3)
-    act(T.cb2[:], T.OH[:, 0:1], ["OH", "cb1"], ["cb2"], func=F.Identity, scale=-16384.0, bias=T.cb1[:])
-    small_out(0, "T0")
-    act(T.cb3[:], T.OH[:, 1:2], ["OH", "cb2"], ["cb3"], func=F.Identity, scale=16.0 * (2048 + 16384 + 16), bias=T.cb2[:])
+    act(T.cb2[:], T.OH[:, 0:1], ["OH", "cb1"], ["cb2"], func=F.Identity, scale=-7168.0, bias=T.cb1[:])
+    act(T.aT0[:], T.T0[0:16, 0:256], ["T0"], ["aT0"])
+    act(T.cb3[:], T.OH[:, 1:2], ["OH", "cb2"], ["cb3"], func=F.Identity, scale=8.0 * (2048 + 32768 + 144), bias=T.cb2[:])
     act(T.U8[:], T.L[:, 0:8], ["L"], ["U8"], scale=8192.0)
-    act(T.cb[:], T.OH[:, 2:3], ["OH", "cb3"], ["cb"], func=F.Identity, scale=2064.0, bias=T.cb3[:])
-    sum_out(0, "T1")
+    act(T.cb[:], T.OH[:, 2:3], ["OH", "cb3"], ["cb"], func=F.Identity, scale=1024.0, bias=T.cb3[:])
+    act(T.Ls[:], T.T1[0:16, 256:384], ["T1"], ["Ls"], bias=float(BIAS))
     double(0)
     double(1)
-    ts(T.wh[:], T.OH[:, 2:3], -1.0, A.mult, ["OH", "wh1"], ["wh"], T.wh1[:], A.add)
-    ts(T.gb[:], T.wN[:], -272.0, A.mult, ["wN"], ["gb"])
+    ts(T.wh[:], T.OH[:, 2:3], -6288.0 / 4096, A.mult, ["OH", "wh1"], ["wh"], T.wh1[:], A.add)
+    ts(T.gb[:], T.OH[:, 3:4], -2064.0, A.mult, ["OH"], ["gb"])
     double(2)
     ts(T.RM[:], T.nB8[:], -2.0, A.mult, ["nB8"], ["RM"])
-    for k, (w, val) in enumerate((("wN", 1.0), ("wh", 0.5), ("wh", -1.0))):
-        ts(T.RH[:, 8 * k:8 * k + 8], T.nB8[:], T[w][:], A.mult, ["nB8", w], ["RH%d" % k], val, A.mult)
-    send(prv, T.PR[:], T.PK[:], "pk", "PK")
+    for k, (w, key, val) in enumerate(((T.OH[:, 3:4], "OH", 1.0), (T.wh[:], "wh", 2.0), (T.wh[:], "wh", -4.0))):
+        ts(T.RH[:, 8 * k:8 * k + 8], T.nB8[:], w, A.mult, ["nB8", key], ["RH%d" % k], val, A.mult)
     for t in range(1, n):
-        send(T.cores[(rank + t) % n], T["lm%d" % t][:], T.lm0[:], "l%d" % t, "lm0")
-    for k, val in (("HI", 0.5), ("Ih", 1.0), ("BI", -FAR), ("nI32", -1.0), ("I16", 1.0 / 16)):
+        send(T.cores[(rank - t) % n], T["TB%d" % t][:], T.TB0[:], "tb%d" % t, ["TB0"])
+    for k, val in (("HI", 0.5), ("Ih", 1.0), ("BI", -FAR), ("nI32", -1.0)):
         diagonal(k, val)
     for k in (0, 1, 2):
         x_book(k)
     for ch in (0, 1):
-        mm(T["T%d" % ch][:, 128:256], T["E%d" % ch][:], T.aT[:, 0:128], True, False, ["E%d" % ch, "aT0"], ["T%d" % ch])
+        spread(T["T%d" % ch][:, 128:256], 0, ch, 0, "E", True, False)
         gain_t(0, ch, True)
     prep_nh_t(0)
     x_copy(0)
@@ -489,7 +522,7 @@ def rank_program(g, core, T, topo):
     x_copy(1)
     x_copy(2)
     own0(0)
-    prep_nh_s(0)
+    prep_nh_s()
     x_heir(4)
     x_book(3)
     x_heir(5)
@@ -498,7 +531,7 @@ def rank_program(g, core, T, topo):
     x_copy(3)
     double(4)
     gain(0)
-    aside(0, "L", "OF0", "d00")
+    aside(0, "L")
     x_heir(6)
     x_book(5)
     x_heir(7)
@@ -510,40 +543,54 @@ def rank_program(g, core, T, topo):
     x_book(6)
     x_book(7)
     gain(1)
-    aside(1, "L", "OF0", "d01")
+    aside(1, "L")
     turn0(1)
-    as_list(0, "T0", "OF0", "f00")
-    as_half(0, "T0", "OW0", "w00")
+    as_list(0, "T")
+    as_half(0, "T")
     x_copy(6)
     x_copy(7)
     scatter_w(0, 0, 2)
     scatter_h(0, 0, 2)
-    ts(T.OF0[:, OWN[1]:OWN[1] + 128], T.T1[:, 0:128], float(BIAS), A.add, ["T1"], ["f01"])
-    vcopy(T.OW0[:, sec(1)], T.T1[:, 0:128], ["T1"], ["w01"])
+    ts(T.OF[:, sec(1)], T.T1[:, 0:128], float(BIAS), A.add, ["T1"], ["f1"])
+    vcopy(T.OW[:, sec(1)], T.T1[:, 0:128], ["T1"], ["w1"])
 
     for t in range(R):
         last = t == R - 1
         u = t + 1
-        if u < n:
-            repeat(u, T["lm%d" % u], (0, 1), ["lm%d" % u, "gate"])
-        gv(t, 0, 0, 0, 128)
-        gs(t, 0, 0, 0, 128)
-        if t == 0:
-            indices(1)
-        init(t, 0)
-        init(t, 1)
         if last:
             for k, lane in (("yha", 0), ("yhb", 1)):
-                op("p", lambda: g.dma_start(out=T[k][:], in_=T.HN[lane:128:16, 0:4096]), HK, ["yhab" if lane else "yha0"], "d_yh", 16)
-            store("y", T.yd[:], T.W[:, 0:4096], WK)
+                op("p", lambda: g.dma_start(out=T[k][:], in_=T.HN0[lane:128:16, 0:4096]), HK[0], ["yhab" if lane else "yha0"], "d_yh", 16)
+            store("y", T.yd[:], T["W%d" % t][:, 0:4096], WK[t])
+        else:
+            pack(t)
+            if t == 0:
+                fill_h(1)
+            ship_h(t)
+            for k in (1, 2, 0, 3):
+                ship_w(t, k)
+            if t == 0:
+                fill_h(2)
+                diagonal("I4", 4.0)
+                diagonal("I8", 1.0 / 8)
+            unpack(u)
+        gv(t, 0, 0, 0, 128)
+        if t:
+            gs(t, 0, 0, 0, S0)
+            as_list(1)
+            as_half(1)
+            gs(t, 0, 0, S0, 128)
+        else:
+            gs(t, 0, 0, 0, 128)
+        init(t, 0)
+        init(t, 1)
         sums_m(0, 0)
         sums_h(0, 0)
         if t == 0:
-            small_t(1, "L")
-        elif last:
-            for ch in (0, 1):
-                mm(T["T%d" % ch][:, 0:128], T.E0[:], T.C2[:], False, False, ["E0", "C2"], ["T%d" % ch])
-        else:
+            mm(T.L[:, 0:256], T.Z[:], T.TB0[:], True, False, ["Z", "TB0"], ["L"])
+            for k in range(1, R):
+                small_t(k, "L")
+            mm(T.L[:, 256:320], T.Z[:], T.Z[:, 0:64], False, True, ["Z"], ["L"])
+        elif not last:
             init_deeds(t, 0)
             init_deeds(t, 1)
             prep_nh_t(u)
@@ -551,7 +598,7 @@ def rank_program(g, core, T, topo):
         gs(t, 1, 0, 0, SS)
         heirs(0)
         if t == 0:
-            small_out(1, "L")
+            act(T.aTA[:], T.L[:, 0:256], ["L"], ["aTA"])
         gs(t, 1, 0, SS, 128)
         first(0)
         sums_m(1, 0)
@@ -560,10 +607,10 @@ def rank_program(g, core, T, topo):
             init_deeds(t, 0)
             init_deeds(t, 1)
             prep_nh_t(u)
-        first_t(0, 1 if last else 2)
+        first_t(0, last)
         if last:
-            mm(T.L[:, 0:256], T.Id[:], T.yha[:], True, False, ["Id", "yhab"], ["L"])
-            mm(T.L[:, 0:256], T.I16[:], T.yhb[:], False, True, ["I16", "yhab"], ["L"])
+            mm(T.L[:, 0:256], T.I4[:], T.yha[:], True, False, ["I4", "yhab"], ["L"])
+            mm(T.L[:, 0:256], T.I8[:], T.yhb[:], False, True, ["I8", "yhab"], ["L"])
         gv(t, 0, 1, 0, 128)
         gs(t, 0, 1, 0, SS)
         heirs(1)
@@ -571,80 +618,54 @@ def rank_program(g, core, T, topo):
         first(1)
         sums_m(0, 1)
         sums_h(0, 1)
-        first_t(1, 1 if last else 2)
+        first_t(1, last)
         gs(t, 1, 1, 0, 96)
         gs(t, 1, 1, 96, 128)
         gv(t, 1, 1, 0, 64)
         near(0)
+        gv(t, 1, 1, 64, 80)
+        second(0)
+        gv(t, 1, 1, 80, 96)
         if last:
-            gv(t, 1, 1, 64, 80)
-            second(0)
-            gv(t, 1, 1, 80, 96)
-            result(0, T.yof[:, 0:128], "yof0")
+            result(0)
             store_yo(0)
         else:
-            gv(t, 1, 1, 64, 96)
+            hit(0)
+            gain(0)
         gv(t, 1, 1, 96, 128)
         sums_m(1, 1, 0, 64)
         sums_m(1, 1, 64, 96)
+        if not last:
+            places(u, 0, "Y0")
+            count(0, "Y0")
         sums_h(1, 1, 0, 96)
         sums_h(1, 1, 96, 128, False)
         sums_m(1, 1, 96, 128, True)
         if last:
-            act(T.yhf[:], T.L[:, 0:256], ["L"], ["yhf"], bias=-16.0)
+            act(T.yhf[:], T.L[:, 0:256], ["L"], ["yhf"], bias=-4240.0)
             store("y", T.yh[:], T.yhf[:], ["yhf"])
             near(1)
             second(1)
-            result(1, T.yof[:, 128:256], "yof1")
+            result(1)
             store_yo(1)
             break
-        sf, sw, of, ow = "SF%d" % u, "SW%d" % u, "OF%d" % u, "OW%d" % u
-
-        def pass_on(k, ch):
-            out, in_, lo, w = (ow, sw, 128 * ch, 128) if k == "w" else (of, sf, OWN[ch], 128) if k == "f" else (of, sf, LIST[ch], 8)
-            send(nxt, T[out][:, lo:lo + w], T[in_][:, lo:lo + w], "%s%d%d" % (k, u, ch), "s%s%d%d" % (k, u, ch))
-
-        prep_nh_s(u)
-        places(u, 0, "L")
-        second(0)
+        prep_nh_s()
+        aside(0, "Y0")
+        owners(0)
         places(u, 1, "Y0")
-        hit(0)
-        count(0, "L")
-        gain(0)
-        turn_gain(0, "X0")
+        scatter_h(u, 0, 1)
+        scatter_w(u, 0, 1)
         near(1)
-        aside(0, "L", sf, "sd%d0" % u)
-        pass_on("d", 0)
         second(1)
-        result(0, T.SD0[:], "SD0")
-        turn_own(T.SD0[:], "SD0", "X0")
+        as_list(0)
+        as_half(0)
         hit(1)
         count(1, "Y0")
-        as_list(0, "X0", sf, "sf%d0" % u)
-        aside(1, "Y0", sf, "sd%d1" % u)
-        pass_on("d", 1)
-        pass_on("f", 0)
         gain(1)
-        turn_gain(1, "X1")
-        result(1, T.SD1[:], "SD1")
-        turn_own(T.SD1[:], "SD1", "X1")
-        as_half(0, "X0", sw, "sw%d0" % u)
-        as_list(1, "X1", sf, "sf%d1" % u)
-        as_half(1, "X1", sw, "sw%d1" % u)
-        pass_on("w", 0)
-        pass_on("f", 1)
-        pass_on("w", 1)
-        if u + 1 < R:
-            indices(u + 1)
-        if u < n:
-            sum_t(u, "Y1")
-            sum_out(u, "Y1")
-        if u + 1 < R:
-            small_t(u + 1, "Y0")
-            small_out(u + 1, "Y0")
-        for ch in (0, 1):
-            scatter_w(u, ch, ch + 1)
-            scatter_h(u, ch, ch + 1)
+        owners(1)
+        aside(1, "Y0")
+        scatter_w(u, 1, 2)
+        scatter_h(u, 1, 2)
 
     g.sync.wait_ge(T.sem.dout, cnt["dout"])
     wait("p", {s: c for s, c in cnt.items() if s != "dout"})

from concourse.mybir import AluOpType as A, ActivationFunctionType as F

BIAS = 2048
TH = 136.5 + 4096
FAR = 256.0
R = 5
WIN = 6144
SS = 64
S0 = 64
VCOPY = (1, 4, 6)
PIECE = (0, 1536, 2560, 3584, 4096)
LANES = (0, 1, 3)
FILL = (0, 2048, 3072, 4096)
SHIP = (0, 1280, 2304, 3328, 4096)

SCRATCH = {}
SEMAPHORES = ["v", "s", "t", "p", "loc", "dout"]


def _buf(name, cols, dtype, where="sbuf", rows=128):
    SCRATCH[name] = (where, [rows, cols], dtype)


for _n, _c in (("pi", 1), ("p15i", 1), ("p31i", 1), ("gi", 8), ("g4i", 8), ("ownI", 256), ("TI", 256)):
    _buf(_n, _c, "int32")
_buf("heirI", 512, "int32", rows=64)
for _n in ("p15", "p31", "wh", "wh1", "cb", "cb1", "cb2", "cb3", "gb", "e80", "fs", "fb"):
    _buf(_n, 1, "float32")
for _n, _c in (("dv", 128), ("i4", 4), ("nB8", 8), ("U8", 8), ("WN", 128), ("WH", 1024), ("EN", 640), ("Id", 128), ("HI", 128), ("BI", 128),
               ("I8", 128), ("I4", 128), ("Z", 128), ("RM", 8), ("yha", 256), ("yhb", 256), ("M0", 2048), ("M1", 2048), ("lm0", 256), ("lr", 4096),
               ("HT0", 128), ("HT1", 128), ("SA0", 128), ("SA1", 128), ("SB0", 128), ("SB1", 128),
               ("ev", 128), ("E0", 128), ("E1", 128), ("nE0", 128), ("nE1", 128)):
    _buf(_n, _c, "bfloat16")
_buf("C2", 128, "bfloat16")
_buf("aT0", 256, "float16", rows=16)
_buf("Ls", 128, "float16", rows=16)
for _n, _c in (("Hs", 512), ("Ih", 128), ("ownH", 256), ("hT0", 128), ("hT1", 128), ("H0", 2048), ("H1", 2048), ("RH", 24),
               ("aTA", 256), ("OW", 256)):
    _buf(_n, _c, "float16")
for _n, _c in (("HN0", WIN), ("HN1", WIN), ("NH", 256), ("OH", 4), ("I32", 128), ("nI32", 128), ("D", 16),
               ("hb0", 128), ("hb1", 128), ("ta0", 128), ("ta1", 128), ("tb0", 128), ("tb1", 128), ("yof", 256), ("yhf", 256)):
    _buf(_n, _c, "float32")
for _n, _c in (("off", 256), ("OF", 256), ("DL", 16)):
    _buf(_n, _c, "uint16")
for _t in range(5):
    _buf("W%d" % _t, WIN, "bfloat16")
    if _t:
        _buf("CP%d" % _t, 768, "float32")
        _buf("CR%d" % _t, 768, "float32")
        SEMAPHORES.extend("%s%d" % (_k, _t) for _k in ("bw", "bh", "cp", "xh"))
        SEMAPHORES.extend("hw%d%d" % (_t, _k) for _k in range(1, len(SHIP) - 1))
for _t in range(4):
    _buf("TB%d" % _t, 256, "float16")
    if _t:
        SEMAPHORES.append("tb%d" % _t)
for _n in ("own0", "own1", "lm", "heir", "ti", "yh", "bk0", "bk1", "bk2", "bk3", "ra", "rb"):
    SEMAPHORES.append("d_" + _n)
BANKS = ["X0", "X1", "Y0", "Y1", "T0", "T1", "L", "P"]
for _n in BANKS:
    _buf(_n, 512, "float16" if _n == "P" else "float32", "psum")


def helper_of(src, dst, T, topo):
    if topo.chip(src) == topo.chip(dst):
        return None
    return [c for c in topo.cores_of(src) if T.rank_of(c) is None and topo.die(c) != topo.die(src) and topo.may_write(c, dst)][0]


def hand_on(g, core, dst, src, T, topo):
    rid, pid, _ = topo.addr(dst)
    spare = len(topo.engines(src, core)) - len(topo.engines(src, dst))
    for u in range(1, R):
        for k in range(1, len(SHIP) - 1):
            piece = T["W%d" % u][:, SHIP[k]:SHIP[k + 1]]
            g.wait_ge(T.sem["hw%d%d" % (u, k)], spare)
            g.remote_dma(piece, piece, T.sem["bw%d" % u], T.sem.loc, pid, rid, topo.mask(core, dst))
    g.wait_ge(T.sem.loc, (R - 1) * (len(SHIP) - 2) * len(topo.engines(core, dst)))


def rank_program(g, core, T, topo):
    rank = T.rank_of(core)
    n = len(T.cores)
    if rank is None:
        for r in range(n):
            if helper_of(T.cores[r], T.cores[r - 1], T, topo) == core:
                hand_on(g, core, T.cores[r - 1], T.cores[r], T, topo)
        return
    eng = {"v": g.vector, "s": g.scalar, "t": g.tensor, "p": g, "y": g.sync}
    know = {q: {} for q in eng}
    cnt = {}
    snap = {}
    wr, rd, acc = {}, {}, {}

    def wait(q, deps):
        todo = {s: c for s, c in deps.items() if know[q].get(s, 0) < c}
        for s, c in sorted(todo.items()):
            if any(o != s and snap.get((o, oc), {}).get(s, 0) >= c for o, oc in todo.items()):
                continue
            eng[q].wait_ge(T.sem[s], c)
        for s, c in todo.items():
            for s2, c2 in snap.get((s, c), {}).items():
                know[q][s2] = max(know[q].get(s2, 0), c2)
            know[q][s] = max(know[q].get(s, 0), c)

    def deps_of(q, reads, writes):
        d = {}

        def put(src, skip=None):
            for s, c in src.items():
                if s != skip:
                    d[s] = max(d.get(s, 0), c)
        for k in list(reads) + list(writes):
            if k in BANKS:
                put(acc.get(k, {}), q)
            else:
                put(wr.get(k, {}))
        for k in writes:
            if k not in BANKS:
                put(rd.get(k, {}))
        return d

    def note(q, sem, inc, reads, writes):
        cnt[sem] = cnt.get(sem, 0) + inc
        c = cnt[sem]
        snap[(sem, c)] = dict(know[q])
        for k in list(reads) + list(writes):
            if k in BANKS:
                acc.setdefault(k, {})[sem] = c
        for k in reads:
            if k not in BANKS:
                rd.setdefault(k, {})[sem] = c
        for k in writes:
            if k not in BANKS:
                wr[k] = {sem: c}
                rd[k] = {}

    def op(q, fn, reads, writes, sem=None, inc=1):
        wait(q, deps_of(q, reads, writes))
        sem = sem or q
        fn().then_inc(T.sem[sem], inc)
        note(q, sem, inc, reads, writes)

    def ts(out, in0, s1, op0, reads, writes, s2=None, op1=None):
        if op1 is None:
            op("v", lambda: g.vector.tensor_scalar(out=out, in0=in0, scalar1=s1, scalar2=None, op0=op0), reads, writes)
        else:
            op("v", lambda: g.vector.tensor_scalar(out=out, in0=in0, scalar1=s1, scalar2=s2, op0=op0, op1=op1), reads, writes)

    def tt(out, in0, in1, o, reads, writes):
        op("v", lambda: g.vector.tensor_tensor(out=out, in0=in0, in1=in1, op=o), reads, writes)

    def vcopy(out, in_, reads, writes):
        op("v", lambda: g.vector.tensor_copy(out=out, in_=in_), reads, writes)

    def fill(ap, key, value):
        op("v", lambda: g.vector.memset(ap, value), [], [key])

    def act(out, in_, reads, writes, func=F.Copy, **kw):
        op("s", lambda: g.scalar.activation(out=out, in_=in_, func=func, **kw), reads, writes)

    def mm(out, lhsT, rhs, start, stop, reads, writes):
        op("t", lambda: g.tensor.matmul(out=out, lhsT=lhsT, rhs=rhs, start=start, stop=stop), reads, writes)

    def dmas(pairs, sem, writes, reads=(), q="y"):
        wait(q, deps_of(q, reads, writes))
        for out, in_ in pairs:
            eng[q].dma_start(out=out, in_=in_).then_inc(T.sem[sem], 16)
        note(q, sem, 16 * len(pairs), reads, writes)

    def store(q, out, in_, reads):
        op(q, lambda: eng[q].dma_start(out=out, in_=in_), reads, [], "dout", 16)

    def iota(ap, key, pattern, base, cm, small=True):
        op("p", lambda: g.iota(ap, pattern, base, cm, allow_small_or_imprecise_dtypes=True) if small
           else g.iota(ap, pattern, base, cm), [], [key])

    def mark(ap, key, pattern, base, value, whole):
        op("p", lambda: g.affine_select(ap, ap, pattern, A.not_equal, value, base, 1), [key] + whole, [key])

    def diagonal(k, value):
        op("p", lambda: g.affine_select(T[k][:], T.Z[:], [[-1, 128]], A.not_equal, value, 0, 1), ["Z"], [k])

    def send(dst, out, in_, sem, keys, without=()):
        wait("p", deps_of("p", keys, []))
        rid, pid, _ = topo.addr(dst)
        use = [e for e in topo.engines(core, dst) if e not in without]
        g.remote_dma(out, in_, T.sem[sem], T.sem.loc, pid, rid, sum(1 << e for e in use))
        cnt["loc"] = cnt.get("loc", 0) + len(use)

    def arrive(sem, key, src, writes=1):
        cnt[sem] = writes * len(topo.engines(src, core))
        wr[key] = {sem: cnt[sem]}
        rd[key] = {}

    nxt = T.cores[(rank + 1) % n]
    prv = T.cores[(rank - 1) % n]
    via = helper_of(core, prv, T, topo)
    for t in range(1, n):
        arrive("tb%d" % t, "TB%d" % t, T.cores[(rank + t) % n])
    for t in range(1, R):
        arrive("bw%d" % t, "W%d" % t, nxt, len(SHIP) - 1)
        arrive("bh%d" % t, "CR%d" % t, nxt)
    WK = [["Wk%d" % k for k in range(4)]] + [["W%d" % t] for t in range(1, R)]
    HK = [["HA%d" % k for k in range(8)], ["HB%d" % k for k in range(len(FILL) - 1)]]

    def sec(ch):
        return slice(128 * ch, 128 * ch + 128)

    def book_in(k):
        dmas([(T.W0[:, PIECE[k]:PIECE[k + 1]], T.bk[:, PIECE[k]:PIECE[k + 1]])], "d_bk%d" % k, ["Wk%d" % k])

    def own_in(ch):
        dmas([(T.ownI[:, 128 * ch + 16 * k:128 * ch + 16 * k + 16], T.own[16 * k:16 * k + 16, sec(ch)]) for k in range(8)],
             "d_own%d" % ch, ["ownI%d" % ch])

    dmas([(T.heirI[:], T.heir[:])], "d_heir", ["heirI"])
    dmas([(T.lm0[:], T.lm[:])], "d_lm", ["lm0"])
    dmas([(T.TI[0:40, :], T.da[:]), (T.TI[40:80, :], T.db[:]), (T.TI[80:120, :], T.db[:]), (T.TI[120:128, :], T.db[:, 0:256])], "d_ti", ["TI"])
    book_in(0)
    book_in(1)
    own_in(0)
    book_in(2)
    book_in(3)
    own_in(1)
    dmas([(T.lr[:, 2048 + 128 * q:2048 + 128 * q + 128], T.lm[:, sec(1)]) for q in range(4)], "d_ra", ["lra"])
    dmas([(T.lr[:, 2048 + 512 * k:2048 + 512 * k + 512], T.lr[:, 2048:2560]) for k in (1, 2, 3)], "d_rb", ["lr1"], ["lra"])

    iota(T.pi[:], "pi", [[0, 1]], 0, 1, False)
    iota(T.gi[:], "gi", [[-16, 8]], 0, 1, False)
    iota(T.i4[:], "i4", [[1, 4]], 0, 0)
    fill(T.Z[:], "Z", 0.0)
    fill(T.WH[:], "WH", 0.0)
    fill(T.EN[:, 128:640], "ENb", 0.0)
    fill(T.C2[:], "C2", float(BIAS))
    act(T.EN[:, 0:128], T.Z[:], ["Z"], ["ENa"], func=F.Silu)
    mark(T.WH[:, 0:1024:16], "WH0", [[-1, 8], [-8, 8]], -64, 8.0, ["WH"])
    mark(T.WH[:, 1:1024:16], "WH1", [[-1, 8], [-8, 8]], 0, 8.0, ["WH"])
    iota(T.dv[:], "dv", [[1, 128]], 0, -1)
    mark(T.WH[:, 1:1024:16], "WH1", [[-1, 8], [-8, 8]], -64, -256.0, ["WH"])
    iota(T.ev[:], "ev", [[0, 16], [1, 8]], 0, 0)
    mark(T.EN[:, 0:640:16], "EN0", [[-1, 5], [-5, 8]], -80, 8.0, ["ENa", "ENb"])
    mark(T.EN[:, 1:640:16], "EN1", [[-1, 5], [-5, 8]], -40, 8.0, ["ENa", "ENb"])
    iota(T.D[:], "D", [[1, 16]], 4096, 16)
    mark(T.EN[:, 1:640:16], "EN1", [[-1, 5], [-5, 8]], -80, -256.0, ["ENa", "ENb"])
    diagonal("I32", 1.0)

    ts(T.p15i[:], T.pi[:], 15, A.bitwise_and, ["pi"], ["p15i"])
    ts(T.e80[:], T.pi[:], 80.0, A.is_ge, ["pi"], ["e80"])
    ts(T.g4i[:], T.gi[:], 4, A.arith_shift_right, ["gi"], ["g4i"])
    ts(T.p31i[:], T.pi[:], 31, A.bitwise_and, ["pi"], ["p31i"])
    vcopy(T.p15[:], T.p15i[:], ["p15i"], ["p15"])
    ts(T.fs[:], T.e80[:], -31.0 / 32, A.mult, ["e80"], ["fs"], 1.0, A.add)
    ts(T.fb[:], T.e80[:], 3072.0, A.mult, ["e80"], ["fb"], -2048.0, A.add)
    ts(T.OH[:], T.i4[:], T.p15[:], A.is_equal, ["i4", "p15"], ["OH"])
    vcopy(T.p31[:], T.p31i[:], ["p31i"], ["p31"])
    ts(T.Hs[0:64, :], T.heirI[:], BIAS, A.subtract, ["heirI"], ["Hs0"])
    act(T.Hs[64:128, :], T.heirI[:], ["heirI"], ["Hs1"], scale=1.0 / 32, bias=1024.0)
    ts(T.Id[:], T.dv[:], 0.0, A.is_equal, ["dv"], ["Id"])
    ts(T.nB8[:], T.g4i[:], 0.0, A.is_equal, ["g4i"], ["nB8"], -1.0, A.mult)
    ts(T.cb1[:], T.OH[:, 3:4], 16.0, A.mult, ["OH"], ["cb1"])
    ts(T.WN[:], T.dv[:], T.p15[:], A.add, ["dv", "p15"], ["WN"], 3.0, A.is_equal)
    for ch in (0, 1):
        ts(T["E%d" % ch][:], T.ev[:], T.p31[:], A.subtract, ["ev", "p31"], ["E%d" % ch], -8.0 * ch, A.is_equal)
    for ch in (0, 1):
        ts(T["nE%d" % ch][:], T["E%d" % ch][:], -1.0, A.mult, ["E%d" % ch], ["nE%d" % ch])
    ts(T.wh1[:], T.OH[:, 1:2], 1.0 / 32, A.mult, ["OH"], ["wh1"], T.OH[:, 0:1], A.add)

    XB = ("Y0", "Y1", "X0", "X1")

    def x_heir(k):
        mm(T[XB[k % 4]][:], T.WH[:, 128 * k:128 * k + 128], T.Hs[:], True, False, ["WH0", "WH1", "Hs0", "Hs1"], [XB[k % 4]])

    def x_book(k):
        wk = [WK[0][j] for j in range(4) if PIECE[j] < 512 * k + 512 and PIECE[j + 1] > 512 * k]
        mm(T[XB[k % 4]][:], T.WN[:], T.W0[:, 512 * k:512 * k + 512], False, True, ["WN"] + wk, [XB[k % 4]])

    def x_copy(k):
        bk = XB[k % 4]
        if k in VCOPY:
            ts(T.HN0[:, 512 * k:512 * k + 512], T[bk][:], T.cb[:], A.add, [bk, "cb"], ["HA%d" % k])
        else:
            act(T.HN0[:, 512 * k:512 * k + 512], T[bk][:], [bk, "cb"], ["HA%d" % k], func=F.Identity, bias=T.cb[:])

    def fill_h(k):
        iota(T.HN1[:, FILL[k]:FILL[k + 1]], "HB%d" % k, [[0, FILL[k + 1] - FILL[k]]], 1024, 0)

    def double(k):
        w = 64 * 2 ** k
        if k < 2:
            vcopy(T.lr[:, sec(k)], T.lm0[:, 0:128], ["lm0"], ["lr.%d" % k])
        else:
            vcopy(T.lr[:, w:2 * w], T.lr[:, 0:w], ["lr.%d" % j for j in range(k)], ["lr0" if k == 4 else "lr.%d" % k])

    def block(t):
        return slice(32 * (t - 1), 32 * (t - 1) + 16) if t else slice(0, 16)

    def table(t, k):
        return T["aTA" if t else "aT0"][block(t), sec(k)], "aTA" if t else "aT0"

    def small_t(t, bk):
        tb = "TB%d" % (t % n)
        for r in range(16):
            mm(T[bk][block(t), r:256:16], T[tb][:, r:256:16], T.Id[:, t:80:5], t == 0 and r == 0, t == 0 and r == 15, [tb, "Id"], [bk])

    def prep_nh_t(t):
        tb = "TB%d" % (t % n)
        mm(T.L[:, 256:512], T.WN[:], T.lm0[:], True, False, ["WN", "lm0"], ["L"])
        mm(T.L[:, 256:512], T.EN[:, sec(t)], T[tb][:], False, True, ["EN0", "EN1", tb], ["L"])

    def prep_nh_s():
        act(T.NH[:], T.L[:, 256:512], ["L", "cb"], ["NH"], func=F.Identity, bias=T.cb[:])

    def spread(out, t, ch, k, sign, start, stop):
        c = str(ch)
        tab, key = table(t, k)
        mm(out, T[sign + c][block(t), :], tab, start, stop, [sign + c, key], ["T" + c])

    def gain_t(t, ch, stop):
        spread(T["T%d" % ch][:, 256:384], t, ch, 1, "E", False, False)
        spread(T["T%d" % ch][:, 256:384], t, ch, 0, "nE", False, stop)

    def places(t, ch, bk):
        tab, key = table(t, 0)
        lo = block(t).start + 8 * ch
        mm(T[bk][:, 0:8], tab, T.Id[block(t), lo:lo + 8], True, False, [key, "Id"], [bk])
        mm(T[bk][:, 0:8], T.E0[block(t), :], T.C2[block(t), 0:8], False, False, ["E0", "C2"], [bk])

    def count(ch, bk):
        mm(T[bk][:, 0:8], T["HT%d" % ch][:], T.U8[:], False, True, ["HT%d" % ch, "U8"], [bk])

    def aside(ch, bk):
        tt(T.DL[:, 8 * ch:8 * ch + 8], T[bk][:, 0:8], T.D[:, 8 * ch:8 * ch + 8], A.min, [bk, "D"], ["d%d" % ch])

    def gain(ch):
        c = str(ch)
        tt(T["hb" + c][:], T["HT" + c][:], T["T" + c][:, 256:384], A.mult, ["HT" + c, "T" + c], ["hb" + c])

    def turn(ch, k, w, start, stop, bk="X"):
        c = str(ch)
        mm(T[bk + c][:, 0:128], T[k + c][:], T[w][:], start, stop, [k + c, w], [bk + c])

    def as_list(ch, bk="X"):
        act(T.OF[:, sec(ch)], T[bk + str(ch)][:, 0:128], [bk + str(ch)], ["f%d" % ch], bias=float(BIAS))

    def as_half(ch, bk="X"):
        act(T.OW[:, sec(ch)], T[bk + str(ch)][:, 0:128], [bk + str(ch)], ["w%d" % ch])

    def scatter_h(t, lo, hi):
        act(T["HN%d" % (t % 2)][:, 0:WIN].indirect(T.DL[:, 8 * lo:8 * hi]), T.NH[:, 128 * lo:128 * hi],
            ["d%d" % c for c in range(lo, hi)] + ["NH"], HK[t % 2], func=F.Silu)

    def scatter_w(t, lo, hi):
        vcopy(T["W%d" % t][:, 0:WIN].indirect(T.DL[:, 8 * lo:8 * hi]), T.lm0[:, 128 * lo:128 * hi],
              ["d%d" % c for c in range(lo, hi)] + ["lm0"], WK[t])

    def rows_of(t, buf):
        hn = T["HN%d" % (t % 2)]
        return [(hn[lane:128:16, 0:4096], T[buf][:, 256 * k:256 * k + 256]) for k, lane in enumerate(LANES)]

    def ship_w(t, k):
        u = t + 1
        out, in_ = T["W%d" % u][:, SHIP[k]:SHIP[k + 1]], T["W%d" % t][:, SHIP[k]:SHIP[k + 1]]
        if k and via is not None:
            send(via, out, in_, "hw%d%d" % (u, k), WK[t], topo.engines(core, prv))
        else:
            send(prv, out, in_, "bw%d" % u, WK[t])

    def ship_h(t):
        u = t + 1
        send(prv, T["CR%d" % u][:], T["CP%d" % u][:], "bh%d" % u, ["CP%d" % u])

    def pack(t):
        u = t + 1
        dmas([(b, a) for a, b in rows_of(t, "CP%d" % u)], "cp%d" % u, ["CP%d" % u], HK[t % 2])

    def unpack(u):
        dmas(rows_of(u, "CR%d" % u), "xh%d" % u, HK[u % 2], ["CR%d" % u])

    def parts(k, lo, hi):
        return [k + "_%d" % j for j in range(lo // 8, hi // 8)]

    def list_of(ch, p, lo, hi):
        k = ("OF", "off")[p]
        return T[k][:, 128 * ch + lo:128 * ch + hi], ("f%d", "off%d")[p] % ch

    def gv(t, ch, p, lo, hi):
        m = "M%d" % ch
        lst, key = list_of(ch, p, lo, hi)
        op("v", lambda: g.vector.tensor_tensor(out=T[m][:, 16 * lo:16 * hi], in0=T["W%d" % t][:, 0:4096].indirect(lst),
                                               in1=T.lr[:, 2048 * ch + 16 * lo:2048 * ch + 16 * hi], op=A.max),
           WK[t] + [key, "lr%d" % ch], parts(m, lo, hi))

    def gs(t, ch, p, lo, hi):
        h = "H%d" % ch
        lst, key = list_of(ch, p, lo, hi)
        act(T[h][:, 16 * lo:16 * hi], T["HN%d" % (t % 2)][:, 0:4096].indirect(lst), HK[t % 2] + [key, "gb"], parts(h, lo, hi),
            func=F.Identity, bias=T.gb[:])

    def init(t, ch):
        c, o = str(ch), "w%d" % ch
        own = T.OW[:, sec(ch)]
        for bk in ("X" + c, "Y" + c):
            mm(T[bk][:, 0:128], T["E" + c][0:16, :], T.Ls[:], True, False, ["E" + c, "Ls"], [bk])
        mm(T["X" + c][:, 256:384], T.Z[:], T.Z[:], False, False, ["Z"], ["X" + c])
        mm(T["X" + c][:, 128:256], own, T.HI[:], False, False, [o, "HI"], ["X" + c])
        if t == R - 1:
            mm(T["T" + c][:, 0:128], own, T.HI[:], True, False, [o, "HI"], ["T" + c])
            mm(T["T" + c][:, 0:128], T.E0[0:16, :], T.C2[0:16, :], False, False, ["E0", "C2"], ["T" + c])
        else:
            mm(T["T" + c][:, 128:256], own, T.HI[:], True, False, [o, "HI"], ["T" + c])

    def init_deeds(t, ch):
        spread(T["T%d" % ch][:, 128:256], t + 1, ch, 0, "nE", False, False)
        gain_t(t + 1, ch, False)

    def sums_h(ch, p, lo=0, hi=128, stop=True):
        bk, h, w = "XY"[p] + str(ch), "H%d" % ch, 3 - p
        for r in range(16):
            mm(T[bk][lo:hi, r:128 * w:16], T[h][:, 16 * lo + r:16 * hi:16], T.RH[:, 0:8 * w], False, stop and r == 15,
               parts(h, lo, hi) + ["RH%d" % k for k in range(3)], [bk])

    def sums_m(ch, p, lo=0, hi=128, stop=False):
        bk, m = "XY"[p] + str(ch), "M%d" % ch
        for r in range(16):
            mm(T[bk][lo:hi, r:128:16], T[m][:, 16 * lo + r:16 * hi:16], T.RM[:], False, stop and r == 15, parts(m, lo, hi) + ["RM"], [bk])

    def heirs(ch):
        c = str(ch)
        act(T["hT" + c][:], T["X" + c][:, 256:384], ["X" + c], ["hT" + c])
        act(T["SA" + c][:], T["X" + c][:, 0:128], ["X" + c], ["SA" + c], func=F.Sign, scale=-1.0, bias=TH)
        op("t", lambda: g.tensor.transpose(T.P[:, sec(ch)], T["hT" + c][:], T.Ih[:]), ["hT" + c, "Ih"], ["P"])
        mm(T["Y" + c][:, 128:256], T.HI[:], T["hT" + c][:], False, False, ["hT" + c, "HI"], ["Y" + c])

    def first(ch):
        c = str(ch)
        ts(T.off[:, sec(ch)], T.P[:, sec(ch)], BIAS, A.add, ["P"], ["off" + c])
        tt(T["ta" + c][:], T["SA" + c][:], T["X" + c][:, 128:256], A.mult, ["SA" + c, "X" + c], ["ta" + c])

    def first_t(ch, last):
        c = str(ch)
        lo = 0 if last else 128
        mm(T["Y" + c][:, 0:128], T.BI[:], T["SA" + c][:], False, False, ["SA" + c, "BI"], ["Y" + c])
        mm(T["T" + c][:, lo:lo + 128], T.HI[:], T["hT" + c][:], False, False, ["hT" + c, "HI"], ["T" + c])
        mm(T["T" + c][:, lo:lo + 128], T.nI32[:], T["ta" + c][:], False, True, ["ta" + c, "nI32"], ["T" + c])
        if not last:
            mm(T["X" + c][:, 0:128], T.HI[:], T.OW[:, sec(ch)], True, False, ["w" + c, "HI"], ["X" + c])
            turn(ch, "hT", "HI", False, False)
            turn(ch, "ta", "nI32", False, False)

    def near(ch):
        ts(T["SB%d" % ch][:], T["Y%d" % ch][:, 0:128], TH - FAR, A.is_le, ["Y%d" % ch], ["SB%d" % ch], 2.0, A.mult)

    def second(ch):
        c = str(ch)
        tt(T["tb" + c][:], T["SB" + c][:], T["Y" + c][:, 128:256], A.mult, ["SB" + c, "Y" + c], ["tb" + c])

    def hit(ch):
        c = str(ch)
        tt(T["HT" + c][:], T["T" + c][:, 128:256], T["tb" + c][:], A.is_equal, ["T" + c, "tb" + c], ["HT" + c])

    def result(ch):
        c = str(ch)
        tt(T.yof[:, sec(ch)], T["T" + c][:, 0:128], T["tb" + c][:], A.subtract, ["T" + c, "tb" + c], ["yof" + c])

    def owners(ch):
        turn(ch, "tb", "nI32", False, False)
        turn(ch, "hb", "I32", False, True)

    def store_yo(ch):
        for k in range(8):
            store("ys"[k % 2] if ch else "y", T.yo[16 * k:16 * k + 16, sec(ch)], T.yof[:, 128 * ch + 16 * k:128 * ch + 16 * k + 16], ["yof%d" % ch])

    def own0(ch):
        act(T.ownH[:, sec(ch)], T.ownI[:, sec(ch)], ["ownI%d" % ch], ["ownH%d" % ch], bias=-float(BIAS))

    def hit0(ch):
        c = str(ch)
        tt(T["HT" + c][:], T["T" + c][:, 128:256], T.ownH[:, sec(ch)], A.is_equal, ["T" + c, "ownH" + c], ["HT" + c])
        places(0, ch, "L")
        count(ch, "L")

    def turn0(ch):
        turn(ch, "hb", "I32", True, False, "T")
        mm(T["T%d" % ch][:, 0:128], T.ownH[:, sec(ch)], T.Id[:], False, True, ["ownH%d" % ch, "Id"], ["T%d" % ch])

    fill_h(0)
    x_heir(0)
    x_heir(1)
    act(T.TB0[:], T.TI[:], ["TI", "fs", "fb"], ["TB0"], func=F.Identity, scale=T.fs[:], bias=T.fb[:])
    mm(T.L[:, 0:8], T.E0[0:16, :], T.Id[0:16, 0:8], True, True, ["E0", "Id"], ["L"])
    small_t(0, "T0")
    for r in range(16):
        mm(T.T1[0:16, 256 + r:384:16], T.lm0[:, r:256:16], T.nB8[:], r == 0, r == 15, ["lm0", "nB8"], ["T1"])
    x_heir(2)
    x_heir(3)
    act(T.cb2[:], T.OH[:, 0:1], ["OH", "cb1"], ["cb2"], func=F.Identity, scale=-7168.0, bias=T.cb1[:])
    act(T.aT0[:], T.T0[0:16, 0:256], ["T0"], ["aT0"])
    act(T.cb3[:], T.OH[:, 1:2], ["OH", "cb2"], ["cb3"], func=F.Identity, scale=8.0 * (2048 + 32768 + 144), bias=T.cb2[:])
    act(T.U8[:], T.L[:, 0:8], ["L"], ["U8"], scale=8192.0)
    act(T.cb[:], T.OH[:, 2:3], ["OH", "cb3"], ["cb"], func=F.Identity, scale=1024.0, bias=T.cb3[:])
    act(T.Ls[:], T.T1[0:16, 256:384], ["T1"], ["Ls"], bias=float(BIAS))
    double(0)
    double(1)
    ts(T.wh[:], T.OH[:, 2:3], -6288.0 / 4096, A.mult, ["OH", "wh1"], ["wh"], T.wh1[:], A.add)
    ts(T.gb[:], T.OH[:, 3:4], -2064.0, A.mult, ["OH"], ["gb"])
    double(2)
    ts(T.RM[:], T.nB8[:], -2.0, A.mult, ["nB8"], ["RM"])
    for k, (w, key, val) in enumerate(((T.OH[:, 3:4], "OH", 1.0), (T.wh[:], "wh", 2.0), (T.wh[:], "wh", -4.0))):
        ts(T.RH[:, 8 * k:8 * k + 8], T.nB8[:], w, A.mult, ["nB8", key], ["RH%d" % k], val, A.mult)
    for t in range(1, n):
        send(T.cores[(rank - t) % n], T["TB%d" % t][:], T.TB0[:], "tb%d" % t, ["TB0"])
    for k, val in (("HI", 0.5), ("Ih", 1.0), ("BI", -FAR), ("nI32", -1.0)):
        diagonal(k, val)
    for k in (0, 1, 2):
        x_book(k)
    for ch in (0, 1):
        spread(T["T%d" % ch][:, 128:256], 0, ch, 0, "E", True, False)
        gain_t(0, ch, True)
    prep_nh_t(0)
    x_copy(0)
    double(3)
    x_copy(1)
    x_copy(2)
    own0(0)
    prep_nh_s()
    x_heir(4)
    x_book(3)
    x_heir(5)
    x_book(4)
    hit0(0)
    x_copy(3)
    double(4)
    gain(0)
    aside(0, "L")
    x_heir(6)
    x_book(5)
    x_heir(7)
    own0(1)
    x_copy(4)
    turn0(0)
    x_copy(5)
    hit0(1)
    x_book(6)
    x_book(7)
    gain(1)
    aside(1, "L")
    turn0(1)
    as_list(0, "T")
    as_half(0, "T")
    x_copy(6)
    x_copy(7)
    scatter_w(0, 0, 2)
    scatter_h(0, 0, 2)
    ts(T.OF[:, sec(1)], T.T1[:, 0:128], float(BIAS), A.add, ["T1"], ["f1"])
    vcopy(T.OW[:, sec(1)], T.T1[:, 0:128], ["T1"], ["w1"])

    for t in range(R):
        last = t == R - 1
        u = t + 1
        if last:
            for k, lane in (("yha", 0), ("yhb", 1)):
                op("p", lambda: g.dma_start(out=T[k][:], in_=T.HN0[lane:128:16, 0:4096]), HK[0], ["yhab" if lane else "yha0"], "d_yh", 16)
            store("y", T.yd[:], T["W%d" % t][:, 0:4096], WK[t])
        else:
            pack(t)
            if t == 0:
                fill_h(1)
            ship_h(t)
            for k in (1, 2, 0, 3):
                ship_w(t, k)
            if t == 0:
                fill_h(2)
                diagonal("I4", 4.0)
                diagonal("I8", 1.0 / 8)
            unpack(u)
        gv(t, 0, 0, 0, 128)
        if t:
            gs(t, 0, 0, 0, S0)
            as_list(1)
            as_half(1)
            gs(t, 0, 0, S0, 128)
        else:
            gs(t, 0, 0, 0, 128)
        init(t, 0)
        init(t, 1)
        sums_m(0, 0)
        sums_h(0, 0)
        if t == 0:
            mm(T.L[:, 0:256], T.Z[:], T.TB0[:], True, False, ["Z", "TB0"], ["L"])
            for k in range(1, R):
                small_t(k, "L")
            mm(T.L[:, 256:320], T.Z[:], T.Z[:, 0:64], False, True, ["Z"], ["L"])
        elif not last:
            init_deeds(t, 0)
            init_deeds(t, 1)
            prep_nh_t(u)
        gv(t, 1, 0, 0, 128)
        gs(t, 1, 0, 0, SS)
        heirs(0)
        if t == 0:
            act(T.aTA[:], T.L[:, 0:256], ["L"], ["aTA"])
        gs(t, 1, 0, SS, 128)
        first(0)
        sums_m(1, 0)
        sums_h(1, 0)
        if t == 0:
            init_deeds(t, 0)
            init_deeds(t, 1)
            prep_nh_t(u)
        first_t(0, last)
        if last:
            mm(T.L[:, 0:256], T.I4[:], T.yha[:], True, False, ["I4", "yhab"], ["L"])
            mm(T.L[:, 0:256], T.I8[:], T.yhb[:], False, True, ["I8", "yhab"], ["L"])
        gv(t, 0, 1, 0, 128)
        gs(t, 0, 1, 0, SS)
        heirs(1)
        gs(t, 0, 1, SS, 128)
        first(1)
        sums_m(0, 1)
        sums_h(0, 1)
        first_t(1, last)
        gs(t, 1, 1, 0, 96)
        gs(t, 1, 1, 96, 128)
        gv(t, 1, 1, 0, 64)
        near(0)
        gv(t, 1, 1, 64, 80)
        second(0)
        gv(t, 1, 1, 80, 96)
        if last:
            result(0)
            store_yo(0)
        else:
            hit(0)
            gain(0)
        gv(t, 1, 1, 96, 128)
        sums_m(1, 1, 0, 64)
        sums_m(1, 1, 64, 96)
        if not last:
            places(u, 0, "Y0")
            count(0, "Y0")
        sums_h(1, 1, 0, 96)
        sums_h(1, 1, 96, 128, False)
        sums_m(1, 1, 96, 128, True)
        if last:
            act(T.yhf[:], T.L[:, 0:256], ["L"], ["yhf"], bias=-4240.0)
            store("y", T.yh[:], T.yhf[:], ["yhf"])
            near(1)
            second(1)
            result(1)
            store_yo(1)
            break
        prep_nh_s()
        aside(0, "Y0")
        owners(0)
        places(u, 1, "Y0")
        scatter_h(u, 0, 1)
        scatter_w(u, 0, 1)
        near(1)
        second(1)
        as_list(0)
        as_half(0)
        hit(1)
        count(1, "Y0")
        gain(1)
        owners(1)
        aside(1, "Y0")
        scatter_w(u, 1, 2)
        scatter_h(u, 1, 2)

    g.sync.wait_ge(T.sem.dout, cnt["dout"])
    wait("p", {s: c for s, c in cnt.items() if s != "dout"})
